import numpy as np
import ml_dtypes


def mxq(x, axis, fmt="e4m3"):
    dtype, down = {"e4m3": (ml_dtypes.float8_e4m3fn, 7), "e5m2": (ml_dtypes.float8_e5m2, 14)}[fmt]
    v = np.moveaxis(np.asarray(x, np.float32).astype(ml_dtypes.bfloat16).astype(np.float64), axis, -1)
    blocks = v.reshape(v.shape[:-1] + (-1, 32))
    amax = np.abs(blocks).max(-1, keepdims=True)
    byte = np.maximum(np.where(amax > 0, np.frexp(amax)[1] - 1 + 127, 0) - down, 1)
    scale = np.exp2(byte - 127.0)
    codes = (blocks / scale).astype(np.float32).astype(dtype).astype(np.float64)
    return np.moveaxis((codes * scale).reshape(v.shape), -1, axis)


WIDE = False


def mx_kscale(k):
    if not WIDE:
        return np.ones(k)
    levels = np.array([10, -10, 5, -5, 0])
    if k % 512:
        return np.exp2(np.random.permutation(np.resize(levels, k // 32))).repeat(32)
    a = np.empty((k // 512, 16))
    for p in range(k // 512):
        a[p, :8] = np.random.permutation(np.resize(levels, 8))
        for g in range(8):
            far = levels[np.abs(levels - a[p, g]) >= 10]
            a[p, g + 8] = far[np.random.randint(len(far))]
    return np.exp2(a.ravel()).repeat(32)


def f64(x):
    return np.asarray(x).astype(np.float64)


def striped(idx):
    return np.tile(idx.reshape(-1, 16).T, (8, 1)).astype(np.uint16)


def unstriped(offs):
    return offs[:16].T.reshape(-1).astype(np.int64)


def pack_weight(w):
    k, n = w.shape
    w = f64(np.asarray(w, np.float32).astype(ml_dtypes.bfloat16)).reshape(k // 32, 32, n)
    amax = np.abs(w).max(1)
    byte = np.clip(np.where(amax > 0, np.frexp(amax)[1] - 1 + 127 - 7, 1), 1, 254)
    scaled = (w * np.exp2(127.0 - byte)[:, None, :]).reshape(k, n).astype(np.float32)
    words = np.ascontiguousarray(scaled.reshape(k // 512, 128, 4, n).transpose(0, 1, 3, 2)).astype(ml_dtypes.float8_e4m3fn).view(np.uint8)
    return words, np.ascontiguousarray(byte.astype(np.uint8).reshape(k // 512, 16, n))


def unpack_weight(words, scales):
    g, p, n, _ = words.shape
    vals = np.ascontiguousarray(words).view(ml_dtypes.float8_e4m3fn).astype(np.float64) * np.repeat(np.exp2(scales.astype(np.float64) - 127.0), 8, axis=1)[..., None]
    return vals.transpose(0, 1, 3, 2).reshape(g * 512, n)


def silu(v):
    return v / (1.0 + np.exp(-np.maximum(v, -700.0)))


K, T, S, H, N = 1024, 1024, 512, 512, 256
P = 2 ** 7


def setup_inputs():
    n = np.random.standard_normal
    s = mx_kscale(K)[:, None]
    u = mx_kscale(H)
    packed_xT = pack_weight(n((K, T)) * s)
    packed_w2 = pack_weight(n((H, N)) / np.sqrt(H) / u[:, None])
    return {
        "x_words": packed_xT[0],
        "x_scales": packed_xT[1],
        "gate": np.tile(np.random.uniform(0.2, 1.0, S), (P, 1)).astype(np.float32),
        "res": n((N, T)).astype(np.float32),
        "w1": (n((K, H)) / np.sqrt(K) / s).astype(np.float32),
        "w3": (n((K, H)) / np.sqrt(K) / s * u).astype(np.float32),
        "w2_words": packed_w2[0],
        "w2_scales": packed_w2[1],
        "offs": striped(np.random.permutation(T)[:S]),
    }


def reference(x_words, x_scales, gate, res, w1, w3, w2_words, w2_scales, offs):
    r = f64(res)[:, unstriped(offs)]
    xq = unpack_weight(x_words, x_scales)[:, unstriped(offs)]
    h = (silu(mxq(f64(w1), 0, "e4m3").T @ xq)) * ((mxq(f64(w3), 0, "e4m3").T @ xq))
    y = unpack_weight(w2_words, w2_scales).T @ mxq(h, 0, "e4m3")
    out = f64(res).copy()
    out[:, unstriped(offs)] = r + y * f64(gate)[:1]
    return out

@@ -1,0 +1,232 @@
+from contextlib import ExitStack
+
+import concourse.mybir as mybir
+from concourse.masks import make_identity
+
+K, T, S, H, N = 1024, 1024, 512, 512, 256
+FLOPS = 2 * (2 * K * H * S + H * N * S)
+
+F32 = mybir.dt.float32
+BF16 = mybir.dt.bfloat16
+I32 = mybir.dt.int32
+U32 = mybir.dt.uint32
+U16 = mybir.dt.uint16
+U8 = mybir.dt.uint8
+FP8X4 = mybir.dt.float8_e4m3fn_x4
+ADD = mybir.AluOpType.add
+MULT = mybir.AluOpType.mult
+SILU = mybir.ActivationFunctionType.Silu
+COPY = mybir.ActivationFunctionType.Copy
+
+P = 128
+PACK = 4
+PASSES = K // (P * PACK)
+CH = 128
+CHUNKS = S // CH
+HALF = H // 2
+MH = HALF // PACK
+BLOCKS = N // P
+VSHARE = [0, 0, 64, 40, 0, 64, 64, 40]
+SCATTERS = [(0, 0, 1), (1, 0, 1), (0, 1, 2), (0, 2, 4), (1, 1, 4)]
+
+
+def tile_picked_modres_glusilu_p_kernel(
+    tc, x_words, x_scales, gate, res, w1, w3, w2_words, w2_scales, offs, out
+):
+    nc = tc.nc
+    with ExitStack() as ctx:
+        keep = ctx.enter_context(tc.tile_pool(name="keep", bufs=1))
+        psum = ctx.enter_context(tc.psum_pool(name="psum", bufs=1))
+
+        offsets = keep.tile([P, S // 16], U16, name="offsets")
+        nc.sync.dma_start(offsets[:], offs)
+
+        xs_tab = keep.tile([P, T], U8, name="xs_tab", align_bytes=64)
+        nc.vector.memset(xs_tab[:].bitcast(I32), 0)
+        for q in range(4):
+            nc.scalar.dma_start(
+                xs_tab[32 * q : 32 * q + 4 * PASSES, :].bitcast(I32),
+                x_scales[:, 4 * q : 4 * q + 4, :].bitcast(I32),
+            )
+        w2s = keep.tile([P, N], U8, name="w2s", align_bytes=64)
+        nc.gpsimd.memset(w2s[:].bitcast(I32), 0)
+        ident = keep.tile([P, P], F32, name="ident")
+        make_identity(nc, ident[:])
+
+        x_tab = [keep.tile([P, T], U32, name="x_tab%d" % g, align_bytes=64) for g in range(PASSES)]
+        raw = [keep.tile([P, PACK, HALF], F32, name="raw%d" % i) for i in range(8)]
+
+        def load_x(g):
+            nc.sync.dma_start(
+                x_tab[g][:].bitcast(I32), x_words[g].rearrange("p n t -> p (n t)").bitcast(I32)
+            )
+
+        def load_w(i):
+            w = (w1, w3)[i // 4]
+            g = (i // 2) % 2
+            u = i % 2
+            rows = w[g * P * PACK : (g + 1) * P * PACK, u * HALF : (u + 1) * HALF]
+            nc.sync.dma_start(raw[i][:], rows.rearrange("(p j) c -> p j c", j=PACK))
+
+        load_x(0)
+        load_w(0)
+        load_x(1)
+        for i in range(1, 8):
+            load_w(i)
+
+        win = [keep.tile([P, T], F32, name="win%d" % b) for b in range(BLOCKS)]
+        w2q = keep.tile([P, N], U32, name="w2q", align_bytes=64)
+        gcol = keep.tile([P, CHUNKS], F32, name="gcol")
+        nc.sync.dma_start(win[0][:], res[0:P, :])
+        nc.sync.dma_start(w2q[:].bitcast(I32), w2_words[0].rearrange("p n t -> p (n t)").bitcast(I32))
+        for q in range(4):
+            nc.sync.dma_start(
+                w2s[32 * q : 32 * q + 4, :].bitcast(I32), w2_scales[0, 4 * q : 4 * q + 4, :].bitcast(I32)
+            )
+        with nc.allow_non_contiguous_dma(reason="one gate weight to a partition"):
+            nc.sync.dma_start(gcol[:], gate[0, :].rearrange("(c p) -> p c", p=P))
+        nc.sync.dma_start(win[1][:], res[P : 2 * P, :])
+
+        xq = [keep.tile([P, S], U32, name="xq%d" % g, align_bytes=64) for g in range(PASSES)]
+        xs = keep.tile([P, S], U8, name="xs", align_bytes=64)
+        nc.vector.tensor_copy(xq[0][:], x_tab[0][:].indirect(offsets[:]))
+        nc.vector.tensor_copy(xs[:], xs_tab[:].indirect(offsets[:]))
+        nc.vector.tensor_copy(xq[1][:], x_tab[1][:].indirect(offsets[:]))
+
+        grouped = [keep.tile([P, PACK, P, PACK], BF16, name="grouped%d" % v, tag="grouped%d" % v, align_bytes=64) for v in range(4)]
+        wq = [keep.tile([P, H], U32, name="wq%d" % v, align_bytes=64) for v in range(4)]
+        ws = [keep.tile([P, H], U8, name="ws%d" % v, align_bytes=64) for v in range(4)]
+
+        def cast(i):
+            v, u = i // 2, i % 2
+            src = raw[i][:].rearrange("p j (m t) -> p m j t", t=PACK)
+            dst = grouped[v][:].rearrange("p t m j -> p m j t")
+            cut = MH - VSHARE[i]
+            if cut > 0:
+                nc.scalar.copy(dst[:, u * MH : u * MH + cut], src[:, 0:cut])
+            if cut < MH:
+                nc.vector.tensor_copy(dst[:, u * MH + cut : (u + 1) * MH], src[:, cut:MH])
+
+        def quant_w(v, parts):
+            flat = grouped[v][:].rearrange("p t m j -> p (t m j)")
+            wd = H // parts
+            for a in range(parts):
+                nc.vector.quantize_mx(
+                    out=wq[v][:, a * wd : (a + 1) * wd].bitcast(FP8X4),
+                    scales=ws[v][:, a * wd : (a + 1) * wd],
+                    in_=flat[:, PACK * a * wd : PACK * (a + 1) * wd],
+                )
+
+        def first_product(w, c, acc):
+            toks = slice(c * CH, (c + 1) * CH)
+            for t in range(PACK):
+                cols = slice(t * P, (t + 1) * P)
+                for g in range(PASSES):
+                    v = 2 * w + g
+                    nc.tensor.matmul_mx(
+                        out=acc[:, t, :],
+                        lhsT=wq[v][:, cols].bitcast(FP8X4),
+                        lhsT_scale=ws[v][:, cols],
+                        rhs=xq[g][:, toks].bitcast(FP8X4),
+                        rhs_scale=xs[4 * g : P, toks],
+                        start=(g == 0),
+                        stop=(g == PASSES - 1),
+                    )
+
+        cast(0)
+        cast(1)
+        cast(2)
+        quant_w(0, 1)
+        cast(3)
+        quant_w(1, 1)
+        cast(4)
+        act = [keep.tile([P, CH, PACK], F32, name="act%d" % c) for c in range(CHUNKS)]
+        gate_acc = [psum.tile([P, PACK, CH], F32, name="ga%d" % c, tag="a%d" % c) for c in range(CHUNKS)]
+        for c in range(CHUNKS):
+            first_product(0, c, gate_acc[c])
+
+        def silu(c):
+            nc.scalar.activation(act[c][:], gate_acc[c][:].rearrange("p t n -> p n t"), SILU)
+
+        cast(5)
+        silu(0)
+        quant_w(2, 1)
+        cast(6)
+        silu(1)
+        silu(2)
+        cast(7)
+        silu(3)
+        quant_w(3, 4)
+
+        up_acc = [psum.tile([P, PACK, CH], F32, name="ua%d" % c, tag="b%d" % c) for c in range(CHUNKS)]
+        for c in range(CHUNKS):
+            first_product(1, c, up_acc[c])
+
+        rg = [None, None]
+        hb = [keep.tile([P, CH, PACK], BF16, name="hb%d" % c, tag="hb%d" % c, align_bytes=64) for c in range(CHUNKS)]
+        hq = [keep.tile([P, CH], U32, name="hq%d" % c, align_bytes=64) for c in range(CHUNKS)]
+        hs = [keep.tile([P, CH], U8, name="hs%d" % c, align_bytes=64) for c in range(CHUNKS)]
+        ygt = [keep.tile([P, N], F32, name="ygt%d" % c) for c in range(CHUNKS)]
+        yg = [keep.tile([P, S], F32, name="yg%d" % b) for b in range(BLOCKS)]
+
+        def gather_res(b, tag):
+            rg[b] = keep.tile([P, S], F32, name="rg%d" % b, tag=tag, align_bytes=64)
+            nc.vector.tensor_copy(rg[b][:], win[b][:].indirect(offsets[:]))
+
+        def hmul(c):
+            nc.vector.tensor_tensor(hb[c][:], up_acc[c][:].rearrange("p t n -> p n t"), act[c][:], MULT)
+
+        def hquant(c):
+            nc.vector.quantize_mx(
+                out=hq[c][:].bitcast(FP8X4), scales=hs[c][:], in_=hb[c][:].rearrange("p n t -> p (n t)")
+            )
+
+        def second_product(c):
+            yt = psum.tile([P, N], F32, name="yt%d" % c, tag="a%d" % c)
+            nc.tensor.matmul_mx(
+                out=yt[:],
+                lhsT=hq[c][:].bitcast(FP8X4),
+                lhsT_scale=hs[c][:],
+                rhs=w2q[:].bitcast(FP8X4),
+                rhs_scale=w2s[:],
+                start=True,
+                stop=True,
+            )
+            nc.scalar.activation(ygt[c][:], yt[:], COPY, scale=gcol[:, c : c + 1])
+
+        def turn_back(c):
+            yb = psum.tile([P, BLOCKS, CH], F32, name="yb%d" % c, tag="b%d" % c)
+            for b in range(BLOCKS):
+                nc.tensor.transpose(yb[:, b, :], ygt[c][:, b * P : (b + 1) * P], ident[:])
+            for b in range(BLOCKS):
+                nc.scalar.copy(yg[b][:, c * CH : (c + 1) * CH], yb[:, b, :])
+
+        gather_res(0, "grouped3")
+        hmul(0)
+        hmul(1)
+        hquant(0)
+        hmul(2)
+        second_product(0)
+        hquant(1)
+        hmul(3)
+        second_product(1)
+        turn_back(0)
+        hquant(2)
+        hquant(3)
+        gather_res(1, "hb3")
+        second_product(2)
+        turn_back(1)
+        second_product(3)
+        turn_back(2)
+        turn_back(3)
+
+        for b, c0, c1 in SCATTERS:
+            toks = slice(c0 * CH, c1 * CH)
+            nc.vector.tensor_tensor(
+                win[b][:].indirect(offsets[:, c0 * CH // 16 : c1 * CH // 16]),
+                yg[b][:, toks],
+                rg[b][:, toks],
+                ADD,
+            )
+            if c1 == CHUNKS:
+                nc.sync.dma_start(out[b * P : (b + 1) * P, :], win[b][:])

@@ -24,10 +24,9 @@ PASSES = K // (P * PACK)
 CH = 128
 CHUNKS = S // CH
 HALF = H // 2
-MH = HALF // PACK
 BLOCKS = N // P
-VSHARE = [0, 0, 64, 40, 0, 64, 64, 40]
-SCATTERS = [(0, 0, 1), (1, 0, 1), (0, 1, 2), (0, 2, 4), (1, 1, 4)]
+VSHARE = [0,32,0,64,0,64,0,40]
+SCATTERS = [(0, 0, 1), (1, 0, 1), (0, 1, 2), (1, 1, 2), (0, 2, 4), (1, 2, 4)]
 
 
 def tile_picked_modres_glusilu_p_kernel(
@@ -42,12 +41,7 @@ def tile_picked_modres_glusilu_p_kernel(
         nc.sync.dma_start(offsets[:], offs)
 
         xs_tab = keep.tile([P, T], U8, name="xs_tab", align_bytes=64)
-        nc.vector.memset(xs_tab[:].bitcast(I32), 0)
-        for q in range(4):
-            nc.scalar.dma_start(
-                xs_tab[32 * q : 32 * q + 4 * PASSES, :].bitcast(I32),
-                x_scales[:, 4 * q : 4 * q + 4, :].bitcast(I32),
-            )
+        nc.gpsimd.memset(xs_tab[:].bitcast(I32), 0)
         w2s = keep.tile([P, N], U8, name="w2s", align_bytes=64)
         nc.gpsimd.memset(w2s[:].bitcast(I32), 0)
         ident = keep.tile([P, P], F32, name="ident")
@@ -61,23 +55,29 @@ def tile_picked_modres_glusilu_p_kernel(
                 x_tab[g][:].bitcast(I32), x_words[g].rearrange("p n t -> p (n t)").bitcast(I32)
             )
 
+        def piece(u, w, g):
+            return 4 * u + 2 * w + g
+
         def load_w(i):
-            w = (w1, w3)[i // 4]
-            g = (i // 2) % 2
-            u = i % 2
-            rows = w[g * P * PACK : (g + 1) * P * PACK, u * HALF : (u + 1) * HALF]
+            u, w, g = i // 4, (i // 2) % 2, i % 2
+            rows = (w1, w3)[w][g * P * PACK : (g + 1) * P * PACK, u * HALF : (u + 1) * HALF]
             nc.sync.dma_start(raw[i][:], rows.rearrange("(p j) c -> p j c", j=PACK))
 
         load_x(0)
-        load_w(0)
+        for q in range(4):
+            nc.sync.dma_start(
+                xs_tab[32 * q : 32 * q + 4 * PASSES, :].bitcast(I32),
+                x_scales[:, 4 * q : 4 * q + 4, :].bitcast(I32),
+            )
         load_x(1)
-        for i in range(1, 8):
+        for i in range(8):
             load_w(i)
 
         win = [keep.tile([P, T], F32, name="win%d" % b) for b in range(BLOCKS)]
         w2q = keep.tile([P, N], U32, name="w2q", align_bytes=64)
         gcol = keep.tile([P, CHUNKS], F32, name="gcol")
         nc.sync.dma_start(win[0][:], res[0:P, :])
+        nc.sync.dma_start(win[1][:], res[P : 2 * P, :])
         nc.sync.dma_start(w2q[:].bitcast(I32), w2_words[0].rearrange("p n t -> p (n t)").bitcast(I32))
         for q in range(4):
             nc.sync.dma_start(
@@ -85,7 +85,6 @@ def tile_picked_modres_glusilu_p_kernel(
             )
         with nc.allow_non_contiguous_dma(reason="one gate weight to a partition"):
             nc.sync.dma_start(gcol[:], gate[0, :].rearrange("(c p) -> p c", p=P))
-        nc.sync.dma_start(win[1][:], res[P : 2 * P, :])
 
         xq = [keep.tile([P, S], U32, name="xq%d" % g, align_bytes=64) for g in range(PASSES)]
         xs = keep.tile([P, S], U8, name="xs", align_bytes=64)
@@ -93,96 +92,117 @@ def tile_picked_modres_glusilu_p_kernel(
         nc.vector.tensor_copy(xs[:], xs_tab[:].indirect(offsets[:]))
         nc.vector.tensor_copy(xq[1][:], x_tab[1][:].indirect(offsets[:]))
 
-        grouped = [keep.tile([P, PACK, P, PACK], BF16, name="grouped%d" % v, tag="grouped%d" % v, align_bytes=64) for v in range(4)]
-        wq = [keep.tile([P, H], U32, name="wq%d" % v, align_bytes=64) for v in range(4)]
-        ws = [keep.tile([P, H], U8, name="ws%d" % v, align_bytes=64) for v in range(4)]
+        grouped = [
+            keep.tile([P, HALF, PACK], BF16, name="grouped%d" % i, tag="grouped%d" % i, align_bytes=64)
+            for i in range(8)
+        ]
+        wq = [keep.tile([P, HALF], U32, name="wq%d" % i, align_bytes=64) for i in range(8)]
+        ws = [keep.tile([P, HALF], U8, name="ws%d" % i, align_bytes=64) for i in range(8)]
 
         def cast(i):
-            v, u = i // 2, i % 2
-            src = raw[i][:].rearrange("p j (m t) -> p m j t", t=PACK)
-            dst = grouped[v][:].rearrange("p t m j -> p m j t")
-            cut = MH - VSHARE[i]
+            src = raw[i][:].rearrange("p j (c e) -> p c j e", e=4)
+            dst = grouped[i][:].rearrange("p (c e) j -> p c j e", e=4)
+            cut = HALF // 4 - VSHARE[i]
             if cut > 0:
-                nc.scalar.copy(dst[:, u * MH : u * MH + cut], src[:, 0:cut])
-            if cut < MH:
-                nc.vector.tensor_copy(dst[:, u * MH + cut : (u + 1) * MH], src[:, cut:MH])
+                nc.scalar.copy(dst[:, 0:cut], src[:, 0:cut])
+            if cut < HALF // 4:
+                nc.vector.tensor_copy(dst[:, cut:], src[:, cut:])
 
-        def quant_w(v, parts):
-            flat = grouped[v][:].rearrange("p t m j -> p (t m j)")
-            wd = H // parts
-            for a in range(parts):
-                nc.vector.quantize_mx(
-                    out=wq[v][:, a * wd : (a + 1) * wd].bitcast(FP8X4),
-                    scales=ws[v][:, a * wd : (a + 1) * wd],
-                    in_=flat[:, PACK * a * wd : PACK * (a + 1) * wd],
-                )
+        def quant_w(i):
+            nc.vector.quantize_mx(
+                out=wq[i][:].bitcast(FP8X4), scales=ws[i][:], in_=grouped[i][:].rearrange("p c j -> p (c j)")
+            )
 
-        def first_product(w, c, acc):
+        def first_pass(u, w, c, g, acc):
             toks = slice(c * CH, (c + 1) * CH)
-            for t in range(PACK):
-                cols = slice(t * P, (t + 1) * P)
+            i = piece(u, w, g)
+            nc.tensor.matmul_mx(
+                out=acc,
+                lhsT=xq[g][:, toks].bitcast(FP8X4),
+                lhsT_scale=xs[4 * g : P, toks],
+                rhs=wq[i][:].bitcast(FP8X4),
+                rhs_scale=ws[i][:],
+                start=(g == 0),
+                stop=(g == PASSES - 1),
+            )
+
+        def pair_product(u, w, banks):
+            accs = [psum.tile([P, 2, HALF], F32, name="acc%d%d%d" % (u, w, cp), tag="bank%d" % banks[cp]) for cp in range(2)]
+            for cp in range(2):
+                first_pass(u, w, 2 * cp, 0, accs[cp][:, 0, :])
+            for cp in range(2):
+                first_pass(u, w, 2 * cp, 1, accs[cp][:, 0, :])
                 for g in range(PASSES):
-                    v = 2 * w + g
-                    nc.tensor.matmul_mx(
-                        out=acc[:, t, :],
-                        lhsT=wq[v][:, cols].bitcast(FP8X4),
-                        lhsT_scale=ws[v][:, cols],
-                        rhs=xq[g][:, toks].bitcast(FP8X4),
-                        rhs_scale=xs[4 * g : P, toks],
-                        start=(g == 0),
-                        stop=(g == PASSES - 1),
-                    )
+                    first_pass(u, w, 2 * cp + 1, g, accs[cp][:, 1, :])
+            return accs
+
+        act = [[keep.tile([P, 2, HALF], F32, name="act%d%d" % (u, cp)) for cp in range(2)] for u in range(2)]
+        hb = [keep.tile([P, H], BF16, name="hb%d" % c, tag="hb%d" % c, align_bytes=64) for c in range(CHUNKS)]
+
+        def silu(u, cp, acc):
+            nc.scalar.activation(act[u][cp][:], acc[:], SILU)
+
+        def hmul(u, c, acc):
+            nc.vector.tensor_tensor(hb[c][:, u * HALF : (u + 1) * HALF], acc, act[u][c // 2][:, c % 2, :], MULT)
 
         cast(0)
         cast(1)
+        quant_w(0)
+        quant_w(1)
+        ga = pair_product(0, 0, (0, 1))
         cast(2)
-        quant_w(0, 1)
         cast(3)
-        quant_w(1, 1)
+        quant_w(2)
+        quant_w(3)
+        ua = pair_product(0, 1, (2, 3))
         cast(4)
-        act = [keep.tile([P, CH, PACK], F32, name="act%d" % c) for c in range(CHUNKS)]
-        gate_acc = [psum.tile([P, PACK, CH], F32, name="ga%d" % c, tag="a%d" % c) for c in range(CHUNKS)]
-        for c in range(CHUNKS):
-            first_product(0, c, gate_acc[c])
-
-        def silu(c):
-            nc.scalar.activation(act[c][:], gate_acc[c][:].rearrange("p t n -> p n t"), SILU)
-
         cast(5)
-        silu(0)
-        quant_w(2, 1)
+        quant_w(4)
+        quant_w(5)
+        gb = pair_product(1, 0, (4, 5))
         cast(6)
-        silu(1)
-        silu(2)
         cast(7)
-        silu(3)
-        quant_w(3, 4)
-
-        up_acc = [psum.tile([P, PACK, CH], F32, name="ua%d" % c, tag="b%d" % c) for c in range(CHUNKS)]
+        quant_w(6)
+        quant_w(7)
+        for cp in range(2):
+            silu(0, cp, ga[cp])
         for c in range(CHUNKS):
-            first_product(1, c, up_acc[c])
+            hmul(0, c, ua[c // 2][:, c % 2, :])
+        for cp in range(2):
+            silu(1, cp, gb[cp])
+        ub = [psum.tile([P, HALF], F32, name="ub%d" % c, tag="bank%d" % (6, 7, 0, 1)[c]) for c in range(CHUNKS)]
+        for g in range(PASSES):
+            for c in range(CHUNKS):
+                first_pass(1, 1, c, g, ub[c][:])
 
-        rg = [None, None]
-        hb = [keep.tile([P, CH, PACK], BF16, name="hb%d" % c, tag="hb%d" % c, align_bytes=64) for c in range(CHUNKS)]
+        hg = [keep.tile([P, CH, PACK], BF16, name="hg%d" % c, tag="hg%d" % c, align_bytes=64) for c in range(CHUNKS)]
         hq = [keep.tile([P, CH], U32, name="hq%d" % c, align_bytes=64) for c in range(CHUNKS)]
         hs = [keep.tile([P, CH], U8, name="hs%d" % c, align_bytes=64) for c in range(CHUNKS)]
         ygt = [keep.tile([P, N], F32, name="ygt%d" % c) for c in range(CHUNKS)]
         yg = [keep.tile([P, S], F32, name="yg%d" % b) for b in range(BLOCKS)]
+        rg = [None, None]
 
         def gather_res(b, tag):
             rg[b] = keep.tile([P, S], F32, name="rg%d" % b, tag=tag, align_bytes=64)
             nc.vector.tensor_copy(rg[b][:], win[b][:].indirect(offsets[:]))
 
-        def hmul(c):
-            nc.vector.tensor_tensor(hb[c][:], up_acc[c][:].rearrange("p t n -> p n t"), act[c][:], MULT)
+        def turn_h(c):
+            words = hb[c][:].bitcast(F32)
+            ht = psum.tile([P, 2, CH], F32, name="ht%d" % c, tag="bank%d" % (2 + c % 2))
+            for e in range(2):
+                nc.tensor.transpose(ht[:, e, :], words[:, e : H // 2 : 2], ident[:])
+            nc.scalar.copy(
+                hg[c][:].rearrange("p n t -> p (n t)").bitcast(F32).rearrange("p (n e) -> p n e", e=2),
+                ht[:].rearrange("p e n -> p n e"),
+            )
 
         def hquant(c):
             nc.vector.quantize_mx(
-                out=hq[c][:].bitcast(FP8X4), scales=hs[c][:], in_=hb[c][:].rearrange("p n t -> p (n t)")
+                out=hq[c][:].bitcast(FP8X4), scales=hs[c][:], in_=hg[c][:].rearrange("p n t -> p (n t)")
             )
 
         def second_product(c):
-            yt = psum.tile([P, N], F32, name="yt%d" % c, tag="a%d" % c)
+            yt = psum.tile([P, N], F32, name="yt%d" % c, tag="bank%d" % (4 + c % 2))
             nc.tensor.matmul_mx(
                 out=yt[:],
                 lhsT=hq[c][:].bitcast(FP8X4),
@@ -195,25 +215,23 @@ def tile_picked_modres_glusilu_p_kernel(
             nc.scalar.activation(ygt[c][:], yt[:], COPY, scale=gcol[:, c : c + 1])
 
         def turn_back(c):
-            yb = psum.tile([P, BLOCKS, CH], F32, name="yb%d" % c, tag="b%d" % c)
+            yb = psum.tile([P, BLOCKS, CH], F32, name="yb%d" % c, tag="bank%d" % (6, 7, 0, 1)[c])
             for b in range(BLOCKS):
                 nc.tensor.transpose(yb[:, b, :], ygt[c][:, b * P : (b + 1) * P], ident[:])
             for b in range(BLOCKS):
                 nc.scalar.copy(yg[b][:, c * CH : (c + 1) * CH], yb[:, b, :])
 
-        gather_res(0, "grouped3")
-        hmul(0)
-        hmul(1)
-        hquant(0)
-        hmul(2)
+        for c in range(CHUNKS):
+            hmul(1, c, ub[c][:])
+        for c in range(CHUNKS):
+            turn_h(c)
+        for c in range(CHUNKS):
+            hquant(c)
+        gather_res(0, "hb0")
+        gather_res(1, "hg3")
         second_product(0)
-        hquant(1)
-        hmul(3)
         second_product(1)
         turn_back(0)
-        hquant(2)
-        hquant(3)
-        gather_res(1, "hb3")
         second_product(2)
         turn_back(1)
         second_product(3)

@@ -25,7 +25,7 @@ CH = 128
 CHUNKS = S // CH
 HALF = H // 2
 BLOCKS = N // P
-VSHARE = [0,32,0,64,0,64,0,40]
+VSHARE = [0,64,0,64,0,64,0,64]
 SCATTERS = [(0, 0, 1), (1, 0, 1), (0, 1, 2), (1, 1, 2), (0, 2, 4), (1, 2, 4)]
 
 
@@ -46,6 +46,10 @@ def tile_picked_modres_glusilu_p_kernel(
         nc.gpsimd.memset(w2s[:].bitcast(I32), 0)
         ident = keep.tile([P, P], F32, name="ident")
         make_identity(nc, ident[:])
+
+        warm = keep.tile([P, 2], F32, name="warm")
+        nc.gpsimd.memset(warm[:, 0:1], 0.0)
+        nc.scalar.activation(warm[:, 1:2], warm[:, 0:1], SILU)
 
         x_tab = [keep.tile([P, T], U32, name="x_tab%d" % g, align_bytes=64) for g in range(PASSES)]
         raw = [keep.tile([P, PACK, HALF], F32, name="raw%d" % i) for i in range(8)]
@@ -77,7 +81,6 @@ def tile_picked_modres_glusilu_p_kernel(
         w2q = keep.tile([P, N], U32, name="w2q", align_bytes=64)
         gcol = keep.tile([P, CHUNKS], F32, name="gcol")
         nc.sync.dma_start(win[0][:], res[0:P, :])
-        nc.sync.dma_start(win[1][:], res[P : 2 * P, :])
         nc.sync.dma_start(w2q[:].bitcast(I32), w2_words[0].rearrange("p n t -> p (n t)").bitcast(I32))
         for q in range(4):
             nc.sync.dma_start(
@@ -85,6 +88,8 @@ def tile_picked_modres_glusilu_p_kernel(
             )
         with nc.allow_non_contiguous_dma(reason="one gate weight to a partition"):
             nc.sync.dma_start(gcol[:], gate[0, :].rearrange("(c p) -> p c", p=P))
+
+        nc.sync.dma_start(win[1][:], res[P : 2 * P, :])
 
         xq = [keep.tile([P, S], U32, name="xq%d" % g, align_bytes=64) for g in range(PASSES)]
         xs = keep.tile([P, S], U8, name="xs", align_bytes=64)
@@ -227,7 +232,7 @@ def tile_picked_modres_glusilu_p_kernel(
             turn_h(c)
         for c in range(CHUNKS):
             hquant(c)
-        gather_res(0, "hb0")
+        gather_res(0, "hb2")
         gather_res(1, "hg3")
         second_product(0)
         second_product(1)

@@ -42,6 +42,8 @@ def tile_picked_modres_glusilu_p_kernel(
 
         xs_tab = keep.tile([P, T], U8, name="xs_tab", align_bytes=64)
         nc.gpsimd.memset(xs_tab[:].bitcast(I32), 0)
+        gate_rows = keep.tile([P, P], F32, name="gate_rows")
+        nc.gpsimd.memset(gate_rows[:], 0.0)
         w2s = keep.tile([P, N], U8, name="w2s", align_bytes=64)
         nc.gpsimd.memset(w2s[:].bitcast(I32), 0)
         ident = keep.tile([P, P], F32, name="ident")
@@ -73,23 +75,26 @@ def tile_picked_modres_glusilu_p_kernel(
                 xs_tab[32 * q : 32 * q + 4 * PASSES, :].bitcast(I32),
                 x_scales[:, 4 * q : 4 * q + 4, :].bitcast(I32),
             )
+        nc.sync.dma_start(gate_rows[0:CHUNKS, :], gate[0, :].rearrange("(c p) -> c p", p=P))
         load_x(1)
         for i in range(8):
             load_w(i)
 
         win = [keep.tile([P, T], F32, name="win%d" % b) for b in range(BLOCKS)]
         w2q = keep.tile([P, N], U32, name="w2q", align_bytes=64)
-        gcol = keep.tile([P, CHUNKS], F32, name="gcol")
         nc.sync.dma_start(win[0][:], res[0:P, :])
         nc.sync.dma_start(w2q[:].bitcast(I32), w2_words[0].rearrange("p n t -> p (n t)").bitcast(I32))
         for q in range(4):
             nc.sync.dma_start(
                 w2s[32 * q : 32 * q + 4, :].bitcast(I32), w2_scales[0, 4 * q : 4 * q + 4, :].bitcast(I32)
             )
-        with nc.allow_non_contiguous_dma(reason="one gate weight to a partition"):
-            nc.sync.dma_start(gcol[:], gate[0, :].rearrange("(c p) -> p c", p=P))
 
         nc.sync.dma_start(win[1][:], res[P : 2 * P, :])
+
+        gcol = keep.tile([P, CHUNKS], F32, name="gcol")
+        gate_turned = psum.tile([P, P], F32, name="gate_turned", tag="bank7")
+        nc.tensor.transpose(gate_turned[:], gate_rows[:], ident[:])
+        nc.scalar.copy(gcol[:], gate_turned[:, 0:CHUNKS])
 
         xq = [keep.tile([P, S], U32, name="xq%d" % g, align_bytes=64) for g in range(PASSES)]
         xs = keep.tile([P, S], U8, name="xs", align_bytes=64)

@@ -20,13 +20,20 @@ COPY = mybir.ActivationFunctionType.Copy
 
 P = 128
 PACK = 4
+QUADRANTS = 4
+SCALE_ROWS = 4
 PASSES = K // (P * PACK)
-CH = 128
-CHUNKS = S // CH
-HALF = H // 2
+CHUNK = 128
+CHUNKS = S // CHUNK
+LIST_COLS = CHUNK // 16
 BLOCKS = N // P
-VSHARE = [0,64,0,64,0,64,0,64]
-SCATTERS = [(0, 0, 1), (1, 0, 1), (0, 1, 2), (1, 1, 2), (0, 2, 4), (1, 2, 4)]
+HALF = H // 2
+RUN = 4
+MX_ALIGN = 64
+
+LAG = 3
+
+SCATTER_RANGES = [(0, 1), (1, 2), (2, 4)]
 
 
 def tile_picked_modres_glusilu_p_kernel(
@@ -37,224 +44,182 @@ def tile_picked_modres_glusilu_p_kernel(
         keep = ctx.enter_context(tc.tile_pool(name="keep", bufs=1))
         psum = ctx.enter_context(tc.psum_pool(name="psum", bufs=1))
 
+        def mx_tile(shape, dtype, name):
+            return keep.tile(shape, dtype, name=name, align_bytes=MX_ALIGN)
+
         offsets = keep.tile([P, S // 16], U16, name="offsets")
         nc.sync.dma_start(offsets[:], offs)
 
-        xs_tab = keep.tile([P, T], U8, name="xs_tab", align_bytes=64)
-        nc.gpsimd.memset(xs_tab[:].bitcast(I32), 0)
+        x_scale_table = mx_tile([P, T], U8, "x_scale_table")
+        nc.gpsimd.memset(x_scale_table[:].bitcast(I32), 0)
         gate_rows = keep.tile([P, P], F32, name="gate_rows")
         nc.gpsimd.memset(gate_rows[:], 0.0)
-        w2s = keep.tile([P, N], U8, name="w2s", align_bytes=64)
-        nc.gpsimd.memset(w2s[:].bitcast(I32), 0)
-        ident = keep.tile([P, P], F32, name="ident")
-        make_identity(nc, ident[:])
+        w2_scale = mx_tile([P, N], U8, "w2_scale")
+        nc.gpsimd.memset(w2_scale[:].bitcast(I32), 0)
+        identity = keep.tile([P, P], F32, name="identity")
+        make_identity(nc, identity[:])
 
-        warm = keep.tile([P, 2], F32, name="warm")
-        nc.gpsimd.memset(warm[:, 0:1], 0.0)
-        nc.scalar.activation(warm[:, 1:2], warm[:, 0:1], SILU)
+        def load_words(tile, words):
+            nc.sync.dma_start(tile[:].bitcast(I32), words.rearrange("p n t -> p (n t)").bitcast(I32))
 
-        x_tab = [keep.tile([P, T], U32, name="x_tab%d" % g, align_bytes=64) for g in range(PASSES)]
-        raw = [keep.tile([P, PACK, HALF], F32, name="raw%d" % i) for i in range(8)]
+        def load_weight(w, g, cols, name):
+            raw = keep.tile([P, PACK, cols.stop - cols.start], F32, name=name)
+            rows = w[g * P * PACK : (g + 1) * P * PACK, cols]
+            nc.sync.dma_start(raw[:], rows.rearrange("(p j) c -> p j c", j=PACK))
+            return raw
 
-        def load_x(g):
+        x_table = [mx_tile([P, T], U32, "x_table%d" % g) for g in range(PASSES)]
+        load_words(x_table[0], x_words[0])
+        for q in range(QUADRANTS):
             nc.sync.dma_start(
-                x_tab[g][:].bitcast(I32), x_words[g].rearrange("p n t -> p (n t)").bitcast(I32)
+                x_scale_table[32 * q : 32 * q + SCALE_ROWS * PASSES, :].bitcast(I32),
+                x_scales[:, SCALE_ROWS * q : SCALE_ROWS * (q + 1), :].bitcast(I32),
             )
+        nc.sync.dma_start(gate_rows[0:CHUNKS, :], gate[0, :].rearrange("(c p) -> c p", p=CHUNK))
+        w1_raw0 = load_weight(w1, 0, slice(0, H), "w1_raw0")
+        load_words(x_table[1], x_words[1])
+        w1_raw1 = load_weight(w1, 1, slice(0, H), "w1_raw1")
+        w3_raw0 = load_weight(w3, 0, slice(0, H), "w3_raw0")
+        w3_raw1 = [load_weight(w3, 1, slice(u * HALF, (u + 1) * HALF), "w3_raw1%d" % u) for u in range(2)]
 
-        def piece(u, w, g):
-            return 4 * u + 2 * w + g
-
-        def load_w(i):
-            u, w, g = i // 4, (i // 2) % 2, i % 2
-            rows = (w1, w3)[w][g * P * PACK : (g + 1) * P * PACK, u * HALF : (u + 1) * HALF]
-            nc.sync.dma_start(raw[i][:], rows.rearrange("(p j) c -> p j c", j=PACK))
-
-        load_x(0)
-        for q in range(4):
+        stream = [keep.tile([P, T], F32, name="stream%d" % b) for b in range(BLOCKS)]
+        w2_codes = mx_tile([P, N], U32, "w2_codes")
+        nc.sync.dma_start(stream[0][:], res[0:P, :])
+        load_words(w2_codes, w2_words[0])
+        for q in range(QUADRANTS):
             nc.sync.dma_start(
-                xs_tab[32 * q : 32 * q + 4 * PASSES, :].bitcast(I32),
-                x_scales[:, 4 * q : 4 * q + 4, :].bitcast(I32),
+                w2_scale[32 * q : 32 * q + SCALE_ROWS, :].bitcast(I32),
+                w2_scales[0, SCALE_ROWS * q : SCALE_ROWS * (q + 1), :].bitcast(I32),
             )
-        nc.sync.dma_start(gate_rows[0:CHUNKS, :], gate[0, :].rearrange("(c p) -> c p", p=P))
-        load_x(1)
-        for i in range(8):
-            load_w(i)
+        nc.sync.dma_start(stream[1][:], res[P : 2 * P, :])
 
-        win = [keep.tile([P, T], F32, name="win%d" % b) for b in range(BLOCKS)]
-        w2q = keep.tile([P, N], U32, name="w2q", align_bytes=64)
-        nc.sync.dma_start(win[0][:], res[0:P, :])
-        nc.sync.dma_start(w2q[:].bitcast(I32), w2_words[0].rearrange("p n t -> p (n t)").bitcast(I32))
-        for q in range(4):
-            nc.sync.dma_start(
-                w2s[32 * q : 32 * q + 4, :].bitcast(I32), w2_scales[0, 4 * q : 4 * q + 4, :].bitcast(I32)
-            )
+        def bank(kind, c, shape, name):
+            return psum.tile(shape, F32, name="%s%d" % (name, c), tag="%s%d" % (kind, c))
 
-        nc.sync.dma_start(win[1][:], res[P : 2 * P, :])
+        gate_cols = keep.tile([P, CHUNKS], F32, name="gate_cols")
+        gate_turned = bank("b", CHUNKS - 1, [P, P], "gate_turned")
+        nc.tensor.transpose(gate_turned[:], gate_rows[:], identity[:])
+        nc.scalar.copy(gate_cols[:], gate_turned[:, 0:CHUNKS])
 
-        gcol = keep.tile([P, CHUNKS], F32, name="gcol")
-        gate_turned = psum.tile([P, P], F32, name="gate_turned", tag="bank7")
-        nc.tensor.transpose(gate_turned[:], gate_rows[:], ident[:])
-        nc.scalar.copy(gcol[:], gate_turned[:, 0:CHUNKS])
+        x_codes = [mx_tile([P, S], U32, "x_codes%d" % g) for g in range(PASSES)]
+        x_scale = mx_tile([P, S], U8, "x_scale")
+        nc.vector.tensor_copy(x_codes[0][:], x_table[0][:].indirect(offsets[:]))
+        nc.vector.tensor_copy(x_scale[:], x_scale_table[:].indirect(offsets[:]))
+        nc.vector.tensor_copy(x_codes[1][:], x_table[1][:].indirect(offsets[:]))
 
-        xq = [keep.tile([P, S], U32, name="xq%d" % g, align_bytes=64) for g in range(PASSES)]
-        xs = keep.tile([P, S], U8, name="xs", align_bytes=64)
-        nc.vector.tensor_copy(xq[0][:], x_tab[0][:].indirect(offsets[:]))
-        nc.vector.tensor_copy(xs[:], xs_tab[:].indirect(offsets[:]))
-        nc.vector.tensor_copy(xq[1][:], x_tab[1][:].indirect(offsets[:]))
-
-        grouped = [
-            keep.tile([P, HALF, PACK], BF16, name="grouped%d" % i, tag="grouped%d" % i, align_bytes=64)
-            for i in range(8)
-        ]
-        wq = [keep.tile([P, HALF], U32, name="wq%d" % i, align_bytes=64) for i in range(8)]
-        ws = [keep.tile([P, HALF], U8, name="ws%d" % i, align_bytes=64) for i in range(8)]
-
-        def cast(i):
-            src = raw[i][:].rearrange("p j (c e) -> p c j e", e=4)
-            dst = grouped[i][:].rearrange("p (c e) j -> p c j e", e=4)
-            cut = HALF // 4 - VSHARE[i]
-            if cut > 0:
-                nc.scalar.copy(dst[:, 0:cut], src[:, 0:cut])
-            if cut < HALF // 4:
+        def cast(raw, scalar_cols, name):
+            width = raw.shape[2]
+            grouped = mx_tile([P, width, PACK], BF16, name)
+            src = raw[:].rearrange("p j (c e) -> p c j e", e=RUN)
+            dst = grouped[:].rearrange("p (c e) j -> p c j e", e=RUN)
+            cut = scalar_cols // RUN
+            if scalar_cols > 0:
+                nc.scalar.copy(dst[:, :cut], src[:, :cut])
+            if scalar_cols < width:
                 nc.vector.tensor_copy(dst[:, cut:], src[:, cut:])
+            return grouped
 
-        def quant_w(i):
+        def quantise(grouped, codes, scale):
             nc.vector.quantize_mx(
-                out=wq[i][:].bitcast(FP8X4), scales=ws[i][:], in_=grouped[i][:].rearrange("p c j -> p (c j)")
+                out=codes.bitcast(FP8X4), scales=scale, in_=grouped[:].rearrange("p c j -> p (c j)")
             )
 
-        def first_pass(u, w, c, g, acc):
-            toks = slice(c * CH, (c + 1) * CH)
-            i = piece(u, w, g)
-            nc.tensor.matmul_mx(
-                out=acc,
-                lhsT=xq[g][:, toks].bitcast(FP8X4),
-                lhsT_scale=xs[4 * g : P, toks],
-                rhs=wq[i][:].bitcast(FP8X4),
-                rhs_scale=ws[i][:],
-                start=(g == 0),
-                stop=(g == PASSES - 1),
-            )
+        w1_codes = [mx_tile([P, H], U32, "w1_codes%d" % g) for g in range(PASSES)]
+        w1_scale = [mx_tile([P, H], U8, "w1_scale%d" % g) for g in range(PASSES)]
+        w3_codes = [mx_tile([P, H], U32, "w3_codes%d" % g) for g in range(PASSES)]
+        w3_scale = [mx_tile([P, H], U8, "w3_scale%d" % g) for g in range(PASSES)]
 
-        def pair_product(u, w, banks):
-            accs = [psum.tile([P, 2, HALF], F32, name="acc%d%d%d" % (u, w, cp), tag="bank%d" % banks[cp]) for cp in range(2)]
-            for cp in range(2):
-                first_pass(u, w, 2 * cp, 0, accs[cp][:, 0, :])
-            for cp in range(2):
-                first_pass(u, w, 2 * cp, 1, accs[cp][:, 0, :])
-                for g in range(PASSES):
-                    first_pass(u, w, 2 * cp + 1, g, accs[cp][:, 1, :])
+        def first_product(kind, codes, scale, name):
+            accs = [bank(kind, c, [CHUNK, H], name) for c in range(CHUNKS)]
+            for g in range(PASSES):
+                for c in range(CHUNKS):
+                    entries = slice(c * CHUNK, (c + 1) * CHUNK)
+                    nc.tensor.matmul_mx(
+                        out=accs[c][:],
+                        lhsT=x_codes[g][:, entries].bitcast(FP8X4),
+                        lhsT_scale=x_scale[SCALE_ROWS * g : P, entries],
+                        rhs=codes[g][:].bitcast(FP8X4),
+                        rhs_scale=scale[g][:],
+                        start=(g == 0),
+                        stop=(g == PASSES - 1),
+                    )
             return accs
 
-        act = [[keep.tile([P, 2, HALF], F32, name="act%d%d" % (u, cp)) for cp in range(2)] for u in range(2)]
-        hb = [keep.tile([P, H], BF16, name="hb%d" % c, tag="hb%d" % c, align_bytes=64) for c in range(CHUNKS)]
+        quantise(cast(w1_raw0, H, "w1_grouped0"), w1_codes[0][:], w1_scale[0][:])
+        quantise(cast(w1_raw1, HALF, "w1_grouped1"), w1_codes[1][:], w1_scale[1][:])
+        w1_acc = first_product("a", w1_codes, w1_scale, "w1_acc")
+        quantise(cast(w3_raw0, 0, "w3_grouped0"), w3_codes[0][:], w3_scale[0][:])
+        for u in range(2):
+            cols = slice(u * HALF, (u + 1) * HALF)
+            quantise(cast(w3_raw1[u], 0, "w3_grouped1%d" % u), w3_codes[1][:, cols], w3_scale[1][:, cols])
+        w3_acc = first_product("b", w3_codes, w3_scale, "w3_acc")
 
-        def silu(u, cp, acc):
-            nc.scalar.activation(act[u][cp][:], acc[:], SILU)
+        def by_word_half(acc):
+            return acc[:].rearrange("n (p e r) -> n e p r", e=2, r=2)
 
-        def hmul(u, c, acc):
-            nc.vector.tensor_tensor(hb[c][:, u * HALF : (u + 1) * HALF], acc, act[u][c // 2][:, c % 2, :], MULT)
-
-        cast(0)
-        cast(1)
-        quant_w(0)
-        quant_w(1)
-        ga = pair_product(0, 0, (0, 1))
-        cast(2)
-        cast(3)
-        quant_w(2)
-        quant_w(3)
-        ua = pair_product(0, 1, (2, 3))
-        cast(4)
-        cast(5)
-        quant_w(4)
-        quant_w(5)
-        gb = pair_product(1, 0, (4, 5))
-        cast(6)
-        cast(7)
-        quant_w(6)
-        quant_w(7)
-        for cp in range(2):
-            silu(0, cp, ga[cp])
+        silu = [keep.tile([CHUNK, 2, P, 2], F32, name="silu%d" % c) for c in range(CHUNKS)]
         for c in range(CHUNKS):
-            hmul(0, c, ua[c // 2][:, c % 2, :])
-        for cp in range(2):
-            silu(1, cp, gb[cp])
-        ub = [psum.tile([P, HALF], F32, name="ub%d" % c, tag="bank%d" % (6, 7, 0, 1)[c]) for c in range(CHUNKS)]
-        for g in range(PASSES):
-            for c in range(CHUNKS):
-                first_pass(1, 1, c, g, ub[c][:])
+            nc.scalar.activation(silu[c][:], by_word_half(w1_acc[c]), SILU)
 
-        hg = [keep.tile([P, CH, PACK], BF16, name="hg%d" % c, tag="hg%d" % c, align_bytes=64) for c in range(CHUNKS)]
-        hq = [keep.tile([P, CH], U32, name="hq%d" % c, align_bytes=64) for c in range(CHUNKS)]
-        hs = [keep.tile([P, CH], U8, name="hs%d" % c, align_bytes=64) for c in range(CHUNKS)]
-        ygt = [keep.tile([P, N], F32, name="ygt%d" % c) for c in range(CHUNKS)]
-        yg = [keep.tile([P, S], F32, name="yg%d" % b) for b in range(BLOCKS)]
-        rg = [None, None]
+        h_codes = [mx_tile([P, CHUNK], U32, "h_codes%d" % c) for c in range(CHUNKS)]
+        h_scale = [mx_tile([P, CHUNK], U8, "h_scale%d" % c) for c in range(CHUNKS)]
+        h_grouped = [mx_tile([P, CHUNK, PACK], BF16, "h_grouped%d" % c) for c in range(CHUNKS)]
+        gated_rows = [keep.tile([CHUNK, N], F32, name="gated_rows%d" % c) for c in range(CHUNKS)]
+        gated = [keep.tile([P, S], F32, name="gated%d" % b) for b in range(BLOCKS)]
+        picked_res = [keep.tile([P, S], F32, name="picked_res%d" % b) for b in range(BLOCKS)]
 
-        def gather_res(b, tag):
-            rg[b] = keep.tile([P, S], F32, name="rg%d" % b, tag=tag, align_bytes=64)
-            nc.vector.tensor_copy(rg[b][:], win[b][:].indirect(offsets[:]))
-
-        def turn_h(c):
-            words = hb[c][:].bitcast(F32)
-            ht = psum.tile([P, 2, CH], F32, name="ht%d" % c, tag="bank%d" % (2 + c % 2))
+        def make_h(c):
+            h = keep.tile([CHUNK, 2, P, 2], BF16, name="h%d" % c)
+            nc.vector.tensor_tensor(h[:], by_word_half(w3_acc[c]), silu[c][:], MULT)
+            pairs = h[:].rearrange("n e p r -> n (e p r)").bitcast(F32)
+            turned = bank("a", c, [P, 2, CHUNK], "h_turned")
             for e in range(2):
-                nc.tensor.transpose(ht[:, e, :], words[:, e : H // 2 : 2], ident[:])
+                nc.tensor.transpose(turned[:, e, :], pairs[:, e * P : (e + 1) * P], identity[:])
             nc.scalar.copy(
-                hg[c][:].rearrange("p n t -> p (n t)").bitcast(F32).rearrange("p (n e) -> p n e", e=2),
-                ht[:].rearrange("p e n -> p n e"),
-            )
-
-        def hquant(c):
-            nc.vector.quantize_mx(
-                out=hq[c][:].bitcast(FP8X4), scales=hs[c][:], in_=hg[c][:].rearrange("p n t -> p (n t)")
+                h_grouped[c][:].rearrange("p n t -> p (n t)").bitcast(F32).rearrange("p (n e) -> p n e", e=2),
+                turned[:].rearrange("p e n -> p n e"),
             )
 
         def second_product(c):
-            yt = psum.tile([P, N], F32, name="yt%d" % c, tag="bank%d" % (4 + c % 2))
+            y = bank("b", c, [CHUNK, N], "y")
             nc.tensor.matmul_mx(
-                out=yt[:],
-                lhsT=hq[c][:].bitcast(FP8X4),
-                lhsT_scale=hs[c][:],
-                rhs=w2q[:].bitcast(FP8X4),
-                rhs_scale=w2s[:],
+                out=y[:],
+                lhsT=h_codes[c][:].bitcast(FP8X4),
+                lhsT_scale=h_scale[c][:],
+                rhs=w2_codes[:].bitcast(FP8X4),
+                rhs_scale=w2_scale[:],
                 start=True,
                 stop=True,
             )
-            nc.scalar.activation(ygt[c][:], yt[:], COPY, scale=gcol[:, c : c + 1])
+            nc.scalar.activation(gated_rows[c][:], y[:], COPY, scale=gate_cols[:, c : c + 1])
 
         def turn_back(c):
-            yb = psum.tile([P, BLOCKS, CH], F32, name="yb%d" % c, tag="bank%d" % (6, 7, 0, 1)[c])
+            turned = bank("a", c, [P, BLOCKS, CHUNK], "y_turned")
             for b in range(BLOCKS):
-                nc.tensor.transpose(yb[:, b, :], ygt[c][:, b * P : (b + 1) * P], ident[:])
+                nc.tensor.transpose(turned[:, b, :], gated_rows[c][:, b * P : (b + 1) * P], identity[:])
             for b in range(BLOCKS):
-                nc.scalar.copy(yg[b][:, c * CH : (c + 1) * CH], yb[:, b, :])
+                nc.scalar.copy(gated[b][:, c * CHUNK : (c + 1) * CHUNK], turned[:, b, :])
 
-        for c in range(CHUNKS):
-            hmul(1, c, ub[c][:])
-        for c in range(CHUNKS):
-            turn_h(c)
-        for c in range(CHUNKS):
-            hquant(c)
-        gather_res(0, "hb2")
-        gather_res(1, "hg3")
-        second_product(0)
-        second_product(1)
-        turn_back(0)
-        second_product(2)
-        turn_back(1)
-        second_product(3)
-        turn_back(2)
-        turn_back(3)
+        for step in range(CHUNKS + LAG):
+            if step >= LAG:
+                c = step - LAG
+                quantise(h_grouped[c], h_codes[c][:], h_scale[c][:])
+                second_product(c)
+                turn_back(c)
+            if step < CHUNKS:
+                make_h(step)
 
-        for b, c0, c1 in SCATTERS:
-            toks = slice(c0 * CH, c1 * CH)
-            nc.vector.tensor_tensor(
-                win[b][:].indirect(offsets[:, c0 * CH // 16 : c1 * CH // 16]),
-                yg[b][:, toks],
-                rg[b][:, toks],
-                ADD,
-            )
-            if c1 == CHUNKS:
-                nc.sync.dma_start(out[b * P : (b + 1) * P, :], win[b][:])
+        for b in range(BLOCKS):
+            nc.vector.tensor_copy(picked_res[b][:], stream[b][:].indirect(offsets[:]))
+
+        for c0, c1 in SCATTER_RANGES:
+            entries = slice(c0 * CHUNK, c1 * CHUNK)
+            for b in range(BLOCKS):
+                nc.vector.tensor_tensor(
+                    stream[b][:].indirect(offsets[:, c0 * LIST_COLS : c1 * LIST_COLS]),
+                    gated[b][:, entries],
+                    picked_res[b][:, entries],
+                    ADD,
+                )
+        for b in range(BLOCKS):
+            nc.sync.dma_start(out[b * P : (b + 1) * P, :], stream[b][:])

@@ -27,11 +27,11 @@ CHUNK = 128
 CHUNKS = S // CHUNK
 LIST_COLS = CHUNK // 16
 BLOCKS = N // P
-HALF = H // 2
+SCALAR_SHARE = 176
 RUN = 4
 MX_ALIGN = 64
 
-LAG = 3
+LAG = 1
 
 SCATTER_RANGES = [(0, 1), (1, 2), (2, 4)]
 
@@ -44,8 +44,8 @@ def tile_picked_modres_glusilu_p_kernel(
         keep = ctx.enter_context(tc.tile_pool(name="keep", bufs=1))
         psum = ctx.enter_context(tc.psum_pool(name="psum", bufs=1))
 
-        def mx_tile(shape, dtype, name):
-            return keep.tile(shape, dtype, name=name, align_bytes=MX_ALIGN)
+        def mx_tile(shape, dtype, name, tag=None):
+            return keep.tile(shape, dtype, name=name, tag=tag or name, align_bytes=MX_ALIGN)
 
         offsets = keep.tile([P, S // 16], U16, name="offsets")
         nc.sync.dma_start(offsets[:], offs)
@@ -63,7 +63,7 @@ def tile_picked_modres_glusilu_p_kernel(
             nc.sync.dma_start(tile[:].bitcast(I32), words.rearrange("p n t -> p (n t)").bitcast(I32))
 
         def load_weight(w, g, cols, name):
-            raw = keep.tile([P, PACK, cols.stop - cols.start], F32, name=name)
+            raw = mx_tile([P, PACK, cols.stop - cols.start], F32, name)
             rows = w[g * P * PACK : (g + 1) * P * PACK, cols]
             nc.sync.dma_start(raw[:], rows.rearrange("(p j) c -> p j c", j=PACK))
             return raw
@@ -80,7 +80,7 @@ def tile_picked_modres_glusilu_p_kernel(
         load_words(x_table[1], x_words[1])
         w1_raw1 = load_weight(w1, 1, slice(0, H), "w1_raw1")
         w3_raw0 = load_weight(w3, 0, slice(0, H), "w3_raw0")
-        w3_raw1 = [load_weight(w3, 1, slice(u * HALF, (u + 1) * HALF), "w3_raw1%d" % u) for u in range(2)]
+        w3_raw1 = load_weight(w3, 1, slice(0, H), "w3_raw1")
 
         stream = [keep.tile([P, T], F32, name="stream%d" % b) for b in range(BLOCKS)]
         w2_codes = mx_tile([P, N], U32, "w2_codes")
@@ -105,11 +105,10 @@ def tile_picked_modres_glusilu_p_kernel(
         x_scale = mx_tile([P, S], U8, "x_scale")
         nc.vector.tensor_copy(x_codes[0][:], x_table[0][:].indirect(offsets[:]))
         nc.vector.tensor_copy(x_scale[:], x_scale_table[:].indirect(offsets[:]))
-        nc.vector.tensor_copy(x_codes[1][:], x_table[1][:].indirect(offsets[:]))
 
         def cast(raw, scalar_cols, name):
             width = raw.shape[2]
-            grouped = mx_tile([P, width, PACK], BF16, name)
+            grouped = mx_tile([P, width, PACK], BF16, name, "grouped")
             src = raw[:].rearrange("p j (c e) -> p c j e", e=RUN)
             dst = grouped[:].rearrange("p (c e) j -> p c j e", e=RUN)
             cut = scalar_cols // RUN
@@ -145,19 +144,19 @@ def tile_picked_modres_glusilu_p_kernel(
                     )
             return accs
 
-        quantise(cast(w1_raw0, H, "w1_grouped0"), w1_codes[0][:], w1_scale[0][:])
-        quantise(cast(w1_raw1, HALF, "w1_grouped1"), w1_codes[1][:], w1_scale[1][:])
+        quantise(cast(w1_raw0, SCALAR_SHARE, "w1_grouped0"), w1_codes[0][:], w1_scale[0][:])
+        nc.vector.tensor_copy(x_codes[1][:], x_table[1][:].indirect(offsets[:]))
+        quantise(cast(w1_raw1, SCALAR_SHARE, "w1_grouped1"), w1_codes[1][:], w1_scale[1][:])
         w1_acc = first_product("a", w1_codes, w1_scale, "w1_acc")
         quantise(cast(w3_raw0, 0, "w3_grouped0"), w3_codes[0][:], w3_scale[0][:])
-        for u in range(2):
-            cols = slice(u * HALF, (u + 1) * HALF)
-            quantise(cast(w3_raw1[u], 0, "w3_grouped1%d" % u), w3_codes[1][:, cols], w3_scale[1][:, cols])
+        quantise(cast(w3_raw1, SCALAR_SHARE, "w3_grouped1"), w3_codes[1][:], w3_scale[1][:])
         w3_acc = first_product("b", w3_codes, w3_scale, "w3_acc")
 
         def by_word_half(acc):
             return acc[:].rearrange("n (p e r) -> n e p r", e=2, r=2)
 
-        silu = [keep.tile([CHUNK, 2, P, 2], F32, name="silu%d" % c) for c in range(CHUNKS)]
+        silu = [mx_tile([CHUNK, 2, P, 2], F32, "silu%d" % c) for c in range(CHUNKS - 1)]
+        silu.append(mx_tile([CHUNK, 2, P, 2], F32, "silu_last", "w3_raw1"))
         for c in range(CHUNKS):
             nc.scalar.activation(silu[c][:], by_word_half(w1_acc[c]), SILU)
 
@@ -166,7 +165,6 @@ def tile_picked_modres_glusilu_p_kernel(
         h_grouped = [mx_tile([P, CHUNK, PACK], BF16, "h_grouped%d" % c) for c in range(CHUNKS)]
         gated_rows = [keep.tile([CHUNK, N], F32, name="gated_rows%d" % c) for c in range(CHUNKS)]
         gated = [keep.tile([P, S], F32, name="gated%d" % b) for b in range(BLOCKS)]
-        picked_res = [keep.tile([P, S], F32, name="picked_res%d" % b) for b in range(BLOCKS)]
 
         def make_h(c):
             h = keep.tile([CHUNK, 2, P, 2], BF16, name="h%d" % c)
@@ -200,6 +198,16 @@ def tile_picked_modres_glusilu_p_kernel(
             for b in range(BLOCKS):
                 nc.scalar.copy(gated[b][:, c * CHUNK : (c + 1) * CHUNK], turned[:, b, :])
 
+        half = S // 2
+        picked_res = {}
+
+        def gather_res(b, u, buffer):
+            picked_res[b, u] = mx_tile([P, half], F32, "picked_res%d%d" % (b, u), buffer)
+            nc.vector.tensor_copy(
+                picked_res[b, u][:], stream[b][:].indirect(offsets[:, u * half // 16 : (u + 1) * half // 16])
+            )
+
+        gather_res(0, 0, "grouped")
         for step in range(CHUNKS + LAG):
             if step >= LAG:
                 c = step - LAG
@@ -208,17 +216,18 @@ def tile_picked_modres_glusilu_p_kernel(
                 turn_back(c)
             if step < CHUNKS:
                 make_h(step)
-
-        for b in range(BLOCKS):
-            nc.vector.tensor_copy(picked_res[b][:], stream[b][:].indirect(offsets[:]))
+        gather_res(1, 0, "h_grouped0")
+        gather_res(0, 1, "h_grouped1")
+        gather_res(1, 1, "h_grouped2")
 
         for c0, c1 in SCATTER_RANGES:
             entries = slice(c0 * CHUNK, c1 * CHUNK)
+            u = entries.start // half
             for b in range(BLOCKS):
                 nc.vector.tensor_tensor(
                     stream[b][:].indirect(offsets[:, c0 * LIST_COLS : c1 * LIST_COLS]),
                     gated[b][:, entries],
-                    picked_res[b][:, entries],
+                    picked_res[b, u][:, entries.start - u * half : entries.stop - u * half],
                     ADD,
                 )
         for b in range(BLOCKS):

@@ -48,7 +48,6 @@ def tile_picked_modres_glusilu_p_kernel(
             return keep.tile(shape, dtype, name=name, tag=tag or name, align_bytes=MX_ALIGN)
 
         offsets = keep.tile([P, S // 16], U16, name="offsets")
-        nc.sync.dma_start(offsets[:], offs)
 
         x_scale_table = mx_tile([P, T], U8, "x_scale_table")
         nc.gpsimd.memset(x_scale_table[:].bitcast(I32), 0)
@@ -70,6 +69,7 @@ def tile_picked_modres_glusilu_p_kernel(
 
         x_table = [mx_tile([P, T], U32, "x_table%d" % g) for g in range(PASSES)]
         load_words(x_table[0], x_words[0])
+        nc.sync.dma_start(offsets[:], offs)
         for q in range(QUADRANTS):
             nc.sync.dma_start(
                 x_scale_table[32 * q : 32 * q + SCALE_ROWS * PASSES, :].bitcast(I32),
@@ -114,14 +114,20 @@ def tile_picked_modres_glusilu_p_kernel(
             cut = scalar_cols // RUN
             if scalar_cols > 0:
                 nc.scalar.copy(dst[:, :cut], src[:, :cut])
-            if scalar_cols < width:
-                nc.vector.tensor_copy(dst[:, cut:], src[:, cut:])
+            middle = width // 2 // RUN
+            nc.vector.tensor_copy(dst[:, cut:middle], src[:, cut:middle])
+            nc.vector.tensor_copy(dst[:, middle:], src[:, middle:])
             return grouped
 
         def quantise(grouped, codes, scale):
             nc.vector.quantize_mx(
-                out=codes.bitcast(FP8X4), scales=scale, in_=grouped[:].rearrange("p c j -> p (c j)")
+                out=codes.bitcast(FP8X4), scales=scale, in_=grouped.rearrange("p c j -> p (c j)")
             )
+
+        def quantise_halves(grouped, codes, scale):
+            for u in range(2):
+                cols = slice(u * H // 2, (u + 1) * H // 2)
+                quantise(grouped[:, cols], codes[:, cols], scale[:, cols])
 
         w1_codes = [mx_tile([P, H], U32, "w1_codes%d" % g) for g in range(PASSES)]
         w1_scale = [mx_tile([P, H], U8, "w1_scale%d" % g) for g in range(PASSES)]
@@ -144,12 +150,12 @@ def tile_picked_modres_glusilu_p_kernel(
                     )
             return accs
 
-        quantise(cast(w1_raw0, SCALAR_SHARE, "w1_grouped0"), w1_codes[0][:], w1_scale[0][:])
+        quantise_halves(cast(w1_raw0, SCALAR_SHARE, "w1_grouped0"), w1_codes[0], w1_scale[0])
         nc.vector.tensor_copy(x_codes[1][:], x_table[1][:].indirect(offsets[:]))
-        quantise(cast(w1_raw1, SCALAR_SHARE, "w1_grouped1"), w1_codes[1][:], w1_scale[1][:])
+        quantise_halves(cast(w1_raw1, SCALAR_SHARE, "w1_grouped1"), w1_codes[1], w1_scale[1])
         w1_acc = first_product("a", w1_codes, w1_scale, "w1_acc")
-        quantise(cast(w3_raw0, 0, "w3_grouped0"), w3_codes[0][:], w3_scale[0][:])
-        quantise(cast(w3_raw1, SCALAR_SHARE, "w3_grouped1"), w3_codes[1][:], w3_scale[1][:])
+        quantise_halves(cast(w3_raw0, 0, "w3_grouped0"), w3_codes[0], w3_scale[0])
+        quantise_halves(cast(w3_raw1, SCALAR_SHARE, "w3_grouped1"), w3_codes[1], w3_scale[1])
         w3_acc = first_product("b", w3_codes, w3_scale, "w3_acc")
 
         def by_word_half(acc):
@@ -179,7 +185,7 @@ def tile_picked_modres_glusilu_p_kernel(
             )
 
         def second_product(c):
-            y = bank("b", c, [CHUNK, N], "y")
+            y = bank("b", c, [CHUNK, N], "y") if c < 2 else bank("a", c - 2, [CHUNK, N], "y_late")
             nc.tensor.matmul_mx(
                 out=y[:],
                 lhsT=h_codes[c][:].bitcast(FP8X4),
@@ -211,7 +217,7 @@ def tile_picked_modres_glusilu_p_kernel(
         for step in range(CHUNKS + LAG):
             if step >= LAG:
                 c = step - LAG
-                quantise(h_grouped[c], h_codes[c][:], h_scale[c][:])
+                quantise(h_grouped[c][:], h_codes[c][:], h_scale[c][:])
                 second_product(c)
                 turn_back(c)
             if step < CHUNKS:

@@ -27,12 +27,9 @@ CHUNK = 128
 CHUNKS = S // CHUNK
 LIST_COLS = CHUNK // 16
 BLOCKS = N // P
-SCALAR_SHARE = 176
-RUN = 4
+SCALAR_SHARE = 44
 MX_ALIGN = 64
-
-LAG = 1
-
+LAG = 4
 SCATTER_RANGES = [(0, 1), (1, 2), (2, 4)]
 
 
@@ -48,7 +45,6 @@ def tile_picked_modres_glusilu_p_kernel(
             return keep.tile(shape, dtype, name=name, tag=tag or name, align_bytes=MX_ALIGN)
 
         offsets = keep.tile([P, S // 16], U16, name="offsets")
-
         x_scale_table = mx_tile([P, T], U8, "x_scale_table")
         nc.gpsimd.memset(x_scale_table[:].bitcast(I32), 0)
         gate_rows = keep.tile([P, P], F32, name="gate_rows")
@@ -61,9 +57,9 @@ def tile_picked_modres_glusilu_p_kernel(
         def load_words(tile, words):
             nc.sync.dma_start(tile[:].bitcast(I32), words.rearrange("p n t -> p (n t)").bitcast(I32))
 
-        def load_weight(w, g, cols, name):
-            raw = mx_tile([P, PACK, cols.stop - cols.start], F32, name)
-            rows = w[g * P * PACK : (g + 1) * P * PACK, cols]
+        def load_weight(w, g, name):
+            raw = mx_tile([P, PACK, H], F32, name)
+            rows = w[g * P * PACK : (g + 1) * P * PACK, :]
             nc.sync.dma_start(raw[:], rows.rearrange("(p j) c -> p j c", j=PACK))
             return raw
 
@@ -75,16 +71,15 @@ def tile_picked_modres_glusilu_p_kernel(
                 x_scale_table[32 * q : 32 * q + SCALE_ROWS * PASSES, :].bitcast(I32),
                 x_scales[:, SCALE_ROWS * q : SCALE_ROWS * (q + 1), :].bitcast(I32),
             )
-        nc.sync.dma_start(gate_rows[0:CHUNKS, :], gate[0, :].rearrange("(c p) -> c p", p=CHUNK))
-        w1_raw0 = load_weight(w1, 0, slice(0, H), "w1_raw0")
+        w1_raw0 = load_weight(w1, 0, "w1_raw0")
         load_words(x_table[1], x_words[1])
-        w1_raw1 = load_weight(w1, 1, slice(0, H), "w1_raw1")
-        w3_raw0 = load_weight(w3, 0, slice(0, H), "w3_raw0")
-        w3_raw1 = load_weight(w3, 1, slice(0, H), "w3_raw1")
-
+        w1_raw1 = load_weight(w1, 1, "w1_raw1")
+        w3_raw0 = load_weight(w3, 0, "w3_raw0")
+        w3_raw1 = load_weight(w3, 1, "w3_raw1")
         stream = [keep.tile([P, T], F32, name="stream%d" % b) for b in range(BLOCKS)]
         w2_codes = mx_tile([P, N], U32, "w2_codes")
         nc.sync.dma_start(stream[0][:], res[0:P, :])
+        nc.sync.dma_start(gate_rows[0:CHUNKS, :], gate[0, :].rearrange("(c p) -> c p", p=CHUNK))
         load_words(w2_codes, w2_words[0])
         for q in range(QUADRANTS):
             nc.sync.dma_start(
@@ -96,96 +91,99 @@ def tile_picked_modres_glusilu_p_kernel(
         def bank(kind, c, shape, name):
             return psum.tile(shape, F32, name="%s%d" % (name, c), tag="%s%d" % (kind, c))
 
-        gate_cols = keep.tile([P, CHUNKS], F32, name="gate_cols")
-        gate_turned = bank("b", CHUNKS - 1, [P, P], "gate_turned")
-        nc.tensor.transpose(gate_turned[:], gate_rows[:], identity[:])
-        nc.scalar.copy(gate_cols[:], gate_turned[:, 0:CHUNKS])
-
         x_codes = [mx_tile([P, S], U32, "x_codes%d" % g) for g in range(PASSES)]
         x_scale = mx_tile([P, S], U8, "x_scale")
         nc.vector.tensor_copy(x_codes[0][:], x_table[0][:].indirect(offsets[:]))
         nc.vector.tensor_copy(x_scale[:], x_scale_table[:].indirect(offsets[:]))
 
-        def cast(raw, scalar_cols, name):
-            width = raw.shape[2]
-            grouped = mx_tile([P, width, PACK], BF16, name, "grouped")
-            src = raw[:].rearrange("p j (c e) -> p c j e", e=RUN)
-            dst = grouped[:].rearrange("p (c e) j -> p c j e", e=RUN)
-            cut = scalar_cols // RUN
-            if scalar_cols > 0:
-                nc.scalar.copy(dst[:, :cut], src[:, :cut])
-            middle = width // 2 // RUN
-            nc.vector.tensor_copy(dst[:, cut:middle], src[:, cut:middle])
-            nc.vector.tensor_copy(dst[:, middle:], src[:, middle:])
-            return grouped
-
-        def quantise(grouped, codes, scale):
-            nc.vector.quantize_mx(
-                out=codes.bitcast(FP8X4), scales=scale, in_=grouped.rearrange("p c j -> p (c j)")
-            )
-
-        def quantise_halves(grouped, codes, scale):
+        def prepare(raw, scalar_groups, name):
+            grouped = mx_tile([P, PACK, P, PACK], BF16, name + "_grouped", "grouped")
+            src = raw[:].rearrange("p j (m t) -> p m j t", t=PACK)
+            dst = grouped[:].rearrange("p t m j -> p m j t")
+            for u in range(2):
+                pair = slice(2 * u, 2 * u + 2)
+                if scalar_groups > 0:
+                    nc.scalar.copy(dst[:, :scalar_groups, :, pair], src[:, :scalar_groups, :, pair])
+                nc.vector.tensor_copy(dst[:, scalar_groups:, :, pair], src[:, scalar_groups:, :, pair])
+            codes = mx_tile([P, H], U32, name + "_codes")
+            scale = mx_tile([P, H], U8, name + "_scale")
             for u in range(2):
                 cols = slice(u * H // 2, (u + 1) * H // 2)
-                quantise(grouped[:, cols], codes[:, cols], scale[:, cols])
+                nc.vector.quantize_mx(
+                    out=codes[:, cols].bitcast(FP8X4),
+                    scales=scale[:, cols],
+                    in_=grouped[:, 2 * u : 2 * u + 2].rearrange("p t m j -> p (t m j)"),
+                )
+            return codes, scale
 
-        w1_codes = [mx_tile([P, H], U32, "w1_codes%d" % g) for g in range(PASSES)]
-        w1_scale = [mx_tile([P, H], U8, "w1_scale%d" % g) for g in range(PASSES)]
-        w3_codes = [mx_tile([P, H], U32, "w3_codes%d" % g) for g in range(PASSES)]
-        w3_scale = [mx_tile([P, H], U8, "w3_scale%d" % g) for g in range(PASSES)]
-
-        def first_product(kind, codes, scale, name):
-            accs = [bank(kind, c, [CHUNK, H], name) for c in range(CHUNKS)]
+        def first_product(kind, passes, name):
+            accs = [bank(kind, c, [P, PACK, CHUNK], name) for c in range(CHUNKS)]
             for g in range(PASSES):
-                for c in range(CHUNKS):
+                codes, scale = passes[g]
+                for c in (3, 0, 1, 2):
                     entries = slice(c * CHUNK, (c + 1) * CHUNK)
-                    nc.tensor.matmul_mx(
-                        out=accs[c][:],
-                        lhsT=x_codes[g][:, entries].bitcast(FP8X4),
-                        lhsT_scale=x_scale[SCALE_ROWS * g : P, entries],
-                        rhs=codes[g][:].bitcast(FP8X4),
-                        rhs_scale=scale[g][:],
-                        start=(g == 0),
-                        stop=(g == PASSES - 1),
-                    )
+                    for t in range(PACK):
+                        cols = slice(t * P, (t + 1) * P)
+                        nc.tensor.matmul_mx(
+                            out=accs[c][:, t, :],
+                            lhsT=codes[:, cols].bitcast(FP8X4),
+                            lhsT_scale=scale[:, cols],
+                            rhs=x_codes[g][:, entries].bitcast(FP8X4),
+                            rhs_scale=x_scale[SCALE_ROWS * g : P, entries],
+                            start=(g == 0 and t == 0),
+                            stop=(g == PASSES - 1 and t == PACK - 1),
+                        )
             return accs
 
-        quantise_halves(cast(w1_raw0, SCALAR_SHARE, "w1_grouped0"), w1_codes[0], w1_scale[0])
+        w1_pass0 = prepare(w1_raw0, SCALAR_SHARE, "w1_0")
         nc.vector.tensor_copy(x_codes[1][:], x_table[1][:].indirect(offsets[:]))
-        quantise_halves(cast(w1_raw1, SCALAR_SHARE, "w1_grouped1"), w1_codes[1], w1_scale[1])
-        w1_acc = first_product("a", w1_codes, w1_scale, "w1_acc")
-        quantise_halves(cast(w3_raw0, 0, "w3_grouped0"), w3_codes[0], w3_scale[0])
-        quantise_halves(cast(w3_raw1, SCALAR_SHARE, "w3_grouped1"), w3_codes[1], w3_scale[1])
-        w3_acc = first_product("b", w3_codes, w3_scale, "w3_acc")
+        w1_pass1 = prepare(w1_raw1, SCALAR_SHARE, "w1_1")
+        w1_acc = first_product("a", (w1_pass0, w1_pass1), "w1_acc")
+        w3_pass0 = prepare(w3_raw0, 0, "w3_0")
+        w3_pass1 = prepare(w3_raw1, SCALAR_SHARE, "w3_1")
+        w3_acc = first_product("b", (w3_pass0, w3_pass1), "w3_acc")
 
-        def by_word_half(acc):
-            return acc[:].rearrange("n (p e r) -> n e p r", e=2, r=2)
+        def by_pairs(acc):
+            return acc[:].rearrange("p t (n e) -> p n t e", e=2)
 
-        silu = [mx_tile([CHUNK, 2, P, 2], F32, "silu%d" % c) for c in range(CHUNKS - 1)]
-        silu.append(mx_tile([CHUNK, 2, P, 2], F32, "silu_last", "w3_raw1"))
-        for c in range(CHUNKS):
-            nc.scalar.activation(silu[c][:], by_word_half(w1_acc[c]), SILU)
+        silu = {}
+        for c in (3, 0, 1, 2):
+            shape = [P, CHUNK, PACK] if c == 3 else [P, CHUNK // 2, PACK, 2]
+            silu[c] = mx_tile(shape, F32, "silu%d" % c, "w3_raw1" if c == 2 else None)
+            dst = silu[c][:].rearrange("p (n e) t -> p n t e", e=2) if c == 3 else silu[c][:]
+            nc.scalar.activation(dst, by_pairs(w1_acc[c]), SILU)
+        last_product = mx_tile([P, CHUNK, PACK], F32, "last_product")
+        for u in range(2):
+            rows = slice(u * CHUNK // 4, (u + 1) * CHUNK // 4)
+            nc.scalar.copy(last_product[:].rearrange("p (n e) t -> p n t e", e=2)[:, rows], by_pairs(w3_acc[3])[:, rows])
 
         h_codes = [mx_tile([P, CHUNK], U32, "h_codes%d" % c) for c in range(CHUNKS)]
         h_scale = [mx_tile([P, CHUNK], U8, "h_scale%d" % c) for c in range(CHUNKS)]
-        h_grouped = [mx_tile([P, CHUNK, PACK], BF16, "h_grouped%d" % c) for c in range(CHUNKS)]
+        h = [mx_tile([P, CHUNK, PACK], BF16, "h%d" % c) for c in range(CHUNKS)]
         gated_rows = [keep.tile([CHUNK, N], F32, name="gated_rows%d" % c) for c in range(CHUNKS)]
-        gated = [keep.tile([P, S], F32, name="gated%d" % b) for b in range(BLOCKS)]
+        gated = keep.tile([P, BLOCKS, S], F32, name="gated")
+        gate_cols = keep.tile([P, CHUNKS], F32, name="gate_cols")
 
         def make_h(c):
-            h = keep.tile([CHUNK, 2, P, 2], BF16, name="h%d" % c)
-            nc.vector.tensor_tensor(h[:], by_word_half(w3_acc[c]), silu[c][:], MULT)
-            pairs = h[:].rearrange("n e p r -> n (e p r)").bitcast(F32)
-            turned = bank("a", c, [P, 2, CHUNK], "h_turned")
-            for e in range(2):
-                nc.tensor.transpose(turned[:, e, :], pairs[:, e * P : (e + 1) * P], identity[:])
-            nc.scalar.copy(
-                h_grouped[c][:].rearrange("p n t -> p (n t)").bitcast(F32).rearrange("p (n e) -> p n e", e=2),
-                turned[:].rearrange("p e n -> p n e"),
+            if c == 3:
+                for u in range(2):
+                    part = slice(u * CHUNK // 2, (u + 1) * CHUNK // 2)
+                    nc.gpsimd.tensor_tensor(h[c][:, part], last_product[:, part], silu[c][:, part], MULT)
+                return
+            nc.vector.tensor_tensor(
+                h[c][:].rearrange("p (n e) t -> p n t e", e=2), by_pairs(w3_acc[c]), silu[c][:], MULT
             )
 
-        def second_product(c):
-            y = bank("b", c, [CHUNK, N], "y") if c < 2 else bank("a", c - 2, [CHUNK, N], "y_late")
+        def turn_gate():
+            gate_turned = bank("b", 0, [P, P], "gate_turned")
+            nc.tensor.transpose(gate_turned[:], gate_rows[:], identity[:])
+            nc.scalar.copy(gate_cols[:], gate_turned[:, 0:CHUNKS])
+
+        def finish(c):
+            nc.vector.quantize_mx(
+                out=h_codes[c][:].bitcast(FP8X4), scales=h_scale[c][:], in_=h[c][:].rearrange("p n t -> p (n t)")
+            )
+            y = bank("a", c, [CHUNK, N], "y") if c < 2 else bank("b", c - 2, [CHUNK, N], "y_late")
             nc.tensor.matmul_mx(
                 out=y[:],
                 lhsT=h_codes[c][:].bitcast(FP8X4),
@@ -196,44 +194,37 @@ def tile_picked_modres_glusilu_p_kernel(
                 stop=True,
             )
             nc.scalar.activation(gated_rows[c][:], y[:], COPY, scale=gate_cols[:, c : c + 1])
-
-        def turn_back(c):
-            turned = bank("a", c, [P, BLOCKS, CHUNK], "y_turned")
+            turned = bank("b", c, [P, BLOCKS, CHUNK], "y_turned")
             for b in range(BLOCKS):
                 nc.tensor.transpose(turned[:, b, :], gated_rows[c][:, b * P : (b + 1) * P], identity[:])
-            for b in range(BLOCKS):
-                nc.scalar.copy(gated[b][:, c * CHUNK : (c + 1) * CHUNK], turned[:, b, :])
+            nc.scalar.copy(gated[:, :, c * CHUNK : (c + 1) * CHUNK], turned[:])
 
-        half = S // 2
         picked_res = {}
 
-        def gather_res(b, u, buffer):
-            picked_res[b, u] = mx_tile([P, half], F32, "picked_res%d%d" % (b, u), buffer)
-            nc.vector.tensor_copy(
-                picked_res[b, u][:], stream[b][:].indirect(offsets[:, u * half // 16 : (u + 1) * half // 16])
-            )
+        def gather_res(b, c0, c1, buffer):
+            picked = mx_tile([P, (c1 - c0) * CHUNK], F32, "picked_res%d%d" % (b, c0), buffer)
+            nc.vector.tensor_copy(picked[:], stream[b][:].indirect(offsets[:, c0 * LIST_COLS : c1 * LIST_COLS]))
+            for c in range(c0, c1):
+                picked_res[b, c] = (picked, c0)
 
-        gather_res(0, 0, "grouped")
+        gather_res(0, 0, 2, "grouped")
         for step in range(CHUNKS + LAG):
             if step >= LAG:
-                c = step - LAG
-                quantise(h_grouped[c][:], h_codes[c][:], h_scale[c][:])
-                second_product(c)
-                turn_back(c)
+                finish(step - LAG)
             if step < CHUNKS:
                 make_h(step)
-        gather_res(1, 0, "h_grouped0")
-        gather_res(0, 1, "h_grouped1")
-        gather_res(1, 1, "h_grouped2")
+            if step == 0:
+                turn_gate()
+        gather_res(1, 0, 4, "h1")
+        gather_res(0, 2, 4, "h2")
 
         for c0, c1 in SCATTER_RANGES:
-            entries = slice(c0 * CHUNK, c1 * CHUNK)
-            u = entries.start // half
             for b in range(BLOCKS):
+                picked, first = picked_res[b, c0]
                 nc.vector.tensor_tensor(
                     stream[b][:].indirect(offsets[:, c0 * LIST_COLS : c1 * LIST_COLS]),
-                    gated[b][:, entries],
-                    picked_res[b, u][:, entries.start - u * half : entries.stop - u * half],
+                    gated[:, b, c0 * CHUNK : c1 * CHUNK],
+                    picked[:, (c0 - first) * CHUNK : (c1 - first) * CHUNK],
                     ADD,
                 )
         for b in range(BLOCKS):

@@ -39,6 +39,7 @@ def tile_picked_modres_glusilu_p_kernel(
     nc = tc.nc
     with ExitStack() as ctx:
         keep = ctx.enter_context(tc.tile_pool(name="keep", bufs=1))
+        staging = ctx.enter_context(tc.tile_pool(name="staging", bufs=1))
         psum = ctx.enter_context(tc.psum_pool(name="psum", bufs=1))
 
         def mx_tile(shape, dtype, name, tag=None):
@@ -97,7 +98,7 @@ def tile_picked_modres_glusilu_p_kernel(
         nc.vector.tensor_copy(x_scale[:], x_scale_table[:].indirect(offsets[:]))
 
         def prepare(raw, scalar_groups, name):
-            grouped = mx_tile([P, PACK, P, PACK], BF16, name + "_grouped", "grouped")
+            grouped = staging.tile([P, PACK, P, PACK], BF16, name=name + "_grouped", offset=0, align_bytes=MX_ALIGN)
             src = raw[:].rearrange("p j (m t) -> p m j t", t=PACK)
             dst = grouped[:].rearrange("p t m j -> p m j t")
             for u in range(2):
@@ -193,6 +194,14 @@ def tile_picked_modres_glusilu_p_kernel(
                 start=True,
                 stop=True,
             )
+            if c == 0:
+                for b in range(BLOCKS):
+                    cols = slice(b * P, (b + 1) * P)
+                    nc.scalar.activation(gated_rows[c][:, cols], y[:, cols], COPY, scale=gate_cols[:, c : c + 1])
+                    turned = bank("b" if b == 1 else "a", 0 if b == 1 else 3, [P, CHUNK], "y_first%d" % b)
+                    nc.tensor.transpose(turned[:], gated_rows[c][:, cols], identity[:])
+                    nc.scalar.copy(gated[:, b, 0:CHUNK], turned[:])
+                return
             nc.scalar.activation(gated_rows[c][:], y[:], COPY, scale=gate_cols[:, c : c + 1])
             turned = bank("b", c, [P, BLOCKS, CHUNK], "y_turned")
             for b in range(BLOCKS):
@@ -202,12 +211,17 @@ def tile_picked_modres_glusilu_p_kernel(
         picked_res = {}
 
         def gather_res(b, c0, c1, buffer):
-            picked = mx_tile([P, (c1 - c0) * CHUNK], F32, "picked_res%d%d" % (b, c0), buffer)
+            shape, name = [P, (c1 - c0) * CHUNK], "picked_res%d%d" % (b, c0)
+            if buffer is None:
+                picked = staging.tile(shape, F32, name=name, offset=4 * c0 * CHUNK, align_bytes=MX_ALIGN)
+            else:
+                picked = mx_tile(shape, F32, name, buffer)
             nc.vector.tensor_copy(picked[:], stream[b][:].indirect(offsets[:, c0 * LIST_COLS : c1 * LIST_COLS]))
             for c in range(c0, c1):
                 picked_res[b, c] = (picked, c0)
 
-        gather_res(0, 0, 2, "grouped")
+        gather_res(0, 2, 4, None)
+        gather_res(0, 0, 1, None)
         for step in range(CHUNKS + LAG):
             if step >= LAG:
                 finish(step - LAG)
@@ -216,7 +230,7 @@ def tile_picked_modres_glusilu_p_kernel(
             if step == 0:
                 turn_gate()
         gather_res(1, 0, 4, "h1")
-        gather_res(0, 2, 4, "h2")
+        gather_res(0, 1, 2, "h2")
 
         for c0, c1 in SCATTER_RANGES:
             for b in range(BLOCKS):

@@ -98,14 +98,15 @@ def tile_picked_modres_glusilu_p_kernel(
         nc.vector.tensor_copy(x_scale[:], x_scale_table[:].indirect(offsets[:]))
 
         def prepare(raw, scalar_groups, name):
-            grouped = staging.tile([P, PACK, P, PACK], BF16, name=name + "_grouped", offset=0, align_bytes=MX_ALIGN)
             src = raw[:].rearrange("p j (m t) -> p m j t", t=PACK)
-            dst = grouped[:].rearrange("p t m j -> p m j t")
+            grouped = []
             for u in range(2):
+                grouped.append(mx_tile([P, 2, P, PACK], BF16, "%s_grouped%d" % (name, u), "staging%d" % u))
+                dst = grouped[u][:].rearrange("p t m j -> p m j t")
                 pair = slice(2 * u, 2 * u + 2)
                 if scalar_groups > 0:
-                    nc.scalar.copy(dst[:, :scalar_groups, :, pair], src[:, :scalar_groups, :, pair])
-                nc.vector.tensor_copy(dst[:, scalar_groups:, :, pair], src[:, scalar_groups:, :, pair])
+                    nc.scalar.copy(dst[:, :scalar_groups], src[:, :scalar_groups, :, pair])
+                nc.vector.tensor_copy(dst[:, scalar_groups:], src[:, scalar_groups:, :, pair])
             codes = mx_tile([P, H], U32, name + "_codes")
             scale = mx_tile([P, H], U8, name + "_scale")
             for u in range(2):
@@ -113,7 +114,7 @@ def tile_picked_modres_glusilu_p_kernel(
                 nc.vector.quantize_mx(
                     out=codes[:, cols].bitcast(FP8X4),
                     scales=scale[:, cols],
-                    in_=grouped[:, 2 * u : 2 * u + 2].rearrange("p t m j -> p (t m j)"),
+                    in_=grouped[u][:].rearrange("p t m j -> p (t m j)"),
                 )
             return codes, scale
 
@@ -147,33 +148,34 @@ def tile_picked_modres_glusilu_p_kernel(
         def by_pairs(acc):
             return acc[:].rearrange("p t (n e) -> p n t e", e=2)
 
+        def in_token_order(tile):
+            return tile.rearrange("p (n e) t -> p n t e", e=2)
+
         silu = {}
         for c in (3, 0, 1, 2):
-            shape = [P, CHUNK, PACK] if c == 3 else [P, CHUNK // 2, PACK, 2]
+            shape = [P, CHUNK, PACK] if c >= 2 else [P, CHUNK // 2, PACK, 2]
             silu[c] = mx_tile(shape, F32, "silu%d" % c, "w3_raw1" if c == 2 else None)
-            dst = silu[c][:].rearrange("p (n e) t -> p n t e", e=2) if c == 3 else silu[c][:]
-            nc.scalar.activation(dst, by_pairs(w1_acc[c]), SILU)
-        last_product = mx_tile([P, CHUNK, PACK], F32, "last_product")
-        for u in range(2):
-            rows = slice(u * CHUNK // 4, (u + 1) * CHUNK // 4)
-            nc.scalar.copy(last_product[:].rearrange("p (n e) t -> p n t e", e=2)[:, rows], by_pairs(w3_acc[3])[:, rows])
+            nc.scalar.activation(in_token_order(silu[c][:]) if c >= 2 else silu[c][:], by_pairs(w1_acc[c]), SILU)
 
         h_codes = [mx_tile([P, CHUNK], U32, "h_codes%d" % c) for c in range(CHUNKS)]
         h_scale = [mx_tile([P, CHUNK], U8, "h_scale%d" % c) for c in range(CHUNKS)]
-        h = [mx_tile([P, CHUNK, PACK], BF16, "h%d" % c) for c in range(CHUNKS)]
+        h = {}
         gated_rows = [keep.tile([CHUNK, N], F32, name="gated_rows%d" % c) for c in range(CHUNKS)]
         gated = keep.tile([P, BLOCKS, S], F32, name="gated")
         gate_cols = keep.tile([P, CHUNKS], F32, name="gate_cols")
 
         def make_h(c):
-            if c == 3:
-                for u in range(2):
-                    part = slice(u * CHUNK // 2, (u + 1) * CHUNK // 2)
-                    nc.gpsimd.tensor_tensor(h[c][:, part], last_product[:, part], silu[c][:, part], MULT)
-                return
-            nc.vector.tensor_tensor(
-                h[c][:].rearrange("p (n e) t -> p n t e", e=2), by_pairs(w3_acc[c]), silu[c][:], MULT
-            )
+            h[c] = mx_tile([P, CHUNK, PACK], BF16, "h%d" % c)
+            nc.vector.tensor_tensor(in_token_order(h[c][:]), by_pairs(w3_acc[c]), silu[c][:], MULT)
+
+        def part_on_gpsimd(c, n0, n1):
+            product = mx_tile([P, n1 - n0, PACK], F32, "product%d_%d" % (c, n0))
+            nc.scalar.copy(in_token_order(product[:]), by_pairs(w3_acc[c])[:, n0 // 2 : n1 // 2])
+            nc.gpsimd.tensor_tensor(h[c][:, n0:n1], product[:], silu[c][:, n0:n1], MULT)
+
+        def part_on_vector(c, n0, n1):
+            product = w3_acc[c][:, :, n0:n1].rearrange("p t n -> p n t")
+            nc.vector.tensor_tensor(h[c][:, n0:n1], product, silu[c][:, n0:n1], MULT)
 
         def turn_gate():
             gate_turned = bank("b", 0, [P, P], "gate_turned")
@@ -184,7 +186,7 @@ def tile_picked_modres_glusilu_p_kernel(
             nc.vector.quantize_mx(
                 out=h_codes[c][:].bitcast(FP8X4), scales=h_scale[c][:], in_=h[c][:].rearrange("p n t -> p (n t)")
             )
-            y = bank("a", c, [CHUNK, N], "y") if c < 2 else bank("b", c - 2, [CHUNK, N], "y_late")
+            y = bank("a", c, [CHUNK, N], "y") if c < 2 else bank("b", 3 - c, [CHUNK, N], "y_late")
             nc.tensor.matmul_mx(
                 out=y[:],
                 lhsT=h_codes[c][:].bitcast(FP8X4),
@@ -220,17 +222,22 @@ def tile_picked_modres_glusilu_p_kernel(
             for c in range(c0, c1):
                 picked_res[b, c] = (picked, c0)
 
-        gather_res(0, 2, 4, None)
-        gather_res(0, 0, 1, None)
-        for step in range(CHUNKS + LAG):
-            if step >= LAG:
-                finish(step - LAG)
-            if step < CHUNKS:
-                make_h(step)
-            if step == 0:
-                turn_gate()
-        gather_res(1, 0, 4, "h1")
-        gather_res(0, 1, 2, "h2")
+        gather_res(0, 0, 4, "staging0")
+        h[3] = mx_tile([P, CHUNK, PACK], BF16, "h3")
+        part_on_gpsimd(3, 0, 48)
+        part_on_gpsimd(3, 48, 112)
+        make_h(0)
+        turn_gate()
+        make_h(1)
+        part_on_vector(3, 112, 128)
+        finish(0)
+        finish(1)
+        h[2] = mx_tile([P, CHUNK, PACK], BF16, "h2", "h0")
+        part_on_gpsimd(2, 0, 32)
+        part_on_vector(2, 32, 128)
+        finish(3)
+        finish(2)
+        gather_res(1, 0, 4, "h3")
 
         for c0, c1 in SCATTER_RANGES:
             for b in range(BLOCKS):

@@ -27,9 +27,14 @@ CHUNK = 128
 CHUNKS = S // CHUNK
 LIST_COLS = CHUNK // 16
 BLOCKS = N // P
-SCALAR_SHARE = 44
 MX_ALIGN = 64
-LAG = 4
+
+SCALAR_SHARE = 44
+
+GPSIMD_EARLY = 104
+GPSIMD_LATE = 28
+PRODUCT_ORDER = (3, 0, 1, 2)
+
 SCATTER_RANGES = [(0, 1), (1, 2), (2, 4)]
 
 
@@ -39,13 +44,16 @@ def tile_picked_modres_glusilu_p_kernel(
     nc = tc.nc
     with ExitStack() as ctx:
         keep = ctx.enter_context(tc.tile_pool(name="keep", bufs=1))
-        staging = ctx.enter_context(tc.tile_pool(name="staging", bufs=1))
         psum = ctx.enter_context(tc.psum_pool(name="psum", bufs=1))
 
         def mx_tile(shape, dtype, name, tag=None):
             return keep.tile(shape, dtype, name=name, tag=tag or name, align_bytes=MX_ALIGN)
 
+        def bank(tag, shape, name):
+            return psum.tile(shape, F32, name=name, tag=tag)
+
         offsets = keep.tile([P, S // 16], U16, name="offsets")
+
         x_scale_table = mx_tile([P, T], U8, "x_scale_table")
         nc.gpsimd.memset(x_scale_table[:].bitcast(I32), 0)
         gate_rows = keep.tile([P, P], F32, name="gate_rows")
@@ -77,6 +85,7 @@ def tile_picked_modres_glusilu_p_kernel(
         w1_raw1 = load_weight(w1, 1, "w1_raw1")
         w3_raw0 = load_weight(w3, 0, "w3_raw0")
         w3_raw1 = load_weight(w3, 1, "w3_raw1")
+
         stream = [keep.tile([P, T], F32, name="stream%d" % b) for b in range(BLOCKS)]
         w2_codes = mx_tile([P, N], U32, "w2_codes")
         nc.sync.dma_start(stream[0][:], res[0:P, :])
@@ -89,24 +98,21 @@ def tile_picked_modres_glusilu_p_kernel(
             )
         nc.sync.dma_start(stream[1][:], res[P : 2 * P, :])
 
-        def bank(kind, c, shape, name):
-            return psum.tile(shape, F32, name="%s%d" % (name, c), tag="%s%d" % (kind, c))
-
         x_codes = [mx_tile([P, S], U32, "x_codes%d" % g) for g in range(PASSES)]
         x_scale = mx_tile([P, S], U8, "x_scale")
         nc.vector.tensor_copy(x_codes[0][:], x_table[0][:].indirect(offsets[:]))
         nc.vector.tensor_copy(x_scale[:], x_scale_table[:].indirect(offsets[:]))
 
-        def prepare(raw, scalar_groups, name):
+        def quantise_weight(raw, scalar_share, name):
             src = raw[:].rearrange("p j (m t) -> p m j t", t=PACK)
-            grouped = []
+            staged = []
             for u in range(2):
-                grouped.append(mx_tile([P, 2, P, PACK], BF16, "%s_grouped%d" % (name, u), "staging%d" % u))
-                dst = grouped[u][:].rearrange("p t m j -> p m j t")
+                staged.append(mx_tile([P, 2, P, PACK], BF16, "%s_staged%d" % (name, u), "staging%d" % u))
+                dst = staged[u][:].rearrange("p t m j -> p m j t")
                 pair = slice(2 * u, 2 * u + 2)
-                if scalar_groups > 0:
-                    nc.scalar.copy(dst[:, :scalar_groups], src[:, :scalar_groups, :, pair])
-                nc.vector.tensor_copy(dst[:, scalar_groups:], src[:, scalar_groups:, :, pair])
+                if scalar_share > 0:
+                    nc.scalar.copy(dst[:, :scalar_share], src[:, :scalar_share, :, pair])
+                nc.vector.tensor_copy(dst[:, scalar_share:], src[:, scalar_share:, :, pair])
             codes = mx_tile([P, H], U32, name + "_codes")
             scale = mx_tile([P, H], U8, name + "_scale")
             for u in range(2):
@@ -114,15 +120,15 @@ def tile_picked_modres_glusilu_p_kernel(
                 nc.vector.quantize_mx(
                     out=codes[:, cols].bitcast(FP8X4),
                     scales=scale[:, cols],
-                    in_=grouped[u][:].rearrange("p t m j -> p (t m j)"),
+                    in_=staged[u][:].rearrange("p t m j -> p (t m j)"),
                 )
             return codes, scale
 
-        def first_product(kind, passes, name):
-            accs = [bank(kind, c, [P, PACK, CHUNK], name) for c in range(CHUNKS)]
+        def first_product(passes, name):
+            accs = [bank("%s_%d" % (name, c), [P, PACK, CHUNK], "%s_acc%d" % (name, c)) for c in range(CHUNKS)]
             for g in range(PASSES):
                 codes, scale = passes[g]
-                for c in (3, 0, 1, 2):
+                for c in PRODUCT_ORDER:
                     entries = slice(c * CHUNK, (c + 1) * CHUNK)
                     for t in range(PACK):
                         cols = slice(t * P, (t + 1) * P)
@@ -137,25 +143,26 @@ def tile_picked_modres_glusilu_p_kernel(
                         )
             return accs
 
-        w1_pass0 = prepare(w1_raw0, SCALAR_SHARE, "w1_0")
+        w1_pass0 = quantise_weight(w1_raw0, SCALAR_SHARE, "w1_0")
         nc.vector.tensor_copy(x_codes[1][:], x_table[1][:].indirect(offsets[:]))
-        w1_pass1 = prepare(w1_raw1, SCALAR_SHARE, "w1_1")
-        w1_acc = first_product("a", (w1_pass0, w1_pass1), "w1_acc")
-        w3_pass0 = prepare(w3_raw0, 0, "w3_0")
-        w3_pass1 = prepare(w3_raw1, SCALAR_SHARE, "w3_1")
-        w3_acc = first_product("b", (w3_pass0, w3_pass1), "w3_acc")
+        w1_pass1 = quantise_weight(w1_raw1, SCALAR_SHARE, "w1_1")
+        w1_acc = first_product((w1_pass0, w1_pass1), "w1")
+        w3_pass0 = quantise_weight(w3_raw0, 0, "w3_0")
+        w3_pass1 = quantise_weight(w3_raw1, SCALAR_SHARE, "w3_1")
+        w3_acc = first_product((w3_pass0, w3_pass1), "w3")
 
         def by_pairs(acc):
             return acc[:].rearrange("p t (n e) -> p n t e", e=2)
 
-        def in_token_order(tile):
+        def words_by_pairs(tile):
             return tile.rearrange("p (n e) t -> p n t e", e=2)
 
         silu = {}
-        for c in (3, 0, 1, 2):
-            shape = [P, CHUNK, PACK] if c >= 2 else [P, CHUNK // 2, PACK, 2]
-            silu[c] = mx_tile(shape, F32, "silu%d" % c, "w3_raw1" if c == 2 else None)
-            nc.scalar.activation(in_token_order(silu[c][:]) if c >= 2 else silu[c][:], by_pairs(w1_acc[c]), SILU)
+        for c in PRODUCT_ORDER:
+            shared = c >= 2
+            shape = [P, CHUNK, PACK] if shared else [P, CHUNK // 2, PACK, 2]
+            silu[c] = mx_tile(shape, F32, "silu%d" % c, "w3_raw1" if c == PRODUCT_ORDER[-1] else None)
+            nc.scalar.activation(words_by_pairs(silu[c][:]) if shared else silu[c][:], by_pairs(w1_acc[c]), SILU)
 
         h_codes = [mx_tile([P, CHUNK], U32, "h_codes%d" % c) for c in range(CHUNKS)]
         h_scale = [mx_tile([P, CHUNK], U8, "h_scale%d" % c) for c in range(CHUNKS)]
@@ -164,29 +171,24 @@ def tile_picked_modres_glusilu_p_kernel(
         gated = keep.tile([P, BLOCKS, S], F32, name="gated")
         gate_cols = keep.tile([P, CHUNKS], F32, name="gate_cols")
 
-        def make_h(c):
+        def h_on_vector(c):
             h[c] = mx_tile([P, CHUNK, PACK], BF16, "h%d" % c)
-            nc.vector.tensor_tensor(in_token_order(h[c][:]), by_pairs(w3_acc[c]), silu[c][:], MULT)
+            nc.vector.tensor_tensor(words_by_pairs(h[c][:]), by_pairs(w3_acc[c]), silu[c][:], MULT)
 
-        def part_on_gpsimd(c, n0, n1):
-            product = mx_tile([P, n1 - n0, PACK], F32, "product%d_%d" % (c, n0))
-            nc.scalar.copy(in_token_order(product[:]), by_pairs(w3_acc[c])[:, n0 // 2 : n1 // 2])
-            nc.gpsimd.tensor_tensor(h[c][:, n0:n1], product[:], silu[c][:, n0:n1], MULT)
+        def first_h_on_gpsimd(c, count):
+            product = mx_tile([P, count, PACK], F32, "product%d" % c)
+            nc.scalar.copy(words_by_pairs(product[:]), by_pairs(w3_acc[c])[:, : count // 2])
+            nc.gpsimd.tensor_tensor(h[c][:, :count], product[:], silu[c][:, :count], MULT)
 
-        def part_on_vector(c, n0, n1):
-            product = w3_acc[c][:, :, n0:n1].rearrange("p t n -> p n t")
-            nc.vector.tensor_tensor(h[c][:, n0:n1], product, silu[c][:, n0:n1], MULT)
+        def other_h_on_vector(c, count):
+            product = w3_acc[c][:, :, count:].rearrange("p t n -> p n t")
+            nc.vector.tensor_tensor(h[c][:, count:], product, silu[c][:, count:], MULT)
 
-        def turn_gate():
-            gate_turned = bank("b", 0, [P, P], "gate_turned")
-            nc.tensor.transpose(gate_turned[:], gate_rows[:], identity[:])
-            nc.scalar.copy(gate_cols[:], gate_turned[:, 0:CHUNKS])
-
-        def finish(c):
+        def second_product(c, tag):
             nc.vector.quantize_mx(
                 out=h_codes[c][:].bitcast(FP8X4), scales=h_scale[c][:], in_=h[c][:].rearrange("p n t -> p (n t)")
             )
-            y = bank("a", c, [CHUNK, N], "y") if c < 2 else bank("b", 3 - c, [CHUNK, N], "y_late")
+            y = bank(tag, [CHUNK, N], "y%d" % c)
             nc.tensor.matmul_mx(
                 out=y[:],
                 lhsT=h_codes[c][:].bitcast(FP8X4),
@@ -196,56 +198,48 @@ def tile_picked_modres_glusilu_p_kernel(
                 start=True,
                 stop=True,
             )
-            if c == 0:
-                for b in range(BLOCKS):
-                    cols = slice(b * P, (b + 1) * P)
-                    nc.scalar.activation(gated_rows[c][:, cols], y[:, cols], COPY, scale=gate_cols[:, c : c + 1])
-                    turned = bank("b" if b == 1 else "a", 0 if b == 1 else 3, [P, CHUNK], "y_first%d" % b)
-                    nc.tensor.transpose(turned[:], gated_rows[c][:, cols], identity[:])
-                    nc.scalar.copy(gated[:, b, 0:CHUNK], turned[:])
-                return
-            nc.scalar.activation(gated_rows[c][:], y[:], COPY, scale=gate_cols[:, c : c + 1])
-            turned = bank("b", c, [P, BLOCKS, CHUNK], "y_turned")
-            for b in range(BLOCKS):
-                nc.tensor.transpose(turned[:, b, :], gated_rows[c][:, b * P : (b + 1) * P], identity[:])
-            nc.scalar.copy(gated[:, :, c * CHUNK : (c + 1) * CHUNK], turned[:])
+            return y
 
-        picked_res = {}
+        def gate_and_turn(c, y, b0, b1, tag):
+            cols = slice(b0 * P, b1 * P)
+            nc.scalar.activation(gated_rows[c][:, cols], y[:, cols], COPY, scale=gate_cols[:, c : c + 1])
+            turned = bank(tag, [P, b1 - b0, CHUNK], "y_turned%d_%d" % (c, b0))
+            for b in range(b0, b1):
+                nc.tensor.transpose(turned[:, b - b0, :], gated_rows[c][:, b * P : (b + 1) * P], identity[:])
+            nc.scalar.copy(gated[:, b0:b1, c * CHUNK : (c + 1) * CHUNK], turned[:])
 
-        def gather_res(b, c0, c1, buffer):
-            shape, name = [P, (c1 - c0) * CHUNK], "picked_res%d%d" % (b, c0)
-            if buffer is None:
-                picked = staging.tile(shape, F32, name=name, offset=4 * c0 * CHUNK, align_bytes=MX_ALIGN)
-            else:
-                picked = mx_tile(shape, F32, name, buffer)
-            nc.vector.tensor_copy(picked[:], stream[b][:].indirect(offsets[:, c0 * LIST_COLS : c1 * LIST_COLS]))
-            for c in range(c0, c1):
-                picked_res[b, c] = (picked, c0)
+        def gather_res(b, tag):
+            picked = mx_tile([P, S], F32, "picked_res%d" % b, tag)
+            nc.vector.tensor_copy(picked[:], stream[b][:].indirect(offsets[:]))
+            return picked
 
-        gather_res(0, 0, 4, "staging0")
+        picked_res = [gather_res(0, "staging0")]
         h[3] = mx_tile([P, CHUNK, PACK], BF16, "h3")
-        part_on_gpsimd(3, 0, 48)
-        part_on_gpsimd(3, 48, 112)
-        make_h(0)
-        turn_gate()
-        make_h(1)
-        part_on_vector(3, 112, 128)
-        finish(0)
-        finish(1)
+        first_h_on_gpsimd(3, GPSIMD_EARLY)
+        h_on_vector(0)
+        gate_turned = bank("w3_0", [P, P], "gate_turned")
+        nc.tensor.transpose(gate_turned[:], gate_rows[:], identity[:])
+        nc.scalar.copy(gate_cols[:], gate_turned[:, 0:CHUNKS])
+        h_on_vector(1)
+        other_h_on_vector(3, GPSIMD_EARLY)
+        y = second_product(0, "w1_0")
+        gate_and_turn(0, y, 0, 1, "w1_3")
+        gate_and_turn(0, y, 1, 2, "w3_0")
+        gate_and_turn(1, second_product(1, "w1_1"), 0, BLOCKS, "w3_1")
         h[2] = mx_tile([P, CHUNK, PACK], BF16, "h2", "h0")
-        part_on_gpsimd(2, 0, 32)
-        part_on_vector(2, 32, 128)
-        finish(3)
-        finish(2)
-        gather_res(1, 0, 4, "h3")
+        first_h_on_gpsimd(2, GPSIMD_LATE)
+        other_h_on_vector(2, GPSIMD_LATE)
+        gate_and_turn(3, second_product(3, "w1_3"), 0, BLOCKS, "w3_3")
+        gate_and_turn(2, second_product(2, "w3_0"), 0, BLOCKS, "w3_2")
+        picked_res.append(gather_res(1, "h3"))
 
         for c0, c1 in SCATTER_RANGES:
+            entries = slice(c0 * CHUNK, c1 * CHUNK)
             for b in range(BLOCKS):
-                picked, first = picked_res[b, c0]
                 nc.vector.tensor_tensor(
                     stream[b][:].indirect(offsets[:, c0 * LIST_COLS : c1 * LIST_COLS]),
-                    gated[:, b, c0 * CHUNK : c1 * CHUNK],
-                    picked[:, (c0 - first) * CHUNK : (c1 - first) * CHUNK],
+                    gated[:, b, entries],
+                    picked_res[b][:, entries],
                     ADD,
                 )
         for b in range(BLOCKS):

@@ -88,7 +88,8 @@ def tile_picked_modres_glusilu_p_kernel(
 
         stream = [keep.tile([P, T], F32, name="stream%d" % b) for b in range(BLOCKS)]
         w2_codes = mx_tile([P, N], U32, "w2_codes")
-        nc.sync.dma_start(stream[0][:], res[0:P, :])
+        for b in range(BLOCKS):
+            nc.sync.dma_start(stream[b][:], res[b * P : (b + 1) * P, :])
         nc.sync.dma_start(gate_rows[0:CHUNKS, :], gate[0, :].rearrange("(c p) -> c p", p=CHUNK))
         load_words(w2_codes, w2_words[0])
         for q in range(QUADRANTS):
@@ -96,7 +97,6 @@ def tile_picked_modres_glusilu_p_kernel(
                 w2_scale[32 * q : 32 * q + SCALE_ROWS, :].bitcast(I32),
                 w2_scales[0, SCALE_ROWS * q : SCALE_ROWS * (q + 1), :].bitcast(I32),
             )
-        nc.sync.dma_start(stream[1][:], res[P : 2 * P, :])
 
         x_codes = [mx_tile([P, S], U32, "x_codes%d" % g) for g in range(PASSES)]
         x_scale = mx_tile([P, S], U8, "x_scale")
@@ -184,26 +184,25 @@ def tile_picked_modres_glusilu_p_kernel(
             product = w3_acc[c][:, :, count:].rearrange("p t n -> p n t")
             nc.vector.tensor_tensor(h[c][:, count:], product, silu[c][:, count:], MULT)
 
-        def second_product(c, tag):
+        def quantise_h(c):
             nc.vector.quantize_mx(
                 out=h_codes[c][:].bitcast(FP8X4), scales=h_scale[c][:], in_=h[c][:].rearrange("p n t -> p (n t)")
             )
-            y = bank(tag, [CHUNK, N], "y%d" % c)
+
+        def gated_result(c, b0, b1, y_tag, turned_tag):
+            cols = slice(b0 * P, b1 * P)
+            y = bank(y_tag, [CHUNK, (b1 - b0) * P], "y%d_%d" % (c, b0))
             nc.tensor.matmul_mx(
                 out=y[:],
                 lhsT=h_codes[c][:].bitcast(FP8X4),
                 lhsT_scale=h_scale[c][:],
-                rhs=w2_codes[:].bitcast(FP8X4),
-                rhs_scale=w2_scale[:],
+                rhs=w2_codes[:, cols].bitcast(FP8X4),
+                rhs_scale=w2_scale[:, cols],
                 start=True,
                 stop=True,
             )
-            return y
-
-        def gate_and_turn(c, y, b0, b1, tag):
-            cols = slice(b0 * P, b1 * P)
-            nc.scalar.activation(gated_rows[c][:, cols], y[:, cols], COPY, scale=gate_cols[:, c : c + 1])
-            turned = bank(tag, [P, b1 - b0, CHUNK], "y_turned%d_%d" % (c, b0))
+            nc.scalar.activation(gated_rows[c][:, cols], y[:], COPY, scale=gate_cols[:, c : c + 1])
+            turned = bank(turned_tag, [P, b1 - b0, CHUNK], "y_turned%d_%d" % (c, b0))
             for b in range(b0, b1):
                 nc.tensor.transpose(turned[:, b - b0, :], gated_rows[c][:, b * P : (b + 1) * P], identity[:])
             nc.scalar.copy(gated[:, b0:b1, c * CHUNK : (c + 1) * CHUNK], turned[:])
@@ -222,16 +221,19 @@ def tile_picked_modres_glusilu_p_kernel(
         nc.scalar.copy(gate_cols[:], gate_turned[:, 0:CHUNKS])
         h_on_vector(1)
         other_h_on_vector(3, GPSIMD_EARLY)
-        y = second_product(0, "w1_0")
-        gate_and_turn(0, y, 0, 1, "w1_3")
-        gate_and_turn(0, y, 1, 2, "w3_0")
-        gate_and_turn(1, second_product(1, "w1_1"), 0, BLOCKS, "w3_1")
+        quantise_h(0)
+        gated_result(0, 0, 1, "w1_0", "w1_3")
+        gated_result(0, 1, 2, "w1_2", "w3_0")
+        quantise_h(1)
+        gated_result(1, 0, BLOCKS, "w1_1", "w3_1")
         h[2] = mx_tile([P, CHUNK, PACK], BF16, "h2", "h0")
         first_h_on_gpsimd(2, GPSIMD_LATE)
         other_h_on_vector(2, GPSIMD_LATE)
-        gate_and_turn(3, second_product(3, "w1_3"), 0, BLOCKS, "w3_3")
-        gate_and_turn(2, second_product(2, "w3_0"), 0, BLOCKS, "w3_2")
-        picked_res.append(gather_res(1, "h3"))
+        quantise_h(3)
+        gated_result(3, 0, BLOCKS, "w1_3", "w3_3")
+        picked_res.append(gather_res(1, "h1"))
+        quantise_h(2)
+        gated_result(2, 0, BLOCKS, "w3_0", "w3_2")
 
         for c0, c1 in SCATTER_RANGES:
             entries = slice(c0 * CHUNK, c1 * CHUNK)

@@ -25,17 +25,8 @@ SCALE_ROWS = 4
 PASSES = K // (P * PACK)
 CHUNK = 128
 CHUNKS = S // CHUNK
-LIST_COLS = CHUNK // 16
-BLOCKS = N // P
 MX_ALIGN = 64
-
 SCALAR_SHARE = 44
-
-GPSIMD_EARLY = 104
-GPSIMD_LATE = 28
-PRODUCT_ORDER = (3, 0, 1, 2)
-
-SCATTER_RANGES = [(0, 1), (1, 2), (2, 4)]
 
 
 def tile_picked_modres_glusilu_p_kernel(
@@ -53,6 +44,9 @@ def tile_picked_modres_glusilu_p_kernel(
             return psum.tile(shape, F32, name=name, tag=tag)
 
         offsets = keep.tile([P, S // 16], U16, name="offsets")
+
+        def entries_of(lo, hi):
+            return offsets[:, lo // 16 : hi // 16]
 
         x_scale_table = mx_tile([P, T], U8, "x_scale_table")
         nc.gpsimd.memset(x_scale_table[:].bitcast(I32), 0)
@@ -86,17 +80,20 @@ def tile_picked_modres_glusilu_p_kernel(
         w3_raw0 = load_weight(w3, 0, "w3_raw0")
         w3_raw1 = load_weight(w3, 1, "w3_raw1")
 
-        stream = [keep.tile([P, T], F32, name="stream%d" % b) for b in range(BLOCKS)]
-        w2_codes = mx_tile([P, N], U32, "w2_codes")
-        for b in range(BLOCKS):
-            nc.sync.dma_start(stream[b][:], res[b * P : (b + 1) * P, :])
+        upper = keep.tile([P, T], F32, name="upper")
+        lower = keep.tile([P, T], F32, name="lower")
+        nc.sync.dma_start(upper[:], res[0:P, :])
+        nc.sync.dma_start(lower[:], res[P:N, :])
         nc.sync.dma_start(gate_rows[0:CHUNKS, :], gate[0, :].rearrange("(c p) -> c p", p=CHUNK))
+        w2_codes = mx_tile([P, N], U32, "w2_codes")
         load_words(w2_codes, w2_words[0])
         for q in range(QUADRANTS):
             nc.sync.dma_start(
                 w2_scale[32 * q : 32 * q + SCALE_ROWS, :].bitcast(I32),
                 w2_scales[0, SCALE_ROWS * q : SCALE_ROWS * (q + 1), :].bitcast(I32),
             )
+        gate_wide = keep.tile([P, S], F32, name="gate_wide")
+        nc.sync.dma_start(gate_wide[:], gate)
 
         x_codes = [mx_tile([P, S], U32, "x_codes%d" % g) for g in range(PASSES)]
         x_scale = mx_tile([P, S], U8, "x_scale")
@@ -128,7 +125,7 @@ def tile_picked_modres_glusilu_p_kernel(
             accs = [bank("%s_%d" % (name, c), [P, PACK, CHUNK], "%s_acc%d" % (name, c)) for c in range(CHUNKS)]
             for g in range(PASSES):
                 codes, scale = passes[g]
-                for c in PRODUCT_ORDER:
+                for c in range(CHUNKS):
                     entries = slice(c * CHUNK, (c + 1) * CHUNK)
                     for t in range(PACK):
                         cols = slice(t * P, (t + 1) * P)
@@ -157,92 +154,110 @@ def tile_picked_modres_glusilu_p_kernel(
         def words_by_pairs(tile):
             return tile.rearrange("p (n e) t -> p n t e", e=2)
 
-        silu = {}
-        for c in PRODUCT_ORDER:
-            shared = c >= 2
-            shape = [P, CHUNK, PACK] if shared else [P, CHUNK // 2, PACK, 2]
-            silu[c] = mx_tile(shape, F32, "silu%d" % c, "w3_raw1" if c == PRODUCT_ORDER[-1] else None)
-            nc.scalar.activation(words_by_pairs(silu[c][:]) if shared else silu[c][:], by_pairs(w1_acc[c]), SILU)
+        silu = []
+        for c in range(CHUNKS):
+            silu.append(mx_tile([P, CHUNK // 2, PACK, 2], F32, "silu%d" % c, "w3_raw1" if c == CHUNKS - 1 else None))
+            nc.scalar.activation(silu[c][:], by_pairs(w1_acc[c]), SILU)
 
-        h_codes = [mx_tile([P, CHUNK], U32, "h_codes%d" % c) for c in range(CHUNKS)]
-        h_scale = [mx_tile([P, CHUNK], U8, "h_scale%d" % c) for c in range(CHUNKS)]
-        h = {}
-        gated_rows = [keep.tile([CHUNK, N], F32, name="gated_rows%d" % c) for c in range(CHUNKS)]
-        gated = keep.tile([P, BLOCKS, S], F32, name="gated")
+        half = S // 2
+        upper_first = mx_tile([P, half], F32, "upper_first", "staging0")
+        nc.vector.tensor_copy(upper_first[:], upper[:].indirect(entries_of(0, half)))
+        upper_second = mx_tile([P, half], F32, "upper_second", "staging1")
+        nc.scalar.activation(upper_second[:], upper[:].indirect(entries_of(half, S)), COPY)
+        upper_picked = [upper_first, upper_second]
+        lower_picked = mx_tile([P, S], F32, "lower_picked", "w3_1_codes")
+        nc.scalar.activation(lower_picked[:], lower[:].indirect(offsets[:]), COPY)
+
         gate_cols = keep.tile([P, CHUNKS], F32, name="gate_cols")
+        gate_turned = bank("w1_2", [P, P], "gate_turned")
+        nc.tensor.transpose(gate_turned[:], gate_rows[:], identity[:])
+        nc.scalar.copy(gate_cols[:], gate_turned[:, 0:CHUNKS])
 
-        def h_on_vector(c):
+        h_codes = mx_tile([P, S], U32, "h_codes")
+        h_scale = mx_tile([P, S], U8, "h_scale")
+        h = {}
+        turned = {}
+        upper_new = {}
+        lower_gated = keep.tile([P, S], F32, name="lower_gated")
+
+        def make_h(c):
             h[c] = mx_tile([P, CHUNK, PACK], BF16, "h%d" % c)
             nc.vector.tensor_tensor(words_by_pairs(h[c][:]), by_pairs(w3_acc[c]), silu[c][:], MULT)
 
-        def first_h_on_gpsimd(c, count):
-            product = mx_tile([P, count, PACK], F32, "product%d" % c)
-            nc.scalar.copy(words_by_pairs(product[:]), by_pairs(w3_acc[c])[:, : count // 2])
-            nc.gpsimd.tensor_tensor(h[c][:, :count], product[:], silu[c][:, :count], MULT)
-
-        def other_h_on_vector(c, count):
-            product = w3_acc[c][:, :, count:].rearrange("p t n -> p n t")
-            nc.vector.tensor_tensor(h[c][:, count:], product, silu[c][:, count:], MULT)
-
         def quantise_h(c):
+            entries = slice(c * CHUNK, (c + 1) * CHUNK)
             nc.vector.quantize_mx(
-                out=h_codes[c][:].bitcast(FP8X4), scales=h_scale[c][:], in_=h[c][:].rearrange("p n t -> p (n t)")
+                out=h_codes[:, entries].bitcast(FP8X4),
+                scales=h_scale[:, entries],
+                in_=h[c][:].rearrange("p n t -> p (n t)"),
             )
 
-        def gated_result(c, b0, b1, y_tag, turned_tag):
-            cols = slice(b0 * P, b1 * P)
-            y = bank(y_tag, [CHUNK, (b1 - b0) * P], "y%d_%d" % (c, b0))
+        def upper_product(c):
+            entries = slice(c * CHUNK, (c + 1) * CHUNK)
+            y = bank("w1_%d" % c, [CHUNK, P], "upper_y%d" % c)
             nc.tensor.matmul_mx(
                 out=y[:],
-                lhsT=h_codes[c][:].bitcast(FP8X4),
-                lhsT_scale=h_scale[c][:],
-                rhs=w2_codes[:, cols].bitcast(FP8X4),
-                rhs_scale=w2_scale[:, cols],
+                lhsT=h_codes[:, entries].bitcast(FP8X4),
+                lhsT_scale=h_scale[:, entries],
+                rhs=w2_codes[:, 0:P].bitcast(FP8X4),
+                rhs_scale=w2_scale[:, 0:P],
                 start=True,
                 stop=True,
             )
-            nc.scalar.activation(gated_rows[c][:, cols], y[:], COPY, scale=gate_cols[:, c : c + 1])
-            turned = bank(turned_tag, [P, b1 - b0, CHUNK], "y_turned%d_%d" % (c, b0))
-            for b in range(b0, b1):
-                nc.tensor.transpose(turned[:, b - b0, :], gated_rows[c][:, b * P : (b + 1) * P], identity[:])
-            nc.scalar.copy(gated[:, b0:b1, c * CHUNK : (c + 1) * CHUNK], turned[:])
+            rows = keep.tile([CHUNK, P], F32, name="upper_rows%d" % c)
+            nc.scalar.activation(rows[:], y[:], COPY, scale=gate_cols[:, c : c + 1])
+            turned[c] = bank("w3_%d" % c, [P, CHUNK], "upper_turned%d" % c)
+            nc.tensor.transpose(turned[c][:], rows[:], identity[:])
 
-        def gather_res(b, tag):
-            picked = mx_tile([P, S], F32, "picked_res%d" % b, tag)
-            nc.vector.tensor_copy(picked[:], stream[b][:].indirect(offsets[:]))
-            return picked
+        def upper_sum(c):
+            upper_new[c] = keep.tile([P, CHUNK], F32, name="upper_new%d" % c)
+            picked = upper_picked[c // 2][:, (c % 2) * CHUNK : (c % 2 + 1) * CHUNK]
+            nc.vector.tensor_tensor(upper_new[c][:], turned[c][:], picked, ADD)
 
-        picked_res = [gather_res(0, "staging0")]
-        h[3] = mx_tile([P, CHUNK, PACK], BF16, "h3")
-        first_h_on_gpsimd(3, GPSIMD_EARLY)
-        h_on_vector(0)
-        gate_turned = bank("w3_0", [P, P], "gate_turned")
-        nc.tensor.transpose(gate_turned[:], gate_rows[:], identity[:])
-        nc.scalar.copy(gate_cols[:], gate_turned[:, 0:CHUNKS])
-        h_on_vector(1)
-        other_h_on_vector(3, GPSIMD_EARLY)
+        def upper_scatter(c):
+            nc.scalar.activation(upper[:].indirect(entries_of(c * CHUNK, (c + 1) * CHUNK)), upper_new[c][:], COPY)
+
+        def lower_product(lo, hi, tag):
+            y = bank(tag, [P, hi - lo], "lower_y%d" % lo)
+            nc.tensor.matmul_mx(
+                out=y[:],
+                lhsT=w2_codes[:, P:N].bitcast(FP8X4),
+                lhsT_scale=w2_scale[:, P:N],
+                rhs=h_codes[:, lo:hi].bitcast(FP8X4),
+                rhs_scale=h_scale[:, lo:hi],
+                start=True,
+                stop=True,
+            )
+            nc.vector.tensor_tensor(lower_gated[:, lo:hi], y[:], gate_wide[:, lo:hi], MULT)
+
+        def lower_scatter(lo, hi):
+            nc.vector.tensor_tensor(
+                lower[:].indirect(entries_of(lo, hi)), lower_gated[:, lo:hi], lower_picked[:, lo:hi], ADD
+            )
+
+        make_h(0)
+        make_h(1)
         quantise_h(0)
-        gated_result(0, 0, 1, "w1_0", "w1_3")
-        gated_result(0, 1, 2, "w1_2", "w3_0")
+        upper_product(0)
+        make_h(2)
         quantise_h(1)
-        gated_result(1, 0, BLOCKS, "w1_1", "w3_1")
-        h[2] = mx_tile([P, CHUNK, PACK], BF16, "h2", "h0")
-        first_h_on_gpsimd(2, GPSIMD_LATE)
-        other_h_on_vector(2, GPSIMD_LATE)
-        quantise_h(3)
-        gated_result(3, 0, BLOCKS, "w1_3", "w3_3")
-        picked_res.append(gather_res(1, "h1"))
+        upper_product(1)
+        upper_sum(0)
+        upper_scatter(0)
+        make_h(3)
         quantise_h(2)
-        gated_result(2, 0, BLOCKS, "w3_0", "w3_2")
-
-        for c0, c1 in SCATTER_RANGES:
-            entries = slice(c0 * CHUNK, c1 * CHUNK)
-            for b in range(BLOCKS):
-                nc.vector.tensor_tensor(
-                    stream[b][:].indirect(offsets[:, c0 * LIST_COLS : c1 * LIST_COLS]),
-                    gated[:, b, entries],
-                    picked_res[b][:, entries],
-                    ADD,
-                )
-        for b in range(BLOCKS):
-            nc.sync.dma_start(out[b * P : (b + 1) * P, :], stream[b][:])
+        upper_product(2)
+        upper_sum(1)
+        upper_scatter(1)
+        quantise_h(3)
+        upper_product(3)
+        lower_product(0, half, "w1_0")
+        upper_sum(2)
+        upper_scatter(2)
+        lower_scatter(0, CHUNK)
+        upper_sum(3)
+        upper_scatter(3)
+        nc.sync.dma_start(out[0:P, :], upper[:])
+        lower_product(half, S, "w1_1")
+        lower_scatter(CHUNK, S)
+        nc.sync.dma_start(out[P:N, :], lower[:])

@@ -1,7 +1,6 @@
 from contextlib import ExitStack
 
 import concourse.mybir as mybir
-from concourse.masks import make_identity
 
 K, T, S, H, N = 1024, 1024, 512, 512, 256
 FLOPS = 2 * (2 * K * H * S + H * N * S)
@@ -27,6 +26,10 @@ CHUNK = 128
 CHUNKS = S // CHUNK
 MX_ALIGN = 64
 SCALAR_SHARE = 44
+PRODUCT_ORDER = (1, 0, 2, 3)
+VECTOR_PICKS = 160
+GPSIMD_EARLY = 48
+GPSIMD_LATE = 80
 
 
 def tile_picked_modres_glusilu_p_kernel(
@@ -50,12 +53,8 @@ def tile_picked_modres_glusilu_p_kernel(
 
         x_scale_table = mx_tile([P, T], U8, "x_scale_table")
         nc.gpsimd.memset(x_scale_table[:].bitcast(I32), 0)
-        gate_rows = keep.tile([P, P], F32, name="gate_rows")
-        nc.gpsimd.memset(gate_rows[:], 0.0)
         w2_scale = mx_tile([P, N], U8, "w2_scale")
         nc.gpsimd.memset(w2_scale[:].bitcast(I32), 0)
-        identity = keep.tile([P, P], F32, name="identity")
-        make_identity(nc, identity[:])
 
         def load_words(tile, words):
             nc.sync.dma_start(tile[:].bitcast(I32), words.rearrange("p n t -> p (n t)").bitcast(I32))
@@ -83,8 +82,9 @@ def tile_picked_modres_glusilu_p_kernel(
         upper = keep.tile([P, T], F32, name="upper")
         lower = keep.tile([P, T], F32, name="lower")
         nc.sync.dma_start(upper[:], res[0:P, :])
+        gate_wide = keep.tile([P, S], F32, name="gate_wide")
+        nc.sync.dma_start(gate_wide[:], gate)
         nc.sync.dma_start(lower[:], res[P:N, :])
-        nc.sync.dma_start(gate_rows[0:CHUNKS, :], gate[0, :].rearrange("(c p) -> c p", p=CHUNK))
         w2_codes = mx_tile([P, N], U32, "w2_codes")
         load_words(w2_codes, w2_words[0])
         for q in range(QUADRANTS):
@@ -92,8 +92,6 @@ def tile_picked_modres_glusilu_p_kernel(
                 w2_scale[32 * q : 32 * q + SCALE_ROWS, :].bitcast(I32),
                 w2_scales[0, SCALE_ROWS * q : SCALE_ROWS * (q + 1), :].bitcast(I32),
             )
-        gate_wide = keep.tile([P, S], F32, name="gate_wide")
-        nc.sync.dma_start(gate_wide[:], gate)
 
         x_codes = [mx_tile([P, S], U32, "x_codes%d" % g) for g in range(PASSES)]
         x_scale = mx_tile([P, S], U8, "x_scale")
@@ -125,9 +123,11 @@ def tile_picked_modres_glusilu_p_kernel(
             accs = [bank("%s_%d" % (name, c), [P, PACK, CHUNK], "%s_acc%d" % (name, c)) for c in range(CHUNKS)]
             for g in range(PASSES):
                 codes, scale = passes[g]
-                for c in range(CHUNKS):
+                for c in PRODUCT_ORDER:
                     entries = slice(c * CHUNK, (c + 1) * CHUNK)
-                    for t in range(PACK):
+                    late = c in PRODUCT_ORDER[2:]
+                    for step in range(PACK):
+                        t = (step + 2) % PACK if late else step
                         cols = slice(t * P, (t + 1) * P)
                         nc.tensor.matmul_mx(
                             out=accs[c][:, t, :],
@@ -135,8 +135,8 @@ def tile_picked_modres_glusilu_p_kernel(
                             lhsT_scale=scale[:, cols],
                             rhs=x_codes[g][:, entries].bitcast(FP8X4),
                             rhs_scale=x_scale[SCALE_ROWS * g : P, entries],
-                            start=(g == 0 and t == 0),
-                            stop=(g == PASSES - 1 and t == PACK - 1),
+                            start=(g == 0 and step == 0),
+                            stop=(g == PASSES - 1 and step == PACK - 1),
                         )
             return accs
 
@@ -154,110 +154,90 @@ def tile_picked_modres_glusilu_p_kernel(
         def words_by_pairs(tile):
             return tile.rearrange("p (n e) t -> p n t e", e=2)
 
-        silu = []
-        for c in range(CHUNKS):
-            silu.append(mx_tile([P, CHUNK // 2, PACK, 2], F32, "silu%d" % c, "w3_raw1" if c == CHUNKS - 1 else None))
-            nc.scalar.activation(silu[c][:], by_pairs(w1_acc[c]), SILU)
+        silu = {}
+        for c in PRODUCT_ORDER:
+            shared = c % 2 == 1
+            shape = [P, CHUNK, PACK] if shared else [P, CHUNK // 2, PACK, 2]
+            silu[c] = mx_tile(shape, F32, "silu%d" % c, "w3_raw1" if c == PRODUCT_ORDER[-1] else None)
+            nc.scalar.activation(words_by_pairs(silu[c][:]) if shared else silu[c][:], by_pairs(w1_acc[c]), SILU)
+
+        def product_for_gpsimd(c, count):
+            product = mx_tile([P, count, PACK], F32, "product%d" % c)
+            nc.scalar.copy(words_by_pairs(product[:]), by_pairs(w3_acc[c])[:, : count // 2])
+            return product
 
         half = S // 2
         upper_first = mx_tile([P, half], F32, "upper_first", "staging0")
-        nc.vector.tensor_copy(upper_first[:], upper[:].indirect(entries_of(0, half)))
-        upper_second = mx_tile([P, half], F32, "upper_second", "staging1")
+        nc.vector.tensor_copy(upper_first[:, :VECTOR_PICKS], upper[:].indirect(entries_of(0, VECTOR_PICKS)))
+        nc.scalar.activation(upper_first[:, VECTOR_PICKS:], upper[:].indirect(entries_of(VECTOR_PICKS, half)), COPY)
+        product1 = product_for_gpsimd(1, GPSIMD_EARLY)
+        product3 = product_for_gpsimd(3, GPSIMD_LATE)
+        upper_second = mx_tile([P, half], F32, "upper_second", "w3_1_scale")
         nc.scalar.activation(upper_second[:], upper[:].indirect(entries_of(half, S)), COPY)
-        upper_picked = [upper_first, upper_second]
         lower_picked = mx_tile([P, S], F32, "lower_picked", "w3_1_codes")
         nc.scalar.activation(lower_picked[:], lower[:].indirect(offsets[:]), COPY)
 
-        gate_cols = keep.tile([P, CHUNKS], F32, name="gate_cols")
-        gate_turned = bank("w1_2", [P, P], "gate_turned")
-        nc.tensor.transpose(gate_turned[:], gate_rows[:], identity[:])
-        nc.scalar.copy(gate_cols[:], gate_turned[:, 0:CHUNKS])
 
-        h_codes = mx_tile([P, S], U32, "h_codes")
-        h_scale = mx_tile([P, S], U8, "h_scale")
-        h = {}
-        turned = {}
-        upper_new = {}
-        lower_gated = keep.tile([P, S], F32, name="lower_gated")
+        upper_new = keep.tile([P, S], F32, name="upper_new")
 
-        def make_h(c):
-            h[c] = mx_tile([P, CHUNK, PACK], BF16, "h%d" % c)
-            nc.vector.tensor_tensor(words_by_pairs(h[c][:]), by_pairs(w3_acc[c]), silu[c][:], MULT)
+        def pair_of_h(pair, product, count):
+            h = mx_tile([P, half, PACK], BF16, "h%d" % pair, "h")
+            first, second = 2 * pair, 2 * pair + 1
+            nc.gpsimd.tensor_tensor(h[:, CHUNK : CHUNK + count], product[:], silu[second][:, :count], MULT)
+            nc.vector.tensor_tensor(words_by_pairs(h[:, :CHUNK]), by_pairs(w3_acc[first]), silu[first][:], MULT)
+            rest = w3_acc[second][:, :, count:].rearrange("p t n -> p n t")
+            nc.vector.tensor_tensor(h[:, CHUNK + count :], rest, silu[second][:, count:], MULT)
+            return h
 
-        def quantise_h(c):
-            entries = slice(c * CHUNK, (c + 1) * CHUNK)
-            nc.vector.quantize_mx(
-                out=h_codes[:, entries].bitcast(FP8X4),
-                scales=h_scale[:, entries],
-                in_=h[c][:].rearrange("p n t -> p (n t)"),
-            )
+        def quantise_h(h, pair, parts):
+            codes = mx_tile([P, half], U32, "h_codes%d" % pair, "h_codes")
+            scale = mx_tile([P, half], U8, "h_scale%d" % pair)
+            for lo in range(0, half, half // parts):
+                part = slice(lo, lo + half // parts)
+                nc.vector.quantize_mx(
+                    out=codes[:, part].bitcast(FP8X4), scales=scale[:, part], in_=h[:, part].rearrange("p n t -> p (n t)")
+                )
+            return codes, scale
 
-        def upper_product(c):
-            entries = slice(c * CHUNK, (c + 1) * CHUNK)
-            y = bank("w1_%d" % c, [CHUNK, P], "upper_y%d" % c)
+        def second_product(rows, quantised, tag):
+            codes, scale = quantised
+            y = bank(tag, [P, half], "y_" + tag)
             nc.tensor.matmul_mx(
                 out=y[:],
-                lhsT=h_codes[:, entries].bitcast(FP8X4),
-                lhsT_scale=h_scale[:, entries],
-                rhs=w2_codes[:, 0:P].bitcast(FP8X4),
-                rhs_scale=w2_scale[:, 0:P],
+                lhsT=w2_codes[:, rows].bitcast(FP8X4),
+                lhsT_scale=w2_scale[:, rows],
+                rhs=codes[:].bitcast(FP8X4),
+                rhs_scale=scale[:],
                 start=True,
                 stop=True,
             )
-            rows = keep.tile([CHUNK, P], F32, name="upper_rows%d" % c)
-            nc.scalar.activation(rows[:], y[:], COPY, scale=gate_cols[:, c : c + 1])
-            turned[c] = bank("w3_%d" % c, [P, CHUNK], "upper_turned%d" % c)
-            nc.tensor.transpose(turned[c][:], rows[:], identity[:])
+            return y
 
-        def upper_sum(c):
-            upper_new[c] = keep.tile([P, CHUNK], F32, name="upper_new%d" % c)
-            picked = upper_picked[c // 2][:, (c % 2) * CHUNK : (c % 2 + 1) * CHUNK]
-            nc.vector.tensor_tensor(upper_new[c][:], turned[c][:], picked, ADD)
+        def times_gate(gated, y, entries):
+            nc.vector.tensor_tensor(gated[:, entries], y[:], gate_wide[:, entries], MULT)
 
-        def upper_scatter(c):
-            nc.scalar.activation(upper[:].indirect(entries_of(c * CHUNK, (c + 1) * CHUNK)), upper_new[c][:], COPY)
+        def put_upper(entries, picked):
+            nc.vector.tensor_tensor(upper_new[:, entries], upper_gated[:, entries], picked[:], ADD)
+            nc.scalar.activation(upper[:].indirect(entries_of(entries.start, entries.stop)), upper_new[:, entries], COPY)
 
-        def lower_product(lo, hi, tag):
-            y = bank(tag, [P, hi - lo], "lower_y%d" % lo)
-            nc.tensor.matmul_mx(
-                out=y[:],
-                lhsT=w2_codes[:, P:N].bitcast(FP8X4),
-                lhsT_scale=w2_scale[:, P:N],
-                rhs=h_codes[:, lo:hi].bitcast(FP8X4),
-                rhs_scale=h_scale[:, lo:hi],
-                start=True,
-                stop=True,
-            )
-            nc.vector.tensor_tensor(lower_gated[:, lo:hi], y[:], gate_wide[:, lo:hi], MULT)
+        upper_gated = keep.tile([P, S], F32, name="upper_gated")
 
-        def lower_scatter(lo, hi):
-            nc.vector.tensor_tensor(
-                lower[:].indirect(entries_of(lo, hi)), lower_gated[:, lo:hi], lower_picked[:, lo:hi], ADD
-            )
-
-        make_h(0)
-        make_h(1)
-        quantise_h(0)
-        upper_product(0)
-        make_h(2)
-        quantise_h(1)
-        upper_product(1)
-        upper_sum(0)
-        upper_scatter(0)
-        make_h(3)
-        quantise_h(2)
-        upper_product(2)
-        upper_sum(1)
-        upper_scatter(1)
-        quantise_h(3)
-        upper_product(3)
-        lower_product(0, half, "w1_0")
-        upper_sum(2)
-        upper_scatter(2)
-        lower_scatter(0, CHUNK)
-        upper_sum(3)
-        upper_scatter(3)
-        nc.sync.dma_start(out[0:P, :], upper[:])
-        lower_product(half, S, "w1_1")
-        lower_scatter(CHUNK, S)
-        nc.sync.dma_start(out[P:N, :], lower[:])
+        upper_rows, lower_rows = slice(0, P), slice(P, N)
+        first, second = slice(0, half), slice(half, S)
+        quantised = quantise_h(pair_of_h(0, product1, GPSIMD_EARLY), 0, 2)
+        upper_y = second_product(upper_rows, quantised, "w1_0")
+        lower_y = second_product(lower_rows, quantised, "w1_1")
+        h23 = pair_of_h(1, product3, GPSIMD_LATE)
+        times_gate(upper_gated, upper_y, first)
+        quantised = quantise_h(h23, 1, 1)
+        put_upper(first, upper_first)
+        lower_gated = mx_tile([P, S], F32, "lower_gated", "h")
+        times_gate(lower_gated, lower_y, first)
+        upper_y = second_product(upper_rows, quantised, "w1_2")
+        lower_y = second_product(lower_rows, quantised, "w1_3")
+        times_gate(upper_gated, upper_y, second)
+        times_gate(lower_gated, lower_y, second)
+        put_upper(second, upper_second)
+        nc.sync.dma_start(out[upper_rows, :], upper[:])
+        nc.vector.tensor_tensor(lower[:].indirect(offsets[:]), lower_gated[:], lower_picked[:], ADD)
+        nc.sync.dma_start(out[lower_rows, :], lower[:])

@@ -26,10 +26,9 @@ CHUNK = 128
 CHUNKS = S // CHUNK
 MX_ALIGN = 64
 SCALAR_SHARE = 44
-PRODUCT_ORDER = (1, 0, 2, 3)
-VECTOR_PICKS = 160
-GPSIMD_EARLY = 48
-GPSIMD_LATE = 80
+PRODUCT_ORDER = (0, 1, 3, 2)
+VECTOR_PICKS = 192
+GPSIMD_SHARE = 80
 
 
 def tile_picked_modres_glusilu_p_kernel(
@@ -81,10 +80,9 @@ def tile_picked_modres_glusilu_p_kernel(
 
         upper = keep.tile([P, T], F32, name="upper")
         lower = keep.tile([P, T], F32, name="lower")
-        nc.sync.dma_start(upper[:], res[0:P, :])
+        nc.sync.dma_start(lower[:], res[P:N, :])
         gate_wide = keep.tile([P, S], F32, name="gate_wide")
         nc.sync.dma_start(gate_wide[:], gate)
-        nc.sync.dma_start(lower[:], res[P:N, :])
         w2_codes = mx_tile([P, N], U32, "w2_codes")
         load_words(w2_codes, w2_words[0])
         for q in range(QUADRANTS):
@@ -92,6 +90,7 @@ def tile_picked_modres_glusilu_p_kernel(
                 w2_scale[32 * q : 32 * q + SCALE_ROWS, :].bitcast(I32),
                 w2_scales[0, SCALE_ROWS * q : SCALE_ROWS * (q + 1), :].bitcast(I32),
             )
+        nc.sync.dma_start(upper[:], res[0:P, :])
 
         x_codes = [mx_tile([P, S], U32, "x_codes%d" % g) for g in range(PASSES)]
         x_scale = mx_tile([P, S], U8, "x_scale")
@@ -156,7 +155,7 @@ def tile_picked_modres_glusilu_p_kernel(
 
         silu = {}
         for c in PRODUCT_ORDER:
-            shared = c % 2 == 1
+            shared = c == 3
             shape = [P, CHUNK, PACK] if shared else [P, CHUNK // 2, PACK, 2]
             silu[c] = mx_tile(shape, F32, "silu%d" % c, "w3_raw1" if c == PRODUCT_ORDER[-1] else None)
             nc.scalar.activation(words_by_pairs(silu[c][:]) if shared else silu[c][:], by_pairs(w1_acc[c]), SILU)
@@ -167,27 +166,19 @@ def tile_picked_modres_glusilu_p_kernel(
             return product
 
         half = S // 2
-        upper_first = mx_tile([P, half], F32, "upper_first", "staging0")
-        nc.vector.tensor_copy(upper_first[:, :VECTOR_PICKS], upper[:].indirect(entries_of(0, VECTOR_PICKS)))
-        nc.scalar.activation(upper_first[:, VECTOR_PICKS:], upper[:].indirect(entries_of(VECTOR_PICKS, half)), COPY)
-        product1 = product_for_gpsimd(1, GPSIMD_EARLY)
-        product3 = product_for_gpsimd(3, GPSIMD_LATE)
+        lower_picked = mx_tile([P, S], F32, "lower_picked", "staging0")
+        nc.vector.tensor_copy(lower_picked[:, :VECTOR_PICKS], lower[:].indirect(entries_of(0, VECTOR_PICKS)))
+        nc.scalar.activation(lower_picked[:, VECTOR_PICKS:], lower[:].indirect(entries_of(VECTOR_PICKS, S)), COPY)
+        product3 = product_for_gpsimd(3, GPSIMD_SHARE)
         upper_second = mx_tile([P, half], F32, "upper_second", "w3_1_scale")
         nc.scalar.activation(upper_second[:], upper[:].indirect(entries_of(half, S)), COPY)
-        lower_picked = mx_tile([P, S], F32, "lower_picked", "w3_1_codes")
-        nc.scalar.activation(lower_picked[:], lower[:].indirect(offsets[:]), COPY)
-
+        upper_first = mx_tile([P, half], F32, "upper_first", "w3_1_codes")
+        nc.scalar.activation(upper_first[:], upper[:].indirect(entries_of(0, half)), COPY)
 
         upper_new = keep.tile([P, S], F32, name="upper_new")
 
-        def pair_of_h(pair, product, count):
-            h = mx_tile([P, half, PACK], BF16, "h%d" % pair, "h")
-            first, second = 2 * pair, 2 * pair + 1
-            nc.gpsimd.tensor_tensor(h[:, CHUNK : CHUNK + count], product[:], silu[second][:, :count], MULT)
-            nc.vector.tensor_tensor(words_by_pairs(h[:, :CHUNK]), by_pairs(w3_acc[first]), silu[first][:], MULT)
-            rest = w3_acc[second][:, :, count:].rearrange("p t n -> p n t")
-            nc.vector.tensor_tensor(h[:, CHUNK + count :], rest, silu[second][:, count:], MULT)
-            return h
+        def make_h(dst, c):
+            nc.vector.tensor_tensor(words_by_pairs(dst), by_pairs(w3_acc[c]), silu[c][:], MULT)
 
         def quantise_h(h, pair, parts):
             codes = mx_tile([P, half], U32, "h_codes%d" % pair, "h_codes")
@@ -214,30 +205,39 @@ def tile_picked_modres_glusilu_p_kernel(
             return y
 
         def times_gate(gated, y, entries):
-            nc.vector.tensor_tensor(gated[:, entries], y[:], gate_wide[:, entries], MULT)
+            nc.vector.tensor_tensor(gated, y[:], gate_wide[:, entries], MULT)
 
-        def put_upper(entries, picked):
-            nc.vector.tensor_tensor(upper_new[:, entries], upper_gated[:, entries], picked[:], ADD)
+        def put_upper(entries, gated, picked):
+            nc.vector.tensor_tensor(upper_new[:, entries], gated[:], picked[:], ADD)
             nc.scalar.activation(upper[:].indirect(entries_of(entries.start, entries.stop)), upper_new[:, entries], COPY)
 
-        upper_gated = keep.tile([P, S], F32, name="upper_gated")
 
         upper_rows, lower_rows = slice(0, P), slice(P, N)
         first, second = slice(0, half), slice(half, S)
-        quantised = quantise_h(pair_of_h(0, product1, GPSIMD_EARLY), 0, 2)
+        h01 = mx_tile([P, half, PACK], BF16, "h01", "h")
+        make_h(h01[:, :CHUNK], 0)
+        make_h(h01[:, CHUNK:], 1)
+        quantised = quantise_h(h01, 0, 2)
         upper_y = second_product(upper_rows, quantised, "w1_0")
         lower_y = second_product(lower_rows, quantised, "w1_1")
-        h23 = pair_of_h(1, product3, GPSIMD_LATE)
-        times_gate(upper_gated, upper_y, first)
+        h23 = mx_tile([P, half, PACK], BF16, "h23", "h")
+        split = CHUNK + GPSIMD_SHARE
+        nc.gpsimd.tensor_tensor(h23[:, CHUNK:split], product3[:], silu[3][:, :GPSIMD_SHARE], MULT)
+        make_h(h23[:, :CHUNK], 2)
+        rest = w3_acc[3][:, :, GPSIMD_SHARE:].rearrange("p t n -> p n t")
+        nc.vector.tensor_tensor(h23[:, split:], rest, silu[3][:, GPSIMD_SHARE:], MULT)
+        upper_gated = mx_tile([P, half], F32, "upper_gated0", "upper_gated")
+        times_gate(upper_gated[:], upper_y, first)
         quantised = quantise_h(h23, 1, 1)
-        put_upper(first, upper_first)
-        lower_gated = mx_tile([P, S], F32, "lower_gated", "h")
-        times_gate(lower_gated, lower_y, first)
+        put_upper(first, upper_gated, upper_first)
+        lower_gated = mx_tile([P, S], F32, "lower_gated", "w3_1_codes")
+        times_gate(lower_gated[:, first], lower_y, first)
         upper_y = second_product(upper_rows, quantised, "w1_2")
         lower_y = second_product(lower_rows, quantised, "w1_3")
-        times_gate(upper_gated, upper_y, second)
-        times_gate(lower_gated, lower_y, second)
-        put_upper(second, upper_second)
+        upper_gated = mx_tile([P, half], F32, "upper_gated1", "upper_gated")
+        times_gate(upper_gated[:], upper_y, second)
+        times_gate(lower_gated[:, second], lower_y, second)
+        put_upper(second, upper_gated, upper_second)
         nc.sync.dma_start(out[upper_rows, :], upper[:])
         nc.vector.tensor_tensor(lower[:].indirect(offsets[:]), lower_gated[:], lower_picked[:], ADD)
         nc.sync.dma_start(out[lower_rows, :], lower[:])

@@ -27,7 +27,7 @@ CHUNKS = S // CHUNK
 MX_ALIGN = 64
 SCALAR_SHARE = 44
 PRODUCT_ORDER = (0, 1, 3, 2)
-VECTOR_PICKS = 192
+VECTOR_PICKS = 224
 GPSIMD_SHARE = 80
 
 
@@ -54,6 +54,11 @@ def tile_picked_modres_glusilu_p_kernel(
         nc.gpsimd.memset(x_scale_table[:].bitcast(I32), 0)
         w2_scale = mx_tile([P, N], U8, "w2_scale")
         nc.gpsimd.memset(w2_scale[:].bitcast(I32), 0)
+        for q in range(QUADRANTS):
+            nc.gpsimd.dma_start(
+                w2_scale[32 * q : 32 * q + SCALE_ROWS, :].bitcast(I32),
+                w2_scales[0, SCALE_ROWS * q : SCALE_ROWS * (q + 1), :].bitcast(I32),
+            )
 
         def load_words(tile, words):
             nc.sync.dma_start(tile[:].bitcast(I32), words.rearrange("p n t -> p (n t)").bitcast(I32))
@@ -81,16 +86,11 @@ def tile_picked_modres_glusilu_p_kernel(
         upper = keep.tile([P, T], F32, name="upper")
         lower = keep.tile([P, T], F32, name="lower")
         nc.sync.dma_start(lower[:], res[P:N, :])
-        gate_wide = keep.tile([P, S], F32, name="gate_wide")
-        nc.sync.dma_start(gate_wide[:], gate)
+        nc.sync.dma_start(upper[:], res[0:P, :])
         w2_codes = mx_tile([P, N], U32, "w2_codes")
         load_words(w2_codes, w2_words[0])
-        for q in range(QUADRANTS):
-            nc.sync.dma_start(
-                w2_scale[32 * q : 32 * q + SCALE_ROWS, :].bitcast(I32),
-                w2_scales[0, SCALE_ROWS * q : SCALE_ROWS * (q + 1), :].bitcast(I32),
-            )
-        nc.sync.dma_start(upper[:], res[0:P, :])
+        gate_wide = keep.tile([P, S], F32, name="gate_wide")
+        nc.sync.dma_start(gate_wide[:], gate)
 
         x_codes = [mx_tile([P, S], U32, "x_codes%d" % g) for g in range(PASSES)]
         x_scale = mx_tile([P, S], U8, "x_scale")
@@ -170,10 +170,10 @@ def tile_picked_modres_glusilu_p_kernel(
         nc.vector.tensor_copy(lower_picked[:, :VECTOR_PICKS], lower[:].indirect(entries_of(0, VECTOR_PICKS)))
         nc.scalar.activation(lower_picked[:, VECTOR_PICKS:], lower[:].indirect(entries_of(VECTOR_PICKS, S)), COPY)
         product3 = product_for_gpsimd(3, GPSIMD_SHARE)
-        upper_second = mx_tile([P, half], F32, "upper_second", "w3_1_scale")
-        nc.scalar.activation(upper_second[:], upper[:].indirect(entries_of(half, S)), COPY)
         upper_first = mx_tile([P, half], F32, "upper_first", "w3_1_codes")
         nc.scalar.activation(upper_first[:], upper[:].indirect(entries_of(0, half)), COPY)
+        upper_second = mx_tile([P, half], F32, "upper_second", "w3_1_scale")
+        nc.scalar.activation(upper_second[:], upper[:].indirect(entries_of(half, S)), COPY)
 
         upper_new = keep.tile([P, S], F32, name="upper_new")
 
@@ -190,18 +190,20 @@ def tile_picked_modres_glusilu_p_kernel(
                 )
             return codes, scale
 
-        def second_product(rows, quantised, tag):
+        def second_product(rows, quantised, tag, parts=1):
             codes, scale = quantised
             y = bank(tag, [P, half], "y_" + tag)
-            nc.tensor.matmul_mx(
-                out=y[:],
-                lhsT=w2_codes[:, rows].bitcast(FP8X4),
-                lhsT_scale=w2_scale[:, rows],
-                rhs=codes[:].bitcast(FP8X4),
-                rhs_scale=scale[:],
-                start=True,
-                stop=True,
-            )
+            for lo in range(0, half, half // parts):
+                part = slice(lo, lo + half // parts)
+                nc.tensor.matmul_mx(
+                    out=y[:, part],
+                    lhsT=w2_codes[:, rows].bitcast(FP8X4),
+                    lhsT_scale=w2_scale[:, rows],
+                    rhs=codes[:, part].bitcast(FP8X4),
+                    rhs_scale=scale[:, part],
+                    start=True,
+                    stop=True,
+                )
             return y
 
         def times_gate(gated, y, entries):
@@ -218,23 +220,23 @@ def tile_picked_modres_glusilu_p_kernel(
         make_h(h01[:, :CHUNK], 0)
         make_h(h01[:, CHUNK:], 1)
         quantised = quantise_h(h01, 0, 2)
-        upper_y = second_product(upper_rows, quantised, "w1_0")
+        upper_y = second_product(upper_rows, quantised, "w1_0", 2)
         lower_y = second_product(lower_rows, quantised, "w1_1")
         h23 = mx_tile([P, half, PACK], BF16, "h23", "h")
         split = CHUNK + GPSIMD_SHARE
         nc.gpsimd.tensor_tensor(h23[:, CHUNK:split], product3[:], silu[3][:, :GPSIMD_SHARE], MULT)
         make_h(h23[:, :CHUNK], 2)
+        upper_gated = mx_tile([P, half], F32, "upper_gated0")
+        times_gate(upper_gated[:], upper_y, first)
         rest = w3_acc[3][:, :, GPSIMD_SHARE:].rearrange("p t n -> p n t")
         nc.vector.tensor_tensor(h23[:, split:], rest, silu[3][:, GPSIMD_SHARE:], MULT)
-        upper_gated = mx_tile([P, half], F32, "upper_gated0", "upper_gated")
-        times_gate(upper_gated[:], upper_y, first)
-        quantised = quantise_h(h23, 1, 1)
         put_upper(first, upper_gated, upper_first)
-        lower_gated = mx_tile([P, S], F32, "lower_gated", "w3_1_codes")
+        quantised = quantise_h(h23, 1, 1)
+        lower_gated = mx_tile([P, S], F32, "lower_gated", "h")
         times_gate(lower_gated[:, first], lower_y, first)
         upper_y = second_product(upper_rows, quantised, "w1_2")
         lower_y = second_product(lower_rows, quantised, "w1_3")
-        upper_gated = mx_tile([P, half], F32, "upper_gated1", "upper_gated")
+        upper_gated = mx_tile([P, half], F32, "upper_gated1")
         times_gate(upper_gated[:], upper_y, second)
         times_gate(lower_gated[:, second], lower_y, second)
         put_upper(second, upper_gated, upper_second)

@@ -27,7 +27,7 @@ CHUNKS = S // CHUNK
 MX_ALIGN = 64
 SCALAR_SHARE = 44
 PRODUCT_ORDER = (0, 1, 3, 2)
-VECTOR_PICKS = 224
+VECTOR_PICKS = 160
 GPSIMD_SHARE = 80
 
 
@@ -54,14 +54,15 @@ def tile_picked_modres_glusilu_p_kernel(
         nc.gpsimd.memset(x_scale_table[:].bitcast(I32), 0)
         w2_scale = mx_tile([P, N], U8, "w2_scale")
         nc.gpsimd.memset(w2_scale[:].bitcast(I32), 0)
-        for q in range(QUADRANTS):
-            nc.gpsimd.dma_start(
-                w2_scale[32 * q : 32 * q + SCALE_ROWS, :].bitcast(I32),
-                w2_scales[0, SCALE_ROWS * q : SCALE_ROWS * (q + 1), :].bitcast(I32),
-            )
 
         def load_words(tile, words):
             nc.sync.dma_start(tile[:].bitcast(I32), words.rearrange("p n t -> p (n t)").bitcast(I32))
+
+        def load_w2_scale_rows(q):
+            nc.sync.dma_start(
+                w2_scale[32 * q : 32 * q + SCALE_ROWS, :].bitcast(I32),
+                w2_scales[0, SCALE_ROWS * q : SCALE_ROWS * (q + 1), :].bitcast(I32),
+            )
 
         def load_weight(w, g, name):
             raw = mx_tile([P, PACK, H], F32, name)
@@ -85,12 +86,15 @@ def tile_picked_modres_glusilu_p_kernel(
 
         upper = keep.tile([P, T], F32, name="upper")
         lower = keep.tile([P, T], F32, name="lower")
-        nc.sync.dma_start(lower[:], res[P:N, :])
         nc.sync.dma_start(upper[:], res[0:P, :])
+        nc.sync.dma_start(lower[:], res[P:N, :])
+        gates = [keep.tile([P, S // 2], F32, name="gate%d" % pair) for pair in range(2)]
+        nc.sync.dma_start(gates[0][:], gate[:, : S // 2])
         w2_codes = mx_tile([P, N], U32, "w2_codes")
         load_words(w2_codes, w2_words[0])
-        gate_wide = keep.tile([P, S], F32, name="gate_wide")
-        nc.sync.dma_start(gate_wide[:], gate)
+        for q in range(QUADRANTS):
+            load_w2_scale_rows(q)
+        nc.sync.dma_start(gates[1][:], gate[:, S // 2 :])
 
         x_codes = [mx_tile([P, S], U32, "x_codes%d" % g) for g in range(PASSES)]
         x_scale = mx_tile([P, S], U8, "x_scale")
@@ -166,29 +170,28 @@ def tile_picked_modres_glusilu_p_kernel(
             return product
 
         half = S // 2
-        lower_picked = mx_tile([P, S], F32, "lower_picked", "staging0")
-        nc.vector.tensor_copy(lower_picked[:, :VECTOR_PICKS], lower[:].indirect(entries_of(0, VECTOR_PICKS)))
-        nc.scalar.activation(lower_picked[:, VECTOR_PICKS:], lower[:].indirect(entries_of(VECTOR_PICKS, S)), COPY)
+        upper_first = mx_tile([P, half], F32, "upper_first", "staging0")
+        nc.vector.tensor_copy(upper_first[:, :VECTOR_PICKS], upper[:].indirect(entries_of(0, VECTOR_PICKS)))
+        nc.scalar.activation(upper_first[:, VECTOR_PICKS:], upper[:].indirect(entries_of(VECTOR_PICKS, half)), COPY)
         product3 = product_for_gpsimd(3, GPSIMD_SHARE)
-        upper_first = mx_tile([P, half], F32, "upper_first", "w3_1_codes")
-        nc.scalar.activation(upper_first[:], upper[:].indirect(entries_of(0, half)), COPY)
         upper_second = mx_tile([P, half], F32, "upper_second", "w3_1_scale")
         nc.scalar.activation(upper_second[:], upper[:].indirect(entries_of(half, S)), COPY)
+        lower_picked = mx_tile([P, S], F32, "lower_picked", "w3_1_codes")
+        nc.scalar.activation(lower_picked[:], lower[:].indirect(offsets[:]), COPY)
 
         upper_new = keep.tile([P, S], F32, name="upper_new")
 
         def make_h(dst, c):
             nc.vector.tensor_tensor(words_by_pairs(dst), by_pairs(w3_acc[c]), silu[c][:], MULT)
 
-        def quantise_h(h, pair, parts):
-            codes = mx_tile([P, half], U32, "h_codes%d" % pair, "h_codes")
-            scale = mx_tile([P, half], U8, "h_scale%d" % pair)
-            for lo in range(0, half, half // parts):
-                part = slice(lo, lo + half // parts)
-                nc.vector.quantize_mx(
-                    out=codes[:, part].bitcast(FP8X4), scales=scale[:, part], in_=h[:, part].rearrange("p n t -> p (n t)")
-                )
-            return codes, scale
+        def packed_pair(pair):
+            return mx_tile([P, half], U32, "h_codes%d" % pair, "h_codes"), mx_tile([P, half], U8, "h_scale%d" % pair)
+
+        def quantise_h(h, quantised, part):
+            codes, scale = quantised
+            nc.vector.quantize_mx(
+                out=codes[:, part].bitcast(FP8X4), scales=scale[:, part], in_=h[:, part].rearrange("p n t -> p (n t)")
+            )
 
         def second_product(rows, quantised, tag, parts=1):
             codes, scale = quantised
@@ -207,7 +210,7 @@ def tile_picked_modres_glusilu_p_kernel(
             return y
 
         def times_gate(gated, y, entries):
-            nc.vector.tensor_tensor(gated, y[:], gate_wide[:, entries], MULT)
+            nc.vector.tensor_tensor(gated, y[:], gates[entries.start // half][:], MULT)
 
         def put_upper(entries, gated, picked):
             nc.vector.tensor_tensor(upper_new[:, entries], gated[:], picked[:], ADD)
@@ -219,7 +222,10 @@ def tile_picked_modres_glusilu_p_kernel(
         h01 = mx_tile([P, half, PACK], BF16, "h01", "h")
         make_h(h01[:, :CHUNK], 0)
         make_h(h01[:, CHUNK:], 1)
-        quantised = quantise_h(h01, 0, 2)
+        front, back = slice(0, CHUNK), slice(CHUNK, half)
+        quantised = packed_pair(0)
+        quantise_h(h01, quantised, front)
+        quantise_h(h01, quantised, back)
         upper_y = second_product(upper_rows, quantised, "w1_0", 2)
         lower_y = second_product(lower_rows, quantised, "w1_1")
         h23 = mx_tile([P, half, PACK], BF16, "h23", "h")
@@ -230,11 +236,13 @@ def tile_picked_modres_glusilu_p_kernel(
         times_gate(upper_gated[:], upper_y, first)
         rest = w3_acc[3][:, :, GPSIMD_SHARE:].rearrange("p t n -> p n t")
         nc.vector.tensor_tensor(h23[:, split:], rest, silu[3][:, GPSIMD_SHARE:], MULT)
+        quantised = packed_pair(1)
+        quantise_h(h23, quantised, front)
         put_upper(first, upper_gated, upper_first)
-        quantised = quantise_h(h23, 1, 1)
+        quantise_h(h23, quantised, back)
         lower_gated = mx_tile([P, S], F32, "lower_gated", "h")
         times_gate(lower_gated[:, first], lower_y, first)
-        upper_y = second_product(upper_rows, quantised, "w1_2")
+        upper_y = second_product(upper_rows, quantised, "w1_2", 2)
         lower_y = second_product(lower_rows, quantised, "w1_3")
         upper_gated = mx_tile([P, half], F32, "upper_gated1")
         times_gate(upper_gated[:], upper_y, second)

@@ -170,12 +170,10 @@ def tile_picked_modres_glusilu_p_kernel(
             return product
 
         half = S // 2
-        upper_first = mx_tile([P, half], F32, "upper_first", "staging0")
-        nc.vector.tensor_copy(upper_first[:, :VECTOR_PICKS], upper[:].indirect(entries_of(0, VECTOR_PICKS)))
-        nc.scalar.activation(upper_first[:, VECTOR_PICKS:], upper[:].indirect(entries_of(VECTOR_PICKS, half)), COPY)
+        upper_picked = mx_tile([P, S], F32, "upper_picked", "staging0")
+        nc.vector.tensor_copy(upper_picked[:, :VECTOR_PICKS], upper[:].indirect(entries_of(0, VECTOR_PICKS)))
+        nc.scalar.activation(upper_picked[:, VECTOR_PICKS:], upper[:].indirect(entries_of(VECTOR_PICKS, S)), COPY)
         product3 = product_for_gpsimd(3, GPSIMD_SHARE)
-        upper_second = mx_tile([P, half], F32, "upper_second", "w3_1_scale")
-        nc.scalar.activation(upper_second[:], upper[:].indirect(entries_of(half, S)), COPY)
         lower_picked = mx_tile([P, S], F32, "lower_picked", "w3_1_codes")
         nc.scalar.activation(lower_picked[:], lower[:].indirect(offsets[:]), COPY)
 
@@ -212,8 +210,8 @@ def tile_picked_modres_glusilu_p_kernel(
         def times_gate(gated, y, entries):
             nc.vector.tensor_tensor(gated, y[:], gates[entries.start // half][:], MULT)
 
-        def put_upper(entries, gated, picked):
-            nc.vector.tensor_tensor(upper_new[:, entries], gated[:], picked[:], ADD)
+        def put_upper(entries):
+            nc.vector.tensor_tensor(upper_new[:, entries], upper_gated[:, entries], upper_picked[:, entries], ADD)
             nc.scalar.activation(upper[:].indirect(entries_of(entries.start, entries.stop)), upper_new[:, entries], COPY)
 
 
@@ -232,22 +230,21 @@ def tile_picked_modres_glusilu_p_kernel(
         split = CHUNK + GPSIMD_SHARE
         nc.gpsimd.tensor_tensor(h23[:, CHUNK:split], product3[:], silu[3][:, :GPSIMD_SHARE], MULT)
         make_h(h23[:, :CHUNK], 2)
-        upper_gated = mx_tile([P, half], F32, "upper_gated0")
-        times_gate(upper_gated[:], upper_y, first)
+        upper_gated = keep.tile([P, S], F32, name="upper_gated")
+        times_gate(upper_gated[:, first], upper_y, first)
         rest = w3_acc[3][:, :, GPSIMD_SHARE:].rearrange("p t n -> p n t")
         nc.vector.tensor_tensor(h23[:, split:], rest, silu[3][:, GPSIMD_SHARE:], MULT)
         quantised = packed_pair(1)
         quantise_h(h23, quantised, front)
-        put_upper(first, upper_gated, upper_first)
+        put_upper(first)
         quantise_h(h23, quantised, back)
         lower_gated = mx_tile([P, S], F32, "lower_gated", "h")
         times_gate(lower_gated[:, first], lower_y, first)
         upper_y = second_product(upper_rows, quantised, "w1_2", 2)
         lower_y = second_product(lower_rows, quantised, "w1_3")
-        upper_gated = mx_tile([P, half], F32, "upper_gated1")
-        times_gate(upper_gated[:], upper_y, second)
+        times_gate(upper_gated[:, second], upper_y, second)
         times_gate(lower_gated[:, second], lower_y, second)
-        put_upper(second, upper_gated, upper_second)
+        put_upper(second)
         nc.sync.dma_start(out[upper_rows, :], upper[:])
         nc.vector.tensor_tensor(lower[:].indirect(offsets[:]), lower_gated[:], lower_picked[:], ADD)
         nc.sync.dma_start(out[lower_rows, :], lower[:])

@@ -21,14 +21,19 @@ P = 128
 PACK = 4
 QUADRANTS = 4
 SCALE_ROWS = 4
+LIST_ROWS = 16
 PASSES = K // (P * PACK)
 CHUNK = 128
 CHUNKS = S // CHUNK
+PAIR = 2 * CHUNK
 MX_ALIGN = 64
+
 SCALAR_SHARE = 44
-PRODUCT_ORDER = (0, 1, 3, 2)
-VECTOR_PICKS = 160
+
+GPSIMD_CHUNK = 3
 GPSIMD_SHARE = 80
+
+PRODUCT_ORDER = (0, 1, GPSIMD_CHUNK, 2)
 
 
 def tile_picked_modres_glusilu_p_kernel(
@@ -45,10 +50,10 @@ def tile_picked_modres_glusilu_p_kernel(
         def bank(tag, shape, name):
             return psum.tile(shape, F32, name=name, tag=tag)
 
-        offsets = keep.tile([P, S // 16], U16, name="offsets")
+        offsets = keep.tile([P, S // LIST_ROWS], U16, name="offsets")
 
-        def entries_of(lo, hi):
-            return offsets[:, lo // 16 : hi // 16]
+        def offsets_of(entries):
+            return offsets[:, entries.start // LIST_ROWS : entries.stop // LIST_ROWS]
 
         x_scale_table = mx_tile([P, T], U8, "x_scale_table")
         nc.gpsimd.memset(x_scale_table[:].bitcast(I32), 0)
@@ -57,12 +62,6 @@ def tile_picked_modres_glusilu_p_kernel(
 
         def load_words(tile, words):
             nc.sync.dma_start(tile[:].bitcast(I32), words.rearrange("p n t -> p (n t)").bitcast(I32))
-
-        def load_w2_scale_rows(q):
-            nc.sync.dma_start(
-                w2_scale[32 * q : 32 * q + SCALE_ROWS, :].bitcast(I32),
-                w2_scales[0, SCALE_ROWS * q : SCALE_ROWS * (q + 1), :].bitcast(I32),
-            )
 
         def load_weight(w, g, name):
             raw = mx_tile([P, PACK, H], F32, name)
@@ -84,17 +83,22 @@ def tile_picked_modres_glusilu_p_kernel(
         w3_raw0 = load_weight(w3, 0, "w3_raw0")
         w3_raw1 = load_weight(w3, 1, "w3_raw1")
 
+        upper_rows, lower_rows = slice(0, P), slice(P, N)
         upper = keep.tile([P, T], F32, name="upper")
         lower = keep.tile([P, T], F32, name="lower")
-        nc.sync.dma_start(upper[:], res[0:P, :])
-        nc.sync.dma_start(lower[:], res[P:N, :])
-        gates = [keep.tile([P, S // 2], F32, name="gate%d" % pair) for pair in range(2)]
-        nc.sync.dma_start(gates[0][:], gate[:, : S // 2])
+        nc.sync.dma_start(upper[:], res[upper_rows, :])
+        nc.sync.dma_start(lower[:], res[lower_rows, :])
+        first, second = slice(0, PAIR), slice(PAIR, S)
+        gates = [keep.tile([P, PAIR], F32, name="gate%d" % pair) for pair in range(2)]
+        nc.sync.dma_start(gates[0][:], gate[:, first])
         w2_codes = mx_tile([P, N], U32, "w2_codes")
         load_words(w2_codes, w2_words[0])
         for q in range(QUADRANTS):
-            load_w2_scale_rows(q)
-        nc.sync.dma_start(gates[1][:], gate[:, S // 2 :])
+            nc.sync.dma_start(
+                w2_scale[32 * q : 32 * q + SCALE_ROWS, :].bitcast(I32),
+                w2_scales[0, SCALE_ROWS * q : SCALE_ROWS * (q + 1), :].bitcast(I32),
+            )
+        nc.sync.dma_start(gates[1][:], gate[:, second])
 
         x_codes = [mx_tile([P, S], U32, "x_codes%d" % g) for g in range(PASSES)]
         x_scale = mx_tile([P, S], U8, "x_scale")
@@ -107,10 +111,10 @@ def tile_picked_modres_glusilu_p_kernel(
             for u in range(2):
                 staged.append(mx_tile([P, 2, P, PACK], BF16, "%s_staged%d" % (name, u), "staging%d" % u))
                 dst = staged[u][:].rearrange("p t m j -> p m j t")
-                pair = slice(2 * u, 2 * u + 2)
+                ts = slice(2 * u, 2 * u + 2)
                 if scalar_share > 0:
-                    nc.scalar.copy(dst[:, :scalar_share], src[:, :scalar_share, :, pair])
-                nc.vector.tensor_copy(dst[:, scalar_share:], src[:, scalar_share:, :, pair])
+                    nc.scalar.copy(dst[:, :scalar_share], src[:, :scalar_share, :, ts])
+                nc.vector.tensor_copy(dst[:, scalar_share:], src[:, scalar_share:, :, ts])
             codes = mx_tile([P, H], U32, name + "_codes")
             scale = mx_tile([P, H], U8, name + "_scale")
             for u in range(2):
@@ -128,9 +132,9 @@ def tile_picked_modres_glusilu_p_kernel(
                 codes, scale = passes[g]
                 for c in PRODUCT_ORDER:
                     entries = slice(c * CHUNK, (c + 1) * CHUNK)
-                    late = c in PRODUCT_ORDER[2:]
+                    first_t = 0 if entries.start < PAIR else PACK // 2
                     for step in range(PACK):
-                        t = (step + 2) % PACK if late else step
+                        t = (first_t + step) % PACK
                         cols = slice(t * P, (t + 1) * P)
                         nc.tensor.matmul_mx(
                             out=accs[c][:, t, :],
@@ -151,51 +155,45 @@ def tile_picked_modres_glusilu_p_kernel(
         w3_pass1 = quantise_weight(w3_raw1, SCALAR_SHARE, "w3_1")
         w3_acc = first_product((w3_pass0, w3_pass1), "w3")
 
-        def by_pairs(acc):
+        def by_twos(acc):
             return acc[:].rearrange("p t (n e) -> p n t e", e=2)
 
-        def words_by_pairs(tile):
+        def words_by_twos(tile):
             return tile.rearrange("p (n e) t -> p n t e", e=2)
 
         silu = {}
         for c in PRODUCT_ORDER:
-            shared = c == 3
+            shared = c == GPSIMD_CHUNK
             shape = [P, CHUNK, PACK] if shared else [P, CHUNK // 2, PACK, 2]
             silu[c] = mx_tile(shape, F32, "silu%d" % c, "w3_raw1" if c == PRODUCT_ORDER[-1] else None)
-            nc.scalar.activation(words_by_pairs(silu[c][:]) if shared else silu[c][:], by_pairs(w1_acc[c]), SILU)
+            nc.scalar.activation(words_by_twos(silu[c][:]) if shared else silu[c][:], by_twos(w1_acc[c]), SILU)
 
-        def product_for_gpsimd(c, count):
-            product = mx_tile([P, count, PACK], F32, "product%d" % c)
-            nc.scalar.copy(words_by_pairs(product[:]), by_pairs(w3_acc[c])[:, : count // 2])
-            return product
-
-        half = S // 2
         upper_picked = mx_tile([P, S], F32, "upper_picked", "staging0")
-        nc.vector.tensor_copy(upper_picked[:, :VECTOR_PICKS], upper[:].indirect(entries_of(0, VECTOR_PICKS)))
-        nc.scalar.activation(upper_picked[:, VECTOR_PICKS:], upper[:].indirect(entries_of(VECTOR_PICKS, S)), COPY)
-        product3 = product_for_gpsimd(3, GPSIMD_SHARE)
+        nc.scalar.activation(upper_picked[:], upper[:].indirect(offsets[:]), COPY)
+        gpsimd_product = mx_tile([P, GPSIMD_SHARE, PACK], F32, "gpsimd_product")
+        nc.scalar.copy(words_by_twos(gpsimd_product[:]), by_twos(w3_acc[GPSIMD_CHUNK])[:, : GPSIMD_SHARE // 2])
         lower_picked = mx_tile([P, S], F32, "lower_picked", "w3_1_codes")
         nc.scalar.activation(lower_picked[:], lower[:].indirect(offsets[:]), COPY)
 
         upper_new = keep.tile([P, S], F32, name="upper_new")
+        front, back = slice(0, CHUNK), slice(CHUNK, PAIR)
 
         def make_h(dst, c):
-            nc.vector.tensor_tensor(words_by_pairs(dst), by_pairs(w3_acc[c]), silu[c][:], MULT)
+            nc.vector.tensor_tensor(words_by_twos(dst), by_twos(w3_acc[c]), silu[c][:], MULT)
 
-        def packed_pair(pair):
-            return mx_tile([P, half], U32, "h_codes%d" % pair, "h_codes"), mx_tile([P, half], U8, "h_scale%d" % pair)
+        def packed_h(pair):
+            return mx_tile([P, PAIR], U32, "h_codes%d" % pair, "h_codes"), mx_tile([P, PAIR], U8, "h_scale%d" % pair)
 
-        def quantise_h(h, quantised, part):
-            codes, scale = quantised
+        def quantise_h(h, packed, part):
+            codes, scale = packed
             nc.vector.quantize_mx(
                 out=codes[:, part].bitcast(FP8X4), scales=scale[:, part], in_=h[:, part].rearrange("p n t -> p (n t)")
             )
 
-        def second_product(rows, quantised, tag, parts=1):
-            codes, scale = quantised
-            y = bank(tag, [P, half], "y_" + tag)
-            for lo in range(0, half, half // parts):
-                part = slice(lo, lo + half // parts)
+        def second_product(rows, packed, tag, parts):
+            codes, scale = packed
+            y = bank(tag, [P, PAIR], "y_" + tag)
+            for part in parts:
                 nc.tensor.matmul_mx(
                     out=y[:, part],
                     lhsT=w2_codes[:, rows].bitcast(FP8X4),
@@ -207,44 +205,45 @@ def tile_picked_modres_glusilu_p_kernel(
                 )
             return y
 
+        def both_products(packed, upper_tag, lower_tag):
+            upper_y = second_product(upper_rows, packed, upper_tag, (front, back))
+            lower_y = second_product(lower_rows, packed, lower_tag, (slice(0, PAIR),))
+            return upper_y, lower_y
+
         def times_gate(gated, y, entries):
-            nc.vector.tensor_tensor(gated, y[:], gates[entries.start // half][:], MULT)
+            nc.vector.tensor_tensor(gated[:, entries], y[:], gates[entries.start // PAIR][:], MULT)
 
-        def put_upper(entries):
-            nc.vector.tensor_tensor(upper_new[:, entries], upper_gated[:, entries], upper_picked[:, entries], ADD)
-            nc.scalar.activation(upper[:].indirect(entries_of(entries.start, entries.stop)), upper_new[:, entries], COPY)
+        def put_upper(gated, entries):
+            nc.vector.tensor_tensor(upper_new[:, entries], gated[:, entries], upper_picked[:, entries], ADD)
+            nc.scalar.activation(upper[:].indirect(offsets_of(entries)), upper_new[:, entries], COPY)
 
+        h01 = mx_tile([P, PAIR, PACK], BF16, "h01", "h")
+        make_h(h01[:, front], 0)
+        make_h(h01[:, back], 1)
+        packed = packed_h(0)
+        quantise_h(h01, packed, front)
+        quantise_h(h01, packed, back)
+        upper_y, lower_y = both_products(packed, "w1_0", "w1_1")
 
-        upper_rows, lower_rows = slice(0, P), slice(P, N)
-        first, second = slice(0, half), slice(half, S)
-        h01 = mx_tile([P, half, PACK], BF16, "h01", "h")
-        make_h(h01[:, :CHUNK], 0)
-        make_h(h01[:, CHUNK:], 1)
-        front, back = slice(0, CHUNK), slice(CHUNK, half)
-        quantised = packed_pair(0)
-        quantise_h(h01, quantised, front)
-        quantise_h(h01, quantised, back)
-        upper_y = second_product(upper_rows, quantised, "w1_0", 2)
-        lower_y = second_product(lower_rows, quantised, "w1_1")
-        h23 = mx_tile([P, half, PACK], BF16, "h23", "h")
+        h23 = mx_tile([P, PAIR, PACK], BF16, "h23", "h")
         split = CHUNK + GPSIMD_SHARE
-        nc.gpsimd.tensor_tensor(h23[:, CHUNK:split], product3[:], silu[3][:, :GPSIMD_SHARE], MULT)
-        make_h(h23[:, :CHUNK], 2)
+        nc.gpsimd.tensor_tensor(h23[:, CHUNK:split], gpsimd_product[:], silu[GPSIMD_CHUNK][:, :GPSIMD_SHARE], MULT)
+        make_h(h23[:, front], 2)
         upper_gated = keep.tile([P, S], F32, name="upper_gated")
-        times_gate(upper_gated[:, first], upper_y, first)
-        rest = w3_acc[3][:, :, GPSIMD_SHARE:].rearrange("p t n -> p n t")
-        nc.vector.tensor_tensor(h23[:, split:], rest, silu[3][:, GPSIMD_SHARE:], MULT)
-        quantised = packed_pair(1)
-        quantise_h(h23, quantised, front)
-        put_upper(first)
-        quantise_h(h23, quantised, back)
+        times_gate(upper_gated, upper_y, first)
+        rest = w3_acc[GPSIMD_CHUNK][:, :, GPSIMD_SHARE:].rearrange("p t n -> p n t")
+        nc.vector.tensor_tensor(h23[:, split:], rest, silu[GPSIMD_CHUNK][:, GPSIMD_SHARE:], MULT)
+        packed = packed_h(1)
+        quantise_h(h23, packed, front)
+        put_upper(upper_gated, first)
+        quantise_h(h23, packed, back)
+
         lower_gated = mx_tile([P, S], F32, "lower_gated", "h")
-        times_gate(lower_gated[:, first], lower_y, first)
-        upper_y = second_product(upper_rows, quantised, "w1_2", 2)
-        lower_y = second_product(lower_rows, quantised, "w1_3")
-        times_gate(upper_gated[:, second], upper_y, second)
-        times_gate(lower_gated[:, second], lower_y, second)
-        put_upper(second)
+        times_gate(lower_gated, lower_y, first)
+        upper_y, lower_y = both_products(packed, "w1_2", "w1_3")
+        times_gate(upper_gated, upper_y, second)
+        times_gate(lower_gated, lower_y, second)
+        put_upper(upper_gated, second)
         nc.sync.dma_start(out[upper_rows, :], upper[:])
         nc.vector.tensor_tensor(lower[:].indirect(offsets[:]), lower_gated[:], lower_picked[:], ADD)
         nc.sync.dma_start(out[lower_rows, :], lower[:])

@@ -79,6 +79,11 @@ def tile_picked_modres_glusilu_p_kernel(
             )
         w1_raw0 = load_weight(w1, 0, "w1_raw0")
         load_words(x_table[1], x_words[1])
+        for q in range(QUADRANTS):
+            nc.sync.dma_start(
+                w2_scale[32 * q : 32 * q + SCALE_ROWS, :].bitcast(I32),
+                w2_scales[0, SCALE_ROWS * q : SCALE_ROWS * (q + 1), :].bitcast(I32),
+            )
         w1_raw1 = load_weight(w1, 1, "w1_raw1")
         w3_raw0 = load_weight(w3, 0, "w3_raw0")
         w3_raw1 = load_weight(w3, 1, "w3_raw1")
@@ -87,17 +92,12 @@ def tile_picked_modres_glusilu_p_kernel(
         upper = keep.tile([P, T], F32, name="upper")
         lower = keep.tile([P, T], F32, name="lower")
         nc.sync.dma_start(upper[:], res[upper_rows, :])
-        nc.sync.dma_start(lower[:], res[lower_rows, :])
         first, second = slice(0, PAIR), slice(PAIR, S)
         gates = [keep.tile([P, PAIR], F32, name="gate%d" % pair) for pair in range(2)]
-        nc.sync.dma_start(gates[0][:], gate[:, first])
         w2_codes = mx_tile([P, N], U32, "w2_codes")
         load_words(w2_codes, w2_words[0])
-        for q in range(QUADRANTS):
-            nc.sync.dma_start(
-                w2_scale[32 * q : 32 * q + SCALE_ROWS, :].bitcast(I32),
-                w2_scales[0, SCALE_ROWS * q : SCALE_ROWS * (q + 1), :].bitcast(I32),
-            )
+        nc.sync.dma_start(gates[0][:], gate[:, first])
+        nc.sync.dma_start(lower[:], res[lower_rows, :])
         nc.sync.dma_start(gates[1][:], gate[:, second])
 
         x_codes = [mx_tile([P, S], U32, "x_codes%d" % g) for g in range(PASSES)]
@@ -169,80 +169,82 @@ def tile_picked_modres_glusilu_p_kernel(
             nc.scalar.activation(words_by_twos(silu[c][:]) if shared else silu[c][:], by_twos(w1_acc[c]), SILU)
 
         upper_picked = mx_tile([P, S], F32, "upper_picked", "staging0")
-        nc.scalar.activation(upper_picked[:], upper[:].indirect(offsets[:]), COPY)
+        nc.scalar.activation(upper_picked[:, first], upper[:].indirect(offsets_of(first)), COPY)
         gpsimd_product = mx_tile([P, GPSIMD_SHARE, PACK], F32, "gpsimd_product")
         nc.scalar.copy(words_by_twos(gpsimd_product[:]), by_twos(w3_acc[GPSIMD_CHUNK])[:, : GPSIMD_SHARE // 2])
+        nc.scalar.activation(upper_picked[:, second], upper[:].indirect(offsets_of(second)), COPY)
         lower_picked = mx_tile([P, S], F32, "lower_picked", "w3_1_codes")
         nc.scalar.activation(lower_picked[:], lower[:].indirect(offsets[:]), COPY)
 
         upper_new = keep.tile([P, S], F32, name="upper_new")
         front, back = slice(0, CHUNK), slice(CHUNK, PAIR)
+        whole = slice(0, PAIR)
 
         def make_h(dst, c):
             nc.vector.tensor_tensor(words_by_twos(dst), by_twos(w3_acc[c]), silu[c][:], MULT)
 
         def packed_h(pair):
-            return mx_tile([P, PAIR], U32, "h_codes%d" % pair, "h_codes"), mx_tile([P, PAIR], U8, "h_scale%d" % pair)
+            return mx_tile([P, PAIR], U32, "h_codes%d" % pair), mx_tile([P, PAIR], U8, "h_scale%d" % pair)
 
         def quantise_h(h, packed, part):
             codes, scale = packed
             nc.vector.quantize_mx(
-                out=codes[:, part].bitcast(FP8X4), scales=scale[:, part], in_=h[:, part].rearrange("p n t -> p (n t)")
+                out=codes[:, part].bitcast(FP8X4), scales=scale[:, part], in_=h.rearrange("p n t -> p (n t)")
             )
 
-        def second_product(rows, packed, tag, parts):
+        def second_product(rows, packed, tag, part):
             codes, scale = packed
             y = bank(tag, [P, PAIR], "y_" + tag)
-            for part in parts:
-                nc.tensor.matmul_mx(
-                    out=y[:, part],
-                    lhsT=w2_codes[:, rows].bitcast(FP8X4),
-                    lhsT_scale=w2_scale[:, rows],
-                    rhs=codes[:, part].bitcast(FP8X4),
-                    rhs_scale=scale[:, part],
-                    start=True,
-                    stop=True,
-                )
+            nc.tensor.matmul_mx(
+                out=y[:, part],
+                lhsT=w2_codes[:, rows].bitcast(FP8X4),
+                lhsT_scale=w2_scale[:, rows],
+                rhs=codes[:, part].bitcast(FP8X4),
+                rhs_scale=scale[:, part],
+                start=True,
+                stop=True,
+            )
             return y
 
-        def both_products(packed, upper_tag, lower_tag):
-            upper_y = second_product(upper_rows, packed, upper_tag, (front, back))
-            lower_y = second_product(lower_rows, packed, lower_tag, (slice(0, PAIR),))
-            return upper_y, lower_y
-
         def times_gate(gated, y, entries):
-            nc.vector.tensor_tensor(gated[:, entries], y[:], gates[entries.start // PAIR][:], MULT)
+            pair = entries.start // PAIR
+            cols = slice(entries.start - pair * PAIR, entries.stop - pair * PAIR)
+            nc.vector.tensor_tensor(gated[:, entries], y[:, cols], gates[pair][:, cols], MULT)
 
         def put_upper(gated, entries):
             nc.vector.tensor_tensor(upper_new[:, entries], gated[:, entries], upper_picked[:, entries], ADD)
             nc.scalar.activation(upper[:].indirect(offsets_of(entries)), upper_new[:, entries], COPY)
 
-        h01 = mx_tile([P, PAIR, PACK], BF16, "h01", "h")
-        make_h(h01[:, front], 0)
-        make_h(h01[:, back], 1)
+        h0 = mx_tile([P, CHUNK, PACK], BF16, "h0", "h")
+        h1 = mx_tile([P, CHUNK, PACK], BF16, "h1")
         packed = packed_h(0)
-        quantise_h(h01, packed, front)
-        quantise_h(h01, packed, back)
-        upper_y, lower_y = both_products(packed, "w1_0", "w1_1")
+        make_h(h0[:], 0)
+        make_h(h1[:], 1)
+        quantise_h(h0[:], packed, front)
+        upper_y0 = second_product(upper_rows, packed, "w1_0", front)
+        quantise_h(h1[:], packed, back)
+        upper_y1 = second_product(upper_rows, packed, "w1_1", back)
+        lower_y01 = second_product(lower_rows, packed, "w1_2", whole)
 
         h23 = mx_tile([P, PAIR, PACK], BF16, "h23", "h")
         split = CHUNK + GPSIMD_SHARE
         nc.gpsimd.tensor_tensor(h23[:, CHUNK:split], gpsimd_product[:], silu[GPSIMD_CHUNK][:, :GPSIMD_SHARE], MULT)
         make_h(h23[:, front], 2)
         upper_gated = keep.tile([P, S], F32, name="upper_gated")
-        times_gate(upper_gated, upper_y, first)
+        times_gate(upper_gated, upper_y0, front)
         rest = w3_acc[GPSIMD_CHUNK][:, :, GPSIMD_SHARE:].rearrange("p t n -> p n t")
         nc.vector.tensor_tensor(h23[:, split:], rest, silu[GPSIMD_CHUNK][:, GPSIMD_SHARE:], MULT)
+        put_upper(upper_gated, front)
         packed = packed_h(1)
-        quantise_h(h23, packed, front)
-        put_upper(upper_gated, first)
-        quantise_h(h23, packed, back)
-
-        lower_gated = mx_tile([P, S], F32, "lower_gated", "h")
-        times_gate(lower_gated, lower_y, first)
-        upper_y, lower_y = both_products(packed, "w1_2", "w1_3")
-        times_gate(upper_gated, upper_y, second)
-        times_gate(lower_gated, lower_y, second)
+        quantise_h(h23[:], packed, whole)
+        upper_y23 = second_product(upper_rows, packed, "w1_3", whole)
+        lower_y23 = second_product(lower_rows, packed, "w3_0", whole)
+        times_gate(upper_gated, upper_y1, back)
+        lower_gated = keep.tile([P, S], F32, name="lower_gated")
+        times_gate(lower_gated, lower_y01, first)
+        put_upper(upper_gated, back)
+        times_gate(upper_gated, upper_y23, second)
+        times_gate(lower_gated, lower_y23, second)
         put_upper(upper_gated, second)
         nc.sync.dma_start(out[upper_rows, :], upper[:])
         nc.vector.tensor_tensor(lower[:].indirect(offsets[:]), lower_gated[:], lower_picked[:], ADD)

@@ -27,6 +27,7 @@ CHUNK = 128
 CHUNKS = S // CHUNK
 PAIR = 2 * CHUNK
 MX_ALIGN = 64
+DMA_ALIGN = 256
 
 SCALAR_SHARE = 44
 
@@ -44,8 +45,8 @@ def tile_picked_modres_glusilu_p_kernel(
         keep = ctx.enter_context(tc.tile_pool(name="keep", bufs=1))
         psum = ctx.enter_context(tc.psum_pool(name="psum", bufs=1))
 
-        def mx_tile(shape, dtype, name, tag=None):
-            return keep.tile(shape, dtype, name=name, tag=tag or name, align_bytes=MX_ALIGN)
+        def mx_tile(shape, dtype, name, tag=None, align=MX_ALIGN):
+            return keep.tile(shape, dtype, name=name, tag=tag or name, align_bytes=align)
 
         def bank(tag, shape, name):
             return psum.tile(shape, F32, name=name, tag=tag)
@@ -55,21 +56,21 @@ def tile_picked_modres_glusilu_p_kernel(
         def offsets_of(entries):
             return offsets[:, entries.start // LIST_ROWS : entries.stop // LIST_ROWS]
 
-        x_scale_table = mx_tile([P, T], U8, "x_scale_table")
+        x_scale_table = mx_tile([P, T], U8, "x_scale_table", align=DMA_ALIGN)
         nc.gpsimd.memset(x_scale_table[:].bitcast(I32), 0)
-        w2_scale = mx_tile([P, N], U8, "w2_scale")
+        w2_scale = mx_tile([P, N], U8, "w2_scale", align=DMA_ALIGN)
         nc.gpsimd.memset(w2_scale[:].bitcast(I32), 0)
 
         def load_words(tile, words):
             nc.sync.dma_start(tile[:].bitcast(I32), words.rearrange("p n t -> p (n t)").bitcast(I32))
 
         def load_weight(w, g, name):
-            raw = mx_tile([P, PACK, H], F32, name)
+            raw = mx_tile([P, PACK, H], F32, name, align=DMA_ALIGN)
             rows = w[g * P * PACK : (g + 1) * P * PACK, :]
             nc.sync.dma_start(raw[:], rows.rearrange("(p j) c -> p j c", j=PACK))
             return raw
 
-        x_table = [mx_tile([P, T], U32, "x_table%d" % g) for g in range(PASSES)]
+        x_table = [mx_tile([P, T], U32, "x_table%d" % g, align=DMA_ALIGN) for g in range(PASSES)]
         load_words(x_table[0], x_words[0])
         nc.sync.dma_start(offsets[:], offs)
         for q in range(QUADRANTS):
@@ -89,12 +90,12 @@ def tile_picked_modres_glusilu_p_kernel(
         w3_raw1 = load_weight(w3, 1, "w3_raw1")
 
         upper_rows, lower_rows = slice(0, P), slice(P, N)
-        upper = keep.tile([P, T], F32, name="upper")
-        lower = keep.tile([P, T], F32, name="lower")
+        upper = mx_tile([P, T], F32, "upper", align=DMA_ALIGN)
+        lower = mx_tile([P, T], F32, "lower", align=DMA_ALIGN)
         nc.sync.dma_start(upper[:], res[upper_rows, :])
         first, second = slice(0, PAIR), slice(PAIR, S)
-        gates = [keep.tile([P, PAIR], F32, name="gate%d" % pair) for pair in range(2)]
-        w2_codes = mx_tile([P, N], U32, "w2_codes")
+        gates = [mx_tile([P, PAIR], F32, "gate%d" % pair, align=DMA_ALIGN) for pair in range(2)]
+        w2_codes = mx_tile([P, N], U32, "w2_codes", align=DMA_ALIGN)
         load_words(w2_codes, w2_words[0])
         nc.sync.dma_start(gates[0][:], gate[:, first])
         nc.sync.dma_start(lower[:], res[lower_rows, :])
@@ -165,7 +166,7 @@ def tile_picked_modres_glusilu_p_kernel(
         for c in PRODUCT_ORDER:
             shared = c == GPSIMD_CHUNK
             shape = [P, CHUNK, PACK] if shared else [P, CHUNK // 2, PACK, 2]
-            silu[c] = mx_tile(shape, F32, "silu%d" % c, "w3_raw1" if c == PRODUCT_ORDER[-1] else None)
+            silu[c] = mx_tile(shape, F32, "silu%d" % c, "w3_raw1" if c == PRODUCT_ORDER[-1] else None, DMA_ALIGN)
             nc.scalar.activation(words_by_twos(silu[c][:]) if shared else silu[c][:], by_twos(w1_acc[c]), SILU)
 
         upper_picked = mx_tile([P, S], F32, "upper_picked", "staging0")

@@ -27,7 +27,7 @@ CHUNK = 128
 CHUNKS = S // CHUNK
 PAIR = 2 * CHUNK
 MX_ALIGN = 64
-DMA_ALIGN = 256
+DMA_ALIGN = 1024
 
 SCALAR_SHARE = 44
 

from contextlib import ExitStack

import concourse.mybir as mybir

K, T, S, H, N = 1024, 1024, 512, 512, 256
FLOPS = 2 * (2 * K * H * S + H * N * S)

F32 = mybir.dt.float32
BF16 = mybir.dt.bfloat16
I32 = mybir.dt.int32
U32 = mybir.dt.uint32
U16 = mybir.dt.uint16
U8 = mybir.dt.uint8
FP8X4 = mybir.dt.float8_e4m3fn_x4
ADD = mybir.AluOpType.add
MULT = mybir.AluOpType.mult
SILU = mybir.ActivationFunctionType.Silu
COPY = mybir.ActivationFunctionType.Copy

P = 128
PACK = 4
QUADRANTS = 4
SCALE_ROWS = 4
LIST_ROWS = 16
PASSES = K // (P * PACK)
CHUNK = 128
CHUNKS = S // CHUNK
PAIR = 2 * CHUNK
MX_ALIGN = 64
DMA_ALIGN = 1024

SCALAR_SHARE = 44

GPSIMD_CHUNK = 3
GPSIMD_SHARE = 80

PRODUCT_ORDER = (0, 1, GPSIMD_CHUNK, 2)


def tile_picked_modres_glusilu_p_kernel(
    tc, x_words, x_scales, gate, res, w1, w3, w2_words, w2_scales, offs, out
):
    nc = tc.nc
    with ExitStack() as ctx:
        keep = ctx.enter_context(tc.tile_pool(name="keep", bufs=1))
        psum = ctx.enter_context(tc.psum_pool(name="psum", bufs=1))

        def mx_tile(shape, dtype, name, tag=None, align=MX_ALIGN):
            return keep.tile(shape, dtype, name=name, tag=tag or name, align_bytes=align)

        def bank(tag, shape, name):
            return psum.tile(shape, F32, name=name, tag=tag)

        offsets = keep.tile([P, S // LIST_ROWS], U16, name="offsets")

        def offsets_of(entries):
            return offsets[:, entries.start // LIST_ROWS : entries.stop // LIST_ROWS]

        x_scale_table = mx_tile([P, T], U8, "x_scale_table", align=DMA_ALIGN)
        nc.gpsimd.memset(x_scale_table[:].bitcast(I32), 0)
        w2_scale = mx_tile([P, N], U8, "w2_scale", align=DMA_ALIGN)
        nc.gpsimd.memset(w2_scale[:].bitcast(I32), 0)

        def load_words(tile, words):
            nc.sync.dma_start(tile[:].bitcast(I32), words.rearrange("p n t -> p (n t)").bitcast(I32))

        def load_weight(w, g, name):
            raw = mx_tile([P, PACK, H], F32, name, align=DMA_ALIGN)
            rows = w[g * P * PACK : (g + 1) * P * PACK, :]
            nc.sync.dma_start(raw[:], rows.rearrange("(p j) c -> p j c", j=PACK))
            return raw

        x_table = [mx_tile([P, T], U32, "x_table%d" % g, align=DMA_ALIGN) for g in range(PASSES)]
        load_words(x_table[0], x_words[0])
        nc.sync.dma_start(offsets[:], offs)
        for q in range(QUADRANTS):
            nc.sync.dma_start(
                x_scale_table[32 * q : 32 * q + SCALE_ROWS * PASSES, :].bitcast(I32),
                x_scales[:, SCALE_ROWS * q : SCALE_ROWS * (q + 1), :].bitcast(I32),
            )
        w1_raw0 = load_weight(w1, 0, "w1_raw0")
        load_words(x_table[1], x_words[1])
        for q in range(QUADRANTS):
            nc.sync.dma_start(
                w2_scale[32 * q : 32 * q + SCALE_ROWS, :].bitcast(I32),
                w2_scales[0, SCALE_ROWS * q : SCALE_ROWS * (q + 1), :].bitcast(I32),
            )
        w1_raw1 = load_weight(w1, 1, "w1_raw1")
        w3_raw0 = load_weight(w3, 0, "w3_raw0")
        w3_raw1 = load_weight(w3, 1, "w3_raw1")

        upper_rows, lower_rows = slice(0, P), slice(P, N)
        upper = mx_tile([P, T], F32, "upper", align=DMA_ALIGN)
        lower = mx_tile([P, T], F32, "lower", align=DMA_ALIGN)
        nc.sync.dma_start(upper[:], res[upper_rows, :])
        first, second = slice(0, PAIR), slice(PAIR, S)
        gates = [mx_tile([P, PAIR], F32, "gate%d" % pair, align=DMA_ALIGN) for pair in range(2)]
        w2_codes = mx_tile([P, N], U32, "w2_codes", align=DMA_ALIGN)
        load_words(w2_codes, w2_words[0])
        nc.sync.dma_start(gates[0][:], gate[:, first])
        nc.sync.dma_start(lower[:], res[lower_rows, :])
        nc.sync.dma_start(gates[1][:], gate[:, second])

        x_codes = [mx_tile([P, S], U32, "x_codes%d" % g) for g in range(PASSES)]
        x_scale = mx_tile([P, S], U8, "x_scale")
        nc.vector.tensor_copy(x_codes[0][:], x_table[0][:].indirect(offsets[:]))
        nc.vector.tensor_copy(x_scale[:], x_scale_table[:].indirect(offsets[:]))

        def quantise_weight(raw, scalar_share, name):
            src = raw[:].rearrange("p j (m t) -> p m j t", t=PACK)
            staged = []
            for u in range(2):
                staged.append(mx_tile([P, 2, P, PACK], BF16, "%s_staged%d" % (name, u), "staging%d" % u))
                dst = staged[u][:].rearrange("p t m j -> p m j t")
                ts = slice(2 * u, 2 * u + 2)
                if scalar_share > 0:
                    nc.scalar.copy(dst[:, :scalar_share], src[:, :scalar_share, :, ts])
                nc.vector.tensor_copy(dst[:, scalar_share:], src[:, scalar_share:, :, ts])
            codes = mx_tile([P, H], U32, name + "_codes")
            scale = mx_tile([P, H], U8, name + "_scale")
            for u in range(2):
                cols = slice(u * H // 2, (u + 1) * H // 2)
                nc.vector.quantize_mx(
                    out=codes[:, cols].bitcast(FP8X4),
                    scales=scale[:, cols],
                    in_=staged[u][:].rearrange("p t m j -> p (t m j)"),
                )
            return codes, scale

        def first_product(passes, name):
            accs = [bank("%s_%d" % (name, c), [P, PACK, CHUNK], "%s_acc%d" % (name, c)) for c in range(CHUNKS)]
            for g in range(PASSES):
                codes, scale = passes[g]
                for c in PRODUCT_ORDER:
                    entries = slice(c * CHUNK, (c + 1) * CHUNK)
                    first_t = 0 if entries.start < PAIR else PACK // 2
                    for step in range(PACK):
                        t = (first_t + step) % PACK
                        cols = slice(t * P, (t + 1) * P)
                        nc.tensor.matmul_mx(
                            out=accs[c][:, t, :],
                            lhsT=codes[:, cols].bitcast(FP8X4),
                            lhsT_scale=scale[:, cols],
                            rhs=x_codes[g][:, entries].bitcast(FP8X4),
                            rhs_scale=x_scale[SCALE_ROWS * g : P, entries],
                            start=(g == 0 and step == 0),
                            stop=(g == PASSES - 1 and step == PACK - 1),
                        )
            return accs

        w1_pass0 = quantise_weight(w1_raw0, SCALAR_SHARE, "w1_0")
        nc.vector.tensor_copy(x_codes[1][:], x_table[1][:].indirect(offsets[:]))
        w1_pass1 = quantise_weight(w1_raw1, SCALAR_SHARE, "w1_1")
        w1_acc = first_product((w1_pass0, w1_pass1), "w1")
        w3_pass0 = quantise_weight(w3_raw0, 0, "w3_0")
        w3_pass1 = quantise_weight(w3_raw1, SCALAR_SHARE, "w3_1")
        w3_acc = first_product((w3_pass0, w3_pass1), "w3")

        def by_twos(acc):
            return acc[:].rearrange("p t (n e) -> p n t e", e=2)

        def words_by_twos(tile):
            return tile.rearrange("p (n e) t -> p n t e", e=2)

        silu = {}
        for c in PRODUCT_ORDER:
            shared = c == GPSIMD_CHUNK
            shape = [P, CHUNK, PACK] if shared else [P, CHUNK // 2, PACK, 2]
            silu[c] = mx_tile(shape, F32, "silu%d" % c, "w3_raw1" if c == PRODUCT_ORDER[-1] else None, DMA_ALIGN)
            nc.scalar.activation(words_by_twos(silu[c][:]) if shared else silu[c][:], by_twos(w1_acc[c]), SILU)

        upper_picked = mx_tile([P, S], F32, "upper_picked", "staging0")
        nc.scalar.activation(upper_picked[:, first], upper[:].indirect(offsets_of(first)), COPY)
        gpsimd_product = mx_tile([P, GPSIMD_SHARE, PACK], F32, "gpsimd_product")
        nc.scalar.copy(words_by_twos(gpsimd_product[:]), by_twos(w3_acc[GPSIMD_CHUNK])[:, : GPSIMD_SHARE // 2])
        nc.scalar.activation(upper_picked[:, second], upper[:].indirect(offsets_of(second)), COPY)
        lower_picked = mx_tile([P, S], F32, "lower_picked", "w3_1_codes")
        nc.scalar.activation(lower_picked[:], lower[:].indirect(offsets[:]), COPY)

        upper_new = keep.tile([P, S], F32, name="upper_new")
        front, back = slice(0, CHUNK), slice(CHUNK, PAIR)
        whole = slice(0, PAIR)

        def make_h(dst, c):
            nc.vector.tensor_tensor(words_by_twos(dst), by_twos(w3_acc[c]), silu[c][:], MULT)

        def packed_h(pair):
            return mx_tile([P, PAIR], U32, "h_codes%d" % pair), mx_tile([P, PAIR], U8, "h_scale%d" % pair)

        def quantise_h(h, packed, part):
            codes, scale = packed
            nc.vector.quantize_mx(
                out=codes[:, part].bitcast(FP8X4), scales=scale[:, part], in_=h.rearrange("p n t -> p (n t)")
            )

        def second_product(rows, packed, tag, part):
            codes, scale = packed
            y = bank(tag, [P, PAIR], "y_" + tag)
            nc.tensor.matmul_mx(
                out=y[:, part],
                lhsT=w2_codes[:, rows].bitcast(FP8X4),
                lhsT_scale=w2_scale[:, rows],
                rhs=codes[:, part].bitcast(FP8X4),
                rhs_scale=scale[:, part],
                start=True,
                stop=True,
            )
            return y

        def times_gate(gated, y, entries):
            pair = entries.start // PAIR
            cols = slice(entries.start - pair * PAIR, entries.stop - pair * PAIR)
            nc.vector.tensor_tensor(gated[:, entries], y[:, cols], gates[pair][:, cols], MULT)

        def put_upper(gated, entries):
            nc.vector.tensor_tensor(upper_new[:, entries], gated[:, entries], upper_picked[:, entries], ADD)
            nc.scalar.activation(upper[:].indirect(offsets_of(entries)), upper_new[:, entries], COPY)

        h0 = mx_tile([P, CHUNK, PACK], BF16, "h0", "h")
        h1 = mx_tile([P, CHUNK, PACK], BF16, "h1")
        packed = packed_h(0)
        make_h(h0[:], 0)
        make_h(h1[:], 1)
        quantise_h(h0[:], packed, front)
        upper_y0 = second_product(upper_rows, packed, "w1_0", front)
        quantise_h(h1[:], packed, back)
        upper_y1 = second_product(upper_rows, packed, "w1_1", back)
        lower_y01 = second_product(lower_rows, packed, "w1_2", whole)

        h23 = mx_tile([P, PAIR, PACK], BF16, "h23", "h")
        split = CHUNK + GPSIMD_SHARE
        nc.gpsimd.tensor_tensor(h23[:, CHUNK:split], gpsimd_product[:], silu[GPSIMD_CHUNK][:, :GPSIMD_SHARE], MULT)
        make_h(h23[:, front], 2)
        upper_gated = keep.tile([P, S], F32, name="upper_gated")
        times_gate(upper_gated, upper_y0, front)
        rest = w3_acc[GPSIMD_CHUNK][:, :, GPSIMD_SHARE:].rearrange("p t n -> p n t")
        nc.vector.tensor_tensor(h23[:, split:], rest, silu[GPSIMD_CHUNK][:, GPSIMD_SHARE:], MULT)
        put_upper(upper_gated, front)
        packed = packed_h(1)
        quantise_h(h23[:], packed, whole)
        upper_y23 = second_product(upper_rows, packed, "w1_3", whole)
        lower_y23 = second_product(lower_rows, packed, "w3_0", whole)
        times_gate(upper_gated, upper_y1, back)
        lower_gated = keep.tile([P, S], F32, name="lower_gated")
        times_gate(lower_gated, lower_y01, first)
        put_upper(upper_gated, back)
        times_gate(upper_gated, upper_y23, second)
        times_gate(lower_gated, lower_y23, second)
        put_upper(upper_gated, second)
        nc.sync.dma_start(out[upper_rows, :], upper[:])
        nc.vector.tensor_tensor(lower[:].indirect(offsets[:]), lower_gated[:], lower_picked[:], ADD)
        nc.sync.dma_start(out[lower_rows, :], lower[:])
